import numpy as np
import ml_dtypes


def mxq(x, axis, fmt="e4m3"):
    dtype, down = {"e4m3": (ml_dtypes.float8_e4m3fn, 7), "e5m2": (ml_dtypes.float8_e5m2, 14)}[fmt]
    v = np.moveaxis(np.asarray(x, np.float32).astype(ml_dtypes.bfloat16).astype(np.float64), axis, -1)
    blocks = v.reshape(v.shape[:-1] + (-1, 32))
    amax = np.abs(blocks).max(-1, keepdims=True)
    byte = np.maximum(np.where(amax > 0, np.frexp(amax)[1] - 1 + 127, 0) - down, 1)
    scale = np.exp2(byte - 127.0)
    codes = (blocks / scale).astype(np.float32).astype(dtype).astype(np.float64)
    return np.moveaxis((codes * scale).reshape(v.shape), -1, axis)


WIDE = False


def mx_kscale(k):
    if not WIDE:
        return np.ones(k)
    levels = np.array([24, -24, 12, -12, 0])
    if k % 512:
        return np.exp2(np.random.permutation(np.resize(levels, k // 32))).repeat(32)
    a = np.empty((k // 512, 16))
    for p in range(k // 512):
        a[p, :8] = np.random.permutation(np.resize(levels, 8))
        for g in range(8):
            far = levels[np.abs(levels - a[p, g]) >= 10]
            a[p, g + 8] = far[np.random.randint(len(far))]
    return np.exp2(a.ravel()).repeat(32)


def f64(x):
    return np.asarray(x).astype(np.float64)


def striped(idx):
    return np.tile(idx.reshape(-1, 16).T, (8, 1)).astype(np.uint16)


def unstriped(offs):
    return offs[:16].T.reshape(-1).astype(np.int64)


E2M1 = np.array([0.0, 0.5, 1.0, 1.5, 2.0, 3.0, 4.0, 6.0, -0.0, -0.5, -1.0, -1.5, -2.0, -3.0, -4.0, -6.0])


def pack_weight(w, fmt):
    k, n = w.shape
    w = f64(np.asarray(w, np.float32).astype(ml_dtypes.bfloat16)).reshape(k // 32, 32, n)
    amax = np.abs(w).max(1)
    if fmt == "e4m3":
        byte = np.frexp(amax)[1] - 1 + 127 - 7
    else:
        mant, ex = np.frexp(amax / 6.0)
        byte = np.where(mant > 0.5, ex, ex - 1) + 127
    byte = np.clip(np.where(amax > 0, byte, 1), 1, 254)
    scaled = (w * np.exp2(127.0 - byte)[:, None, :]).reshape(k, n).astype(np.float32)
    by_word = np.ascontiguousarray(scaled.reshape(k // 512, 128, 4, n).transpose(0, 1, 3, 2))
    if fmt == "e4m3":
        words = by_word.astype(ml_dtypes.float8_e4m3fn).view(np.uint8)
    else:
        c = by_word.astype(ml_dtypes.float4_e2m1fn).view(np.uint8) & 0xF
        words = (c[..., 0::2] | (c[..., 1::2] << 4)).reshape(k // 512, 128, 2 * n)
    return np.ascontiguousarray(words), np.ascontiguousarray(byte.astype(np.uint8).reshape(k // 512, 16, n))


def unpack_weight(words, scales, fmt):
    g, _, n = scales.shape
    words = np.ascontiguousarray(words).reshape(g, 128, n, -1)
    if fmt == "e4m3":
        vals = words.view(ml_dtypes.float8_e4m3fn).astype(np.float64)
    else:
        nib = np.empty((g, 128, n, 4), np.uint8)
        nib[..., 0::2] = words & 0xF
        nib[..., 1::2] = words >> 4
        vals = E2M1[nib]
    vals = vals * np.repeat(np.exp2(scales.astype(np.float64) - 127.0), 8, axis=1)[..., None]
    return vals.transpose(0, 1, 3, 2).reshape(g * 512, n)


K, R, N, T, J = 512, 1024, 512, 4096, 1024


def setup_inputs():
    n = np.random.standard_normal
    s = mx_kscale(K)[:, None]
    u = mx_kscale(R)[:, None]
    p_tab = pack_weight(n((K, T)) * s, "e4m3")
    p_wu = pack_weight(n((K, R)) / np.sqrt(K) / s * u.T, "e2m1")
    return {
        "tab_words": p_tab[0],
        "tab_scales": p_tab[1],
        "wg": (n((K, R)) / np.sqrt(K) / s).astype(np.float32),
        "wu_words": p_wu[0],
        "wu_scales": p_wu[1],
        "wd": (n((R, N)) / np.sqrt(R) / u).astype(np.float32),
        "b": (0.3 * n(N)).astype(np.float32),
        "offs": striped(np.random.permutation(T)[:J]),
    }


def reference(tab_words, tab_scales, wg, wu_words, wu_scales, wd, b, offs):
    idx = unstriped(offs)
    tab_ = unpack_weight(tab_words, tab_scales, "e4m3")[:, idx]
    wg_ = mxq(f64(wg), 0, "e4m3")
    wu_ = unpack_weight(wu_words, wu_scales, "e2m1")
    ga = wg_.T @ tab_
    ub = wu_.T @ tab_
    h = np.maximum(ga, 0.0) * ub
    h_ = mxq(h, 0, "e4m3")
    wd_ = mxq(f64(wd), 0, "e4m3")
    y = wd_.T @ h_
    return y + f64(b)[:, None]

@@ -1,0 +1,235 @@
+from contextlib import ExitStack
+
+import concourse.mybir as mybir
+
+K, R, N, T, J = 512, 1024, 512, 4096, 1024
+FLOPS = 2 * K * R * J * 2 + 2 * R * N * J
+
+F32 = mybir.dt.float32
+BF16 = mybir.dt.bfloat16
+I32 = mybir.dt.int32
+U32 = mybir.dt.uint32
+U16 = mybir.dt.uint16
+U8 = mybir.dt.uint8
+FP8X4 = mybir.dt.float8_e4m3fn_x4
+FP4X4 = mybir.dt.float4_e2m1fn_x4
+ALU = mybir.AluOpType
+ACT = mybir.ActivationFunctionType
+
+P = 128
+PASSES = 2
+CHUNK = 128
+CHUNKS = J // CHUNK
+Y_GROUPS = ((0, 2), (2, 4), (4, 6), (6, 7), (7, 8))
+
+
+def tile_list_gmlpt_relu_bias_kernel(tc, tab_words, tab_scales, wg, wu_words, wu_scales, wd, b, offs, out):
+    nc = tc.nc
+    with ExitStack() as ctx:
+        keep = ctx.enter_context(tc.tile_pool(name="keep", bufs=1))
+        ps_u = ctx.enter_context(tc.psum_pool(name="ps_u", bufs=2))
+        ps_g = ctx.enter_context(tc.psum_pool(name="ps_g", bufs=3))
+        ps_y = ctx.enter_context(tc.psum_pool(name="ps_y", bufs=3))
+
+        def tile(name, shape, dtype):
+            return keep.tile(shape, dtype, name=name, align_bytes=64)
+
+        offsets = keep.tile([P, J // 16], U16, name="offsets")
+        tw = tile("tw", [P, T], I32)
+        ts = tile("ts", [P, T // 4], I32)
+        uw_raw = tile("uw_raw", [P, R // 2], I32)
+        us_raw = tile("us_raw", [P, R // 4], I32)
+        uw = tile("uw", [P, R // 2], I32)
+        us = tile("us", [P, R // 4], I32)
+        vw = tile("vw", [P, J], U32)
+        vs = tile("vs", [P, J], U8)
+        bias = tile("bias", [P, 4], F32)
+        g_raw = [[tile("g_raw%d%d" % (a, hf), [P, 4, 256], F32) for hf in range(2)] for a in range(PASSES)]
+        g_bf = [tile("g_bf%d" % a, [P, 2048], BF16) for a in range(PASSES)]
+        gw = [tile("gw%d" % a, [P, 512], U32) for a in range(PASSES)]
+        gs = [tile("gs%d" % a, [P, 512], U8) for a in range(PASSES)]
+        d_raw = [tile("d_raw%d" % a, [P, 4, N], F32) for a in range(PASSES)]
+        d_bf = [tile("d_bf%d" % a, [P, 4 * N], BF16) for a in range(PASSES)]
+        dw = [tile("dw%d" % a, [P, N], U32) for a in range(PASSES)]
+        ds = [tile("ds%d" % a, [P, N], U8) for a in range(PASSES)]
+        ub = [tile("ub%d" % a, [P, 4 * J], F32) for a in range(PASSES)]
+        h_bf = [tile("h_bf%d" % a, [P, 4 * J], BF16) for a in range(PASSES)]
+        hw = [tile("hw%d" % a, [P, J], U32) for a in range(PASSES)]
+        hs = [tile("hs%d" % a, [P, J], U8) for a in range(PASSES)]
+        y_sb = [tile("y_sb%d" % g, [P, 4, CHUNK * (c1 - c0)], F32) for g, (c0, c1) in enumerate(Y_GROUPS)]
+
+        nc.vector.memset(ts[:], 0)
+        nc.gpsimd.memset(us_raw[:], 0)
+        nc.sync.dma_start(offsets[:], offs)
+        nc.sync.dma_start(uw_raw[:], wu_words[0].bitcast(I32))
+        ts_rows = tab_scales[0].bitcast(I32)
+        us_rows = wu_scales[0].bitcast(I32)
+        for q in range(4):
+            nc.sync.dma_start(ts[32 * q : 32 * q + 4, :], ts_rows[4 * q : 4 * q + 4, :])
+        nc.sync.dma_start(tw[:], tab_words[0].rearrange("p t i -> p (t i)").bitcast(I32))
+        for q in range(4):
+            nc.sync.dma_start(us_raw[32 * q : 32 * q + 4, :], us_rows[4 * q : 4 * q + 4, :])
+        wg_rows = wg.rearrange("(p i) r -> p i r", i=4)
+        for a in range(PASSES):
+            for hf in range(2):
+                c0 = 512 * a + 256 * hf
+                nc.sync.dma_start(g_raw[a][hf][:], wg_rows[:, :, c0 : c0 + 256])
+        for a in range(PASSES):
+            rows = wd[512 * a : 512 * (a + 1), :].rearrange("(q t s) n -> t q s n", t=4, s=8)
+            for t in range(4):
+                nc.sync.dma_start(d_raw[a][:, t, :], rows[t])
+        with nc.allow_non_contiguous_dma(reason="one bias value to a partition"):
+            nc.sync.dma_start(bias[:], b.rearrange("(u p) -> p u", p=P))
+
+        nc.vector.tensor_copy(
+            uw[:].rearrange("p (a t q w) -> p a t q w", a=2, t=4, w=4),
+            uw_raw[:].rearrange("p (a q t w) -> p a t q w", a=2, t=4, w=4),
+        )
+        nc.vector.tensor_copy(vs[:], ts[:].bitcast(U8).indirect(offsets[:]))
+        for jh in range(2):
+            nc.vector.tensor_copy(
+                vw[:, 512 * jh : 512 * (jh + 1)],
+                tw[:].bitcast(U32).indirect(offsets[:, 32 * jh : 32 * (jh + 1)]),
+            )
+            if jh == 0:
+                nc.vector.tensor_copy(
+                    us[:].rearrange("p (a t q w) -> p a t q w", a=2, t=4, w=2),
+                    us_raw[:].rearrange("p (a q t w) -> p a t q w", a=2, t=4, w=2),
+                )
+
+        def cast_wg(copy, a, hf):
+            dst = g_bf[a][:].rearrange("p (t q u v i) -> p u q t i v", t=4, q=16, u=2, v=4, i=4)
+            src = g_raw[a][hf][:].rearrange("p i (q t u v) -> p u q t i v", t=4, u=2, v=4)
+            for u in range(2):
+                copy(dst[:, u, 8 * hf : 8 * hf + 8], src[:, u])
+
+        def quantize(words, scales, src):
+            nc.vector.quantize_mx(out=words.bitcast(FP8X4), scales=scales, in_=src)
+
+        def up(a, c):
+            cols = slice(CHUNK * c, CHUNK * (c + 1))
+            bank = ps_u.tile([P, 4, CHUNK], F32, name="bank_u")
+            for t in range(4):
+                m = 4 * a + t
+                nc.tensor.matmul_mx(
+                    out=bank[:, t, :],
+                    lhsT=uw[:].bitcast(U8)[:, 256 * m : 256 * (m + 1)].bitcast(FP4X4),
+                    lhsT_scale=us[:].bitcast(U8)[:, 128 * m : 128 * (m + 1)],
+                    rhs=vw[:, cols].bitcast(FP8X4),
+                    rhs_scale=vs[:, cols],
+                    start=True,
+                    stop=True,
+                )
+            nc.scalar.activation(
+                ub[a][:, 512 * c : 512 * (c + 1)].rearrange("p (j t) -> p j t", t=4),
+                bank[:].rearrange("p t j -> p j t"),
+                ACT.Copy,
+            )
+
+        def gate(a, c):
+            cols = slice(CHUNK * c, CHUNK * (c + 1))
+            bank = ps_g.tile([P, 4, CHUNK], F32, name="bank_g")
+            for t in range(4):
+                nc.tensor.matmul_mx(
+                    out=bank[:, t, :],
+                    lhsT=gw[a][:, 128 * t : 128 * (t + 1)].bitcast(FP8X4),
+                    lhsT_scale=gs[a][:, 128 * t : 128 * (t + 1)],
+                    rhs=vw[:, cols].bitcast(FP8X4),
+                    rhs_scale=vs[:, cols],
+                    start=True,
+                    stop=True,
+                )
+            nc.vector.scalar_tensor_tensor(
+                out=h_bf[a][:, 512 * c : 512 * (c + 1)].rearrange("p (j t) -> p j t", t=4),
+                in0=bank[:].rearrange("p t j -> p j t"),
+                scalar=0.0,
+                in1=ub[a][:, 512 * c : 512 * (c + 1)].rearrange("p (j t) -> p j t", t=4),
+                op0=ALU.max,
+                op1=ALU.mult,
+            )
+
+        def quantize_h(a, c0, c1):
+            cols = slice(CHUNK * c0, CHUNK * c1)
+            quantize(hw[a][:, cols], hs[a][:, cols], h_bf[a][:, 512 * c0 : 512 * c1])
+
+        def cast_wd(copy, a, hf):
+            dst = d_bf[a][:, 1024 * hf : 1024 * (hf + 1)].rearrange("p (c v t) -> p c t v", t=4, v=4)
+            src = d_raw[a][:, :, 256 * hf : 256 * (hf + 1)].rearrange("p t (c v) -> p c t v", v=4)
+            copy(dst, src)
+
+        def down(g):
+            c0, c1 = Y_GROUPS[g]
+            cols = slice(CHUNK * c0, CHUNK * c1)
+            width = CHUNK * (c1 - c0)
+            for pair in range(2):
+                bank = ps_y.tile([P, 2, width], F32, name="bank_y")
+                for e in range(2):
+                    u = 2 * pair + e
+                    for a in range(PASSES):
+                        nc.tensor.matmul_mx(
+                            out=bank[:, e, :],
+                            lhsT=dw[a][:, 128 * u : 128 * (u + 1)].bitcast(FP8X4),
+                            lhsT_scale=ds[a][:, 128 * u : 128 * (u + 1)],
+                            rhs=hw[a][:, cols].bitcast(FP8X4),
+                            rhs_scale=hs[a][:, cols],
+                            start=(a == 0),
+                            stop=(a == PASSES - 1),
+                        )
+                for e in range(2):
+                    u = 2 * pair + e
+                    if g >= 2 and pair == 1:
+                        nc.vector.tensor_scalar_add(y_sb[g][:, u, :], bank[:, e, :], bias[:, u : u + 1])
+                    else:
+                        nc.scalar.activation(y_sb[g][:, u, :], bank[:, e, :], ACT.Identity, bias=bias[:, u : u + 1])
+            nc.sync.dma_start(out.rearrange("(u p) j -> p u j", p=P)[:, :, cols], y_sb[g][:])
+
+        cast_wg(nc.vector.tensor_copy, 0, 0)
+        cast_wg(nc.vector.tensor_copy, 0, 1)
+        for hf in range(2):
+            cols = slice(256 * hf, 256 * (hf + 1))
+            quantize(gw[0][:, cols], gs[0][:, cols], g_bf[0][:, 1024 * hf : 1024 * (hf + 1)])
+        for c in range(3):
+            up(0, c)
+        gate(0, 0)
+        for c in range(3, 8):
+            up(0, c)
+            gate(0, c - 2)
+        cast_wg(nc.scalar.copy, 1, 0)
+        cast_wg(nc.scalar.copy, 1, 1)
+        quantize_h(0, 0, 4)
+        up(1, 0)
+        gate(0, 6)
+        up(1, 1)
+        cast_wd(nc.vector.tensor_copy, 0, 0)
+        gate(0, 7)
+        up(1, 2)
+        quantize(gw[1][:], gs[1][:], g_bf[1][:])
+        cast_wd(nc.vector.tensor_copy, 0, 1)
+        up(1, 3)
+        cast_wd(nc.scalar.copy, 1, 0)
+        cast_wd(nc.scalar.copy, 1, 1)
+        gate(1, 0)
+        quantize(dw[0][:], ds[0][:], d_bf[0][:])
+        gate(1, 1)
+        quantize_h(0, 4, 8)
+        up(1, 4)
+        gate(1, 2)
+        up(1, 5)
+        quantize_h(1, 0, 2)
+        gate(1, 3)
+        quantize(dw[1][:], ds[1][:], d_bf[1][:])
+        up(1, 6)
+        up(1, 7)
+        down(0)
+        gate(1, 4)
+        quantize_h(1, 2, 4)
+        down(1)
+        gate(1, 5)
+        gate(1, 6)
+        quantize_h(1, 4, 6)
+        gate(1, 7)
+        quantize_h(1, 6, 7)
+        quantize_h(1, 7, 8)
+        down(2)
+        down(3)
+        down(4)

@@ -27,9 +27,8 @@ def tile_list_gmlpt_relu_bias_kernel(tc, tab_words, tab_scales, wg, wu_words, wu
     nc = tc.nc
     with ExitStack() as ctx:
         keep = ctx.enter_context(tc.tile_pool(name="keep", bufs=1))
-        ps_u = ctx.enter_context(tc.psum_pool(name="ps_u", bufs=2))
-        ps_g = ctx.enter_context(tc.psum_pool(name="ps_g", bufs=3))
-        ps_y = ctx.enter_context(tc.psum_pool(name="ps_y", bufs=3))
+        ps_s = ctx.enter_context(tc.psum_pool(name="ps_s", bufs=4))
+        ps_v = ctx.enter_context(tc.psum_pool(name="ps_v", bufs=4))
 
         def tile(name, shape, dtype):
             return keep.tile(shape, dtype, name=name, align_bytes=64)
@@ -38,13 +37,14 @@ def tile_list_gmlpt_relu_bias_kernel(tc, tab_words, tab_scales, wg, wu_words, wu
         tw = tile("tw", [P, T], I32)
         ts = tile("ts", [P, T // 4], I32)
         uw_raw = tile("uw_raw", [P, R // 2], I32)
-        us_raw = tile("us_raw", [P, R // 4], I32)
+        us_raw = keep.tile([P, R // 4], I32, name="us_raw", tag="shared", align_bytes=64)
         uw = tile("uw", [P, R // 2], I32)
         us = tile("us", [P, R // 4], I32)
-        vw = tile("vw", [P, J], U32)
+        vw0 = tile("vw0", [P, J // 2], U32)
         vs = tile("vs", [P, J], U8)
         bias = tile("bias", [P, 4], F32)
-        g_raw = [[tile("g_raw%d%d" % (a, hf), [P, 4, 256], F32) for hf in range(2)] for a in range(PASSES)]
+        g_raw0 = [tile("g_raw0%d" % hf, [P, 4, 256], F32) for hf in range(2)]
+        g_raw1 = tile("g_raw1", [P, 4, 512], F32)
         g_bf = [tile("g_bf%d" % a, [P, 2048], BF16) for a in range(PASSES)]
         gw = [tile("gw%d" % a, [P, 512], U32) for a in range(PASSES)]
         gs = [tile("gs%d" % a, [P, 512], U8) for a in range(PASSES)]
@@ -64,16 +64,15 @@ def tile_list_gmlpt_relu_bias_kernel(tc, tab_words, tab_scales, wg, wu_words, wu
         nc.sync.dma_start(uw_raw[:], wu_words[0].bitcast(I32))
         ts_rows = tab_scales[0].bitcast(I32)
         us_rows = wu_scales[0].bitcast(I32)
-        for q in range(4):
-            nc.sync.dma_start(ts[32 * q : 32 * q + 4, :], ts_rows[4 * q : 4 * q + 4, :])
-        nc.sync.dma_start(tw[:], tab_words[0].rearrange("p t i -> p (t i)").bitcast(I32))
-        for q in range(4):
-            nc.sync.dma_start(us_raw[32 * q : 32 * q + 4, :], us_rows[4 * q : 4 * q + 4, :])
         wg_rows = wg.rearrange("(p i) r -> p i r", i=4)
-        for a in range(PASSES):
-            for hf in range(2):
-                c0 = 512 * a + 256 * hf
-                nc.sync.dma_start(g_raw[a][hf][:], wg_rows[:, :, c0 : c0 + 256])
+        nc.sync.dma_start(g_raw0[0][:], wg_rows[:, :, 0:256])
+        for r in range(4):
+            nc.sync.dma_start(ts[r:P:32, :], ts_rows[r:16:4, :])
+        nc.sync.dma_start(tw[:], tab_words[0].rearrange("p t i -> p (t i)").bitcast(I32))
+        for r in range(4):
+            nc.sync.dma_start(us_raw[r:P:32, :], us_rows[r:16:4, :])
+        nc.sync.dma_start(g_raw0[1][:], wg_rows[:, :, 256:512])
+        nc.sync.dma_start(g_raw1[:], wg_rows[:, :, 512:1024])
         for a in range(PASSES):
             rows = wd[512 * a : 512 * (a + 1), :].rearrange("(q t s) n -> t q s n", t=4, s=8)
             for t in range(4):
@@ -86,36 +85,34 @@ def tile_list_gmlpt_relu_bias_kernel(tc, tab_words, tab_scales, wg, wu_words, wu
             uw_raw[:].rearrange("p (a q t w) -> p a t q w", a=2, t=4, w=4),
         )
         nc.vector.tensor_copy(vs[:], ts[:].bitcast(U8).indirect(offsets[:]))
-        for jh in range(2):
-            nc.vector.tensor_copy(
-                vw[:, 512 * jh : 512 * (jh + 1)],
-                tw[:].bitcast(U32).indirect(offsets[:, 32 * jh : 32 * (jh + 1)]),
-            )
-            if jh == 0:
-                nc.vector.tensor_copy(
-                    us[:].rearrange("p (a t q w) -> p a t q w", a=2, t=4, w=2),
-                    us_raw[:].rearrange("p (a q t w) -> p a t q w", a=2, t=4, w=2),
-                )
+        nc.vector.tensor_copy(vw0[:], tw[:].bitcast(U32).indirect(offsets[:, 0:32]))
+        nc.vector.tensor_copy(
+            us[:].rearrange("p (a t q w) -> p a t q w", a=2, t=4, w=2),
+            us_raw[:].rearrange("p (a q t w) -> p a t q w", a=2, t=4, w=2),
+        )
+        vw1 = keep.tile([P, J // 2], U32, name="vw1", tag="shared", align_bytes=64)
+        nc.vector.tensor_copy(vw1[:], tw[:].bitcast(U32).indirect(offsets[:, 32:64]))
+        vw = (vw0, vw1)
 
-        def cast_wg(copy, a, hf):
+        def cast_wg(copy, a, raw, q0, q1):
             dst = g_bf[a][:].rearrange("p (t q u v i) -> p u q t i v", t=4, q=16, u=2, v=4, i=4)
-            src = g_raw[a][hf][:].rearrange("p i (q t u v) -> p u q t i v", t=4, u=2, v=4)
+            src = raw.rearrange("p i (q t u v) -> p u q t i v", t=4, u=2, v=4)
             for u in range(2):
-                copy(dst[:, u, 8 * hf : 8 * hf + 8], src[:, u])
+                copy(dst[:, u, q0:q1], src[:, u])
 
         def quantize(words, scales, src):
             nc.vector.quantize_mx(out=words.bitcast(FP8X4), scales=scales, in_=src)
 
         def up(a, c):
             cols = slice(CHUNK * c, CHUNK * (c + 1))
-            bank = ps_u.tile([P, 4, CHUNK], F32, name="bank_u")
+            bank = ps_s.tile([P, 4, CHUNK], F32, name="bank_s")
             for t in range(4):
                 m = 4 * a + t
                 nc.tensor.matmul_mx(
                     out=bank[:, t, :],
                     lhsT=uw[:].bitcast(U8)[:, 256 * m : 256 * (m + 1)].bitcast(FP4X4),
                     lhsT_scale=us[:].bitcast(U8)[:, 128 * m : 128 * (m + 1)],
-                    rhs=vw[:, cols].bitcast(FP8X4),
+                    rhs=vw[c // 4][:, CHUNK * (c % 4) : CHUNK * (c % 4 + 1)].bitcast(FP8X4),
                     rhs_scale=vs[:, cols],
                     start=True,
                     stop=True,
@@ -128,13 +125,13 @@ def tile_list_gmlpt_relu_bias_kernel(tc, tab_words, tab_scales, wg, wu_words, wu
 
         def gate(a, c):
             cols = slice(CHUNK * c, CHUNK * (c + 1))
-            bank = ps_g.tile([P, 4, CHUNK], F32, name="bank_g")
+            bank = ps_v.tile([P, 4, CHUNK], F32, name="bank_v")
             for t in range(4):
                 nc.tensor.matmul_mx(
                     out=bank[:, t, :],
                     lhsT=gw[a][:, 128 * t : 128 * (t + 1)].bitcast(FP8X4),
                     lhsT_scale=gs[a][:, 128 * t : 128 * (t + 1)],
-                    rhs=vw[:, cols].bitcast(FP8X4),
+                    rhs=vw[c // 4][:, CHUNK * (c % 4) : CHUNK * (c % 4 + 1)].bitcast(FP8X4),
                     rhs_scale=vs[:, cols],
                     start=True,
                     stop=True,
@@ -157,12 +154,27 @@ def tile_list_gmlpt_relu_bias_kernel(tc, tab_words, tab_scales, wg, wu_words, wu
             src = d_raw[a][:, :, 256 * hf : 256 * (hf + 1)].rearrange("p t (c v) -> p c t v", v=4)
             copy(dst, src)
 
+        def cast_wd_gpsimd(a):
+            for u in range(4):
+                dst = d_bf[a][:, 512 * u : 512 * (u + 1)].rearrange("p (n t) -> p n t", t=4)
+                src = d_raw[a][:, :, 128 * u : 128 * (u + 1)].rearrange("p t n -> p n t")
+                nc.gpsimd.tensor_scalar(dst, src, 1.0, 0.0, ALU.mult, ALU.add)
+
+        def cast_wg_gpsimd():
+            src = g_raw1[:].rearrange("p i (q t s) -> p t q s i", t=4, s=8)
+            dst = g_bf[1][:].rearrange("p (t q s i) -> p t q s i", t=4, s=8, i=4)
+            for t in range(4):
+                nc.gpsimd.tensor_scalar(dst[:, t], src[:, t], 1.0, 0.0, ALU.mult, ALU.add)
+
         def down(g):
             c0, c1 = Y_GROUPS[g]
             cols = slice(CHUNK * c0, CHUNK * c1)
             width = CHUNK * (c1 - c0)
             for pair in range(2):
-                bank = ps_y.tile([P, 2, width], F32, name="bank_y")
+                if g >= 3 and pair == 1:
+                    bank = ps_v.tile([P, 2, width], F32, name="bank_v")
+                else:
+                    bank = ps_s.tile([P, 2, width], F32, name="bank_s")
                 for e in range(2):
                     u = 2 * pair + e
                     for a in range(PASSES):
@@ -177,59 +189,57 @@ def tile_list_gmlpt_relu_bias_kernel(tc, tab_words, tab_scales, wg, wu_words, wu
                         )
                 for e in range(2):
                     u = 2 * pair + e
-                    if g >= 2 and pair == 1:
+                    if g >= 3 and pair == 1:
                         nc.vector.tensor_scalar_add(y_sb[g][:, u, :], bank[:, e, :], bias[:, u : u + 1])
                     else:
                         nc.scalar.activation(y_sb[g][:, u, :], bank[:, e, :], ACT.Identity, bias=bias[:, u : u + 1])
             nc.sync.dma_start(out.rearrange("(u p) j -> p u j", p=P)[:, :, cols], y_sb[g][:])
 
-        cast_wg(nc.vector.tensor_copy, 0, 0)
-        cast_wg(nc.vector.tensor_copy, 0, 1)
+        cast_wg(nc.scalar.copy, 0, g_raw0[0][:], 0, 8)
+        cast_wg(nc.scalar.copy, 0, g_raw0[1][:], 8, 16)
         for hf in range(2):
             cols = slice(256 * hf, 256 * (hf + 1))
             quantize(gw[0][:, cols], gs[0][:, cols], g_bf[0][:, 1024 * hf : 1024 * (hf + 1)])
-        for c in range(3):
-            up(0, c)
-        gate(0, 0)
-        for c in range(3, 8):
-            up(0, c)
-            gate(0, c - 2)
-        cast_wg(nc.scalar.copy, 1, 0)
-        cast_wg(nc.scalar.copy, 1, 1)
+        cast_wg_gpsimd()
+        cast_wd_gpsimd(0)
+        cast_wd_gpsimd(1)
+        up(0, 0)
+        up(0, 1)
+        up(0, 2)
+        for c in range(5):
+            gate(0, c)
+            up(0, c + 3)
         quantize_h(0, 0, 4)
+        gate(0, 5)
         up(1, 0)
+        quantize(gw[1][:], gs[1][:], g_bf[1][:])
         gate(0, 6)
         up(1, 1)
-        cast_wd(nc.vector.tensor_copy, 0, 0)
         gate(0, 7)
         up(1, 2)
-        quantize(gw[1][:], gs[1][:], g_bf[1][:])
-        cast_wd(nc.vector.tensor_copy, 0, 1)
-        up(1, 3)
-        cast_wd(nc.scalar.copy, 1, 0)
-        cast_wd(nc.scalar.copy, 1, 1)
-        gate(1, 0)
         quantize(dw[0][:], ds[0][:], d_bf[0][:])
-        gate(1, 1)
+        gate(1, 0)
+        up(1, 3)
         quantize_h(0, 4, 8)
+        gate(1, 1)
         up(1, 4)
         gate(1, 2)
-        up(1, 5)
         quantize_h(1, 0, 2)
-        gate(1, 3)
         quantize(dw[1][:], ds[1][:], d_bf[1][:])
-        up(1, 6)
-        up(1, 7)
+        up(1, 5)
+        gate(1, 3)
         down(0)
+        up(1, 6)
         gate(1, 4)
         quantize_h(1, 2, 4)
-        down(1)
+        up(1, 7)
         gate(1, 5)
+        down(1)
         gate(1, 6)
         quantize_h(1, 4, 6)
         gate(1, 7)
+        down(2)
         quantize_h(1, 6, 7)
         quantize_h(1, 7, 8)
-        down(2)
         down(3)
         down(4)

@@ -20,7 +20,7 @@ P = 128
 PASSES = 2
 CHUNK = 128
 CHUNKS = J // CHUNK
-Y_GROUPS = ((0, 2), (2, 4), (4, 6), (6, 7), (7, 8))
+Y_GROUPS = ((0, 4), (4, 6), (6, 7), (7, 8))
 
 
 def tile_list_gmlpt_relu_bias_kernel(tc, tab_words, tab_scales, wg, wu_words, wu_scales, wd, b, offs, out):
@@ -154,29 +154,20 @@ def tile_list_gmlpt_relu_bias_kernel(tc, tab_words, tab_scales, wg, wu_words, wu
             src = d_raw[a][:, :, 256 * hf : 256 * (hf + 1)].rearrange("p t (c v) -> p c t v", v=4)
             copy(dst, src)
 
-        def cast_wd_gpsimd(a):
-            for u in range(4):
-                dst = d_bf[a][:, 512 * u : 512 * (u + 1)].rearrange("p (n t) -> p n t", t=4)
-                src = d_raw[a][:, :, 128 * u : 128 * (u + 1)].rearrange("p t n -> p n t")
-                nc.gpsimd.tensor_scalar(dst, src, 1.0, 0.0, ALU.mult, ALU.add)
-
-        def cast_wg_gpsimd():
-            src = g_raw1[:].rearrange("p i (q t s) -> p t q s i", t=4, s=8)
-            dst = g_bf[1][:].rearrange("p (t q s i) -> p t q s i", t=4, s=8, i=4)
-            for t in range(4):
-                nc.gpsimd.tensor_scalar(dst[:, t], src[:, t], 1.0, 0.0, ALU.mult, ALU.add)
-
         def down(g):
             c0, c1 = Y_GROUPS[g]
             cols = slice(CHUNK * c0, CHUNK * c1)
             width = CHUNK * (c1 - c0)
-            for pair in range(2):
-                if g >= 3 and pair == 1:
-                    bank = ps_v.tile([P, 2, width], F32, name="bank_v")
+            per_bank = 1 if width == 512 else 2
+            out_rows = out.rearrange("(u p) j -> p u j", p=P)
+            for u0 in range(0, 4, per_bank):
+                on_vector = g >= 2 and u0 == 2
+                if on_vector:
+                    bank = ps_v.tile([P, per_bank, width], F32, name="bank_v")
                 else:
-                    bank = ps_s.tile([P, 2, width], F32, name="bank_s")
-                for e in range(2):
-                    u = 2 * pair + e
+                    bank = ps_s.tile([P, per_bank, width], F32, name="bank_s")
+                for e in range(per_bank):
+                    u = u0 + e
                     for a in range(PASSES):
                         nc.tensor.matmul_mx(
                             out=bank[:, e, :],
@@ -187,59 +178,67 @@ def tile_list_gmlpt_relu_bias_kernel(tc, tab_words, tab_scales, wg, wu_words, wu
                             start=(a == 0),
                             stop=(a == PASSES - 1),
                         )
-                for e in range(2):
-                    u = 2 * pair + e
-                    if g >= 3 and pair == 1:
+                for e in range(per_bank):
+                    u = u0 + e
+                    if on_vector:
                         nc.vector.tensor_scalar_add(y_sb[g][:, u, :], bank[:, e, :], bias[:, u : u + 1])
                     else:
                         nc.scalar.activation(y_sb[g][:, u, :], bank[:, e, :], ACT.Identity, bias=bias[:, u : u + 1])
-            nc.sync.dma_start(out.rearrange("(u p) j -> p u j", p=P)[:, :, cols], y_sb[g][:])
+                if g == 0 and u0 % 2 == 1:
+                    nc.sync.dma_start(out_rows[:, u0 - 1 : u0 + 1, cols], y_sb[g][:, u0 - 1 : u0 + 1, :])
+            if g > 0:
+                nc.sync.dma_start(out_rows[:, :, cols], y_sb[g][:])
 
         cast_wg(nc.scalar.copy, 0, g_raw0[0][:], 0, 8)
         cast_wg(nc.scalar.copy, 0, g_raw0[1][:], 8, 16)
         for hf in range(2):
             cols = slice(256 * hf, 256 * (hf + 1))
             quantize(gw[0][:, cols], gs[0][:, cols], g_bf[0][:, 1024 * hf : 1024 * (hf + 1)])
-        cast_wg_gpsimd()
-        cast_wd_gpsimd(0)
-        cast_wd_gpsimd(1)
-        up(0, 0)
-        up(0, 1)
-        up(0, 2)
-        for c in range(5):
-            gate(0, c)
-            up(0, c + 3)
-        quantize_h(0, 0, 4)
-        gate(0, 5)
+        for c in range(4):
+            up(0, c)
+        gate(0, 0)
+        cast_wg(nc.vector.tensor_copy, 1, g_raw1[:], 0, 16)
         up(1, 0)
+        gate(0, 1)
         quantize(gw[1][:], gs[1][:], g_bf[1][:])
-        gate(0, 6)
         up(1, 1)
-        gate(0, 7)
+        gate(0, 2)
         up(1, 2)
-        quantize(dw[0][:], ds[0][:], d_bf[0][:])
-        gate(1, 0)
+        gate(0, 3)
         up(1, 3)
-        quantize_h(0, 4, 8)
+        cast_wd(nc.scalar.copy, 0, 0)
+        cast_wd(nc.scalar.copy, 0, 1)
+        gate(1, 0)
+        quantize_h(0, 0, 4)
         gate(1, 1)
-        up(1, 4)
+        up(0, 4)
         gate(1, 2)
-        quantize_h(1, 0, 2)
-        quantize(dw[1][:], ds[1][:], d_bf[1][:])
-        up(1, 5)
+        up(0, 5)
+        quantize(dw[0][:], ds[0][:], d_bf[0][:])
         gate(1, 3)
-        down(0)
+        cast_wd(nc.scalar.copy, 1, 0)
+        cast_wd(nc.scalar.copy, 1, 1)
+        up(0, 6)
+        gate(0, 4)
+        quantize_h(1, 0, 4)
+        up(0, 7)
+        gate(0, 5)
+        quantize(dw[1][:], ds[1][:], d_bf[1][:])
+        up(1, 4)
+        gate(0, 6)
+        up(1, 5)
+        gate(0, 7)
         up(1, 6)
-        gate(1, 4)
-        quantize_h(1, 2, 4)
         up(1, 7)
+        down(0)
+        gate(1, 4)
+        quantize_h(0, 4, 8)
         gate(1, 5)
-        down(1)
         gate(1, 6)
         quantize_h(1, 4, 6)
         gate(1, 7)
-        down(2)
+        down(1)
         quantize_h(1, 6, 7)
         quantize_h(1, 7, 8)
+        down(2)
         down(3)
-        down(4)

@@ -53,9 +53,11 @@ def tile_list_gmlpt_relu_bias_kernel(tc, tab_words, tab_scales, wg, wu_words, wu
         dw = [tile("dw%d" % a, [P, N], U32) for a in range(PASSES)]
         ds = [tile("ds%d" % a, [P, N], U8) for a in range(PASSES)]
         ub = [tile("ub%d" % a, [P, 4 * J], F32) for a in range(PASSES)]
-        h_bf = [tile("h_bf%d" % a, [P, 4 * J], BF16) for a in range(PASSES)]
-        hw = [tile("hw%d" % a, [P, J], U32) for a in range(PASSES)]
-        hs = [tile("hs%d" % a, [P, J], U8) for a in range(PASSES)]
+        widths = [CHUNK * (c1 - c0) for c0, c1 in Y_GROUPS]
+        h_bf = [tile("h_bf%d" % g, [P, PASSES * 4 * w], BF16) for g, w in enumerate(widths)]
+        hw = [tile("hw%d" % g, [P, PASSES * w], U32) for g, w in enumerate(widths)]
+        hs = [tile("hs%d" % g, [P, PASSES * w], U8) for g, w in enumerate(widths)]
+        group_of = [g for g, (c0, c1) in enumerate(Y_GROUPS) for c in range(c0, c1)]
         y_sb = [tile("y_sb%d" % g, [P, 4, CHUNK * (c1 - c0)], F32) for g, (c0, c1) in enumerate(Y_GROUPS)]
 
         nc.vector.memset(ts[:], 0)
@@ -136,8 +138,10 @@ def tile_list_gmlpt_relu_bias_kernel(tc, tab_words, tab_scales, wg, wu_words, wu
                     start=True,
                     stop=True,
                 )
+            g = group_of[c]
+            first = 4 * (widths[g] * a + CHUNK * (c - Y_GROUPS[g][0]))
             nc.vector.scalar_tensor_tensor(
-                out=h_bf[a][:, 512 * c : 512 * (c + 1)].rearrange("p (j t) -> p j t", t=4),
+                out=h_bf[g][:, first : first + 512].rearrange("p (j t) -> p j t", t=4),
                 in0=bank[:].rearrange("p t j -> p j t"),
                 scalar=0.0,
                 in1=ub[a][:, 512 * c : 512 * (c + 1)].rearrange("p (j t) -> p j t", t=4),
@@ -145,23 +149,22 @@ def tile_list_gmlpt_relu_bias_kernel(tc, tab_words, tab_scales, wg, wu_words, wu
                 op1=ALU.mult,
             )
 
-        def quantize_h(a, c0, c1):
-            cols = slice(CHUNK * c0, CHUNK * c1)
-            quantize(hw[a][:, cols], hs[a][:, cols], h_bf[a][:, 512 * c0 : 512 * c1])
+        def quantize_h(g, a0, a1):
+            cols = slice(widths[g] * a0, widths[g] * a1)
+            quantize(hw[g][:, cols], hs[g][:, cols], h_bf[g][:, 4 * cols.start : 4 * cols.stop])
 
-        def cast_wd(copy, a, hf):
-            dst = d_bf[a][:, 1024 * hf : 1024 * (hf + 1)].rearrange("p (c v t) -> p c t v", t=4, v=4)
-            src = d_raw[a][:, :, 256 * hf : 256 * (hf + 1)].rearrange("p t (c v) -> p c t v", v=4)
+        def cast_wd(copy, a, n0, n1):
+            dst = d_bf[a][:, 4 * n0 : 4 * n1].rearrange("p (c v t) -> p c t v", t=4, v=4)
+            src = d_raw[a][:, :, n0:n1].rearrange("p t (c v) -> p c t v", v=4)
             copy(dst, src)
 
-        def down(g):
+        def down(g, u0, on_vector):
             c0, c1 = Y_GROUPS[g]
             cols = slice(CHUNK * c0, CHUNK * c1)
             width = CHUNK * (c1 - c0)
             per_bank = 1 if width == 512 else 2
             out_rows = out.rearrange("(u p) j -> p u j", p=P)
-            for u0 in range(0, 4, per_bank):
-                on_vector = g >= 2 and u0 == 2
+            if True:
                 if on_vector:
                     bank = ps_v.tile([P, per_bank, width], F32, name="bank_v")
                 else:
@@ -173,72 +176,111 @@ def tile_list_gmlpt_relu_bias_kernel(tc, tab_words, tab_scales, wg, wu_words, wu
                             out=bank[:, e, :],
                             lhsT=dw[a][:, 128 * u : 128 * (u + 1)].bitcast(FP8X4),
                             lhsT_scale=ds[a][:, 128 * u : 128 * (u + 1)],
-                            rhs=hw[a][:, cols].bitcast(FP8X4),
-                            rhs_scale=hs[a][:, cols],
+                            rhs=hw[g][:, width * a : width * (a + 1)].bitcast(FP8X4),
+                            rhs_scale=hs[g][:, width * a : width * (a + 1)],
                             start=(a == 0),
                             stop=(a == PASSES - 1),
                         )
-                for e in range(per_bank):
-                    u = u0 + e
-                    if on_vector:
-                        nc.vector.tensor_scalar_add(y_sb[g][:, u, :], bank[:, e, :], bias[:, u : u + 1])
-                    else:
+                if on_vector:
+                    nc.vector.tensor_tensor(
+                        y_sb[g][:, u0 : u0 + 2, :],
+                        bank[:],
+                        bias[:, u0 : u0 + 2].unsqueeze(2).to_broadcast([P, 2, width]),
+                        ALU.add,
+                    )
+                else:
+                    for e in range(per_bank):
+                        u = u0 + e
                         nc.scalar.activation(y_sb[g][:, u, :], bank[:, e, :], ACT.Identity, bias=bias[:, u : u + 1])
-                if g == 0 and u0 % 2 == 1:
-                    nc.sync.dma_start(out_rows[:, u0 - 1 : u0 + 1, cols], y_sb[g][:, u0 - 1 : u0 + 1, :])
-            if g > 0:
-                nc.sync.dma_start(out_rows[:, :, cols], y_sb[g][:])
+
+        def down_pass(bank, g, u, a):
+            width = widths[g]
+            nc.tensor.matmul_mx(
+                out=bank[:],
+                lhsT=dw[a][:, 128 * u : 128 * (u + 1)].bitcast(FP8X4),
+                lhsT_scale=ds[a][:, 128 * u : 128 * (u + 1)],
+                rhs=hw[g][:, width * a : width * (a + 1)].bitcast(FP8X4),
+                rhs_scale=hs[g][:, width * a : width * (a + 1)],
+                start=(a == 0),
+                stop=(a == PASSES - 1),
+            )
+
+        def store(g, u0, u1):
+            c0, c1 = Y_GROUPS[g]
+            out_rows = out.rearrange("(u p) j -> p u j", p=P)
+            nc.sync.dma_start(out_rows[:, u0:u1, CHUNK * c0 : CHUNK * c1], y_sb[g][:, u0:u1, :])
 
         cast_wg(nc.scalar.copy, 0, g_raw0[0][:], 0, 8)
         cast_wg(nc.scalar.copy, 0, g_raw0[1][:], 8, 16)
-        for hf in range(2):
-            cols = slice(256 * hf, 256 * (hf + 1))
-            quantize(gw[0][:, cols], gs[0][:, cols], g_bf[0][:, 1024 * hf : 1024 * (hf + 1)])
-        for c in range(4):
-            up(0, c)
+        quantize(gw[0][:, 0:256], gs[0][:, 0:256], g_bf[0][:, 0:1024])
+        quantize(gw[0][:, 256:512], gs[0][:, 256:512], g_bf[0][:, 1024:2048])
+        up(0, 0)
         gate(0, 0)
-        cast_wg(nc.vector.tensor_copy, 1, g_raw1[:], 0, 16)
-        up(1, 0)
+        up(0, 1)
         gate(0, 1)
-        quantize(gw[1][:], gs[1][:], g_bf[1][:])
-        up(1, 1)
+        up(0, 2)
+        cast_wg(nc.vector.tensor_copy, 1, g_raw1[:], 0, 16)
+        up(0, 3)
         gate(0, 2)
-        up(1, 2)
+        quantize(gw[1][:], gs[1][:], g_bf[1][:])
+        up(1, 0)
         gate(0, 3)
-        up(1, 3)
-        cast_wd(nc.scalar.copy, 0, 0)
-        cast_wd(nc.scalar.copy, 0, 1)
+        up(1, 1)
         gate(1, 0)
-        quantize_h(0, 0, 4)
+        up(1, 2)
+        quantize_h(0, 0, 1)
+        up(1, 3)
+        cast_wd(nc.scalar.copy, 0, 0, 512)
         gate(1, 1)
-        up(0, 4)
         gate(1, 2)
-        up(0, 5)
+        up(0, 4)
         quantize(dw[0][:], ds[0][:], d_bf[0][:])
         gate(1, 3)
-        cast_wd(nc.scalar.copy, 1, 0)
-        cast_wd(nc.scalar.copy, 1, 1)
-        up(0, 6)
-        gate(0, 4)
-        quantize_h(1, 0, 4)
-        up(0, 7)
-        gate(0, 5)
-        quantize(dw[1][:], ds[1][:], d_bf[1][:])
+        cast_wd(nc.vector.tensor_copy, 1, 0, 192)
+        cast_wd(nc.scalar.copy, 1, 192, 512)
         up(1, 4)
-        gate(0, 6)
+        up(0, 5)
+        gate(0, 4)
+        quantize_h(0, 1, 2)
+        quantize(dw[1][:], ds[1][:], d_bf[1][:])
         up(1, 5)
-        gate(0, 7)
-        up(1, 6)
-        up(1, 7)
-        down(0)
         gate(1, 4)
-        quantize_h(0, 4, 8)
+        down(0, 0, False)
+        store(0, 0, 1)
+        up(0, 6)
+        gate(0, 5)
+        down(0, 1, False)
+        store(0, 1, 2)
+        up(1, 6)
         gate(1, 5)
+        down(0, 2, False)
+        store(0, 2, 3)
+        up(0, 7)
+        up(1, 7)
+        gate(0, 6)
+        down(0, 3, False)
+        store(0, 3, 4)
+        quantize_h(1, 0, 2)
         gate(1, 6)
-        quantize_h(1, 4, 6)
+        gate(0, 7)
+        quantize_h(2, 0, 2)
         gate(1, 7)
-        down(1)
-        quantize_h(1, 6, 7)
-        quantize_h(1, 7, 8)
-        down(2)
-        down(3)
+        quantize_h(3, 0, 1)
+        down(1, 0, False)
+        store(1, 0, 2)
+        down(1, 2, False)
+        store(1, 2, 4)
+        quantize_h(3, 1, 2)
+        down(2, 0, False)
+        down(2, 2, True)
+        store(2, 0, 4)
+        last_banks = [ps_s.tile([P, CHUNK], F32, name="bank_s") for u in range(2)]
+        last_banks += [ps_v.tile([P, CHUNK], F32, name="bank_v") for u in range(2)]
+        for a in range(PASSES):
+            for u in (0, 2, 1, 3):
+                down_pass(last_banks[u], 3, u, a)
+        for u in range(2):
+            nc.scalar.activation(y_sb[3][:, u, :], last_banks[u][:], ACT.Identity, bias=bias[:, u : u + 1])
+        for u in range(2, 4):
+            nc.vector.tensor_scalar_add(y_sb[3][:, u, :], last_banks[u][:], bias[:, u : u + 1])
+        store(3, 0, 4)

@@ -20,6 +20,7 @@ P = 128
 PASSES = 2
 CHUNK = 128
 CHUNKS = J // CHUNK
+ROW0 = P - 16
 Y_GROUPS = ((0, 4), (4, 6), (6, 7), (7, 8))
 
 
@@ -30,74 +31,74 @@ def tile_list_gmlpt_relu_bias_kernel(tc, tab_words, tab_scales, wg, wu_words, wu
         ps_s = ctx.enter_context(tc.psum_pool(name="ps_s", bufs=4))
         ps_v = ctx.enter_context(tc.psum_pool(name="ps_v", bufs=4))
 
-        def tile(name, shape, dtype):
-            return keep.tile(shape, dtype, name=name, align_bytes=64)
+        def tile(name, shape, dtype, tag=None):
+            return keep.tile(shape, dtype, name=name, tag=tag or name, align_bytes=64)
 
         offsets = keep.tile([P, J // 16], U16, name="offsets")
-        tw = tile("tw", [P, T], I32)
-        ts = tile("ts", [P, T // 4], I32)
+        tw = tile("tw", [P, T], I32, tag="tw_then_d_raw1")
+        ts = tile("ts", [P, T // 4], I32, tag="ts_then_g_raw1")
         uw_raw = tile("uw_raw", [P, R // 2], I32)
-        us_raw = keep.tile([P, R // 4], I32, name="us_raw", tag="shared", align_bytes=64)
+        us_raw = tile("us_raw", [P, R // 4], I32, tag="us_raw_then_d_raw0")
         uw = tile("uw", [P, R // 2], I32)
         us = tile("us", [P, R // 4], I32)
-        vw0 = tile("vw0", [P, J // 2], U32)
+        vw = [tile("vw%d" % hf, [P, J // 2], U32) for hf in range(2)]
+        vs_raw = tile("vs_raw", [P, J], U8)
         vs = tile("vs", [P, J], U8)
-        bias = tile("bias", [P, 4], F32)
-        g_raw0 = [tile("g_raw0%d" % hf, [P, 4, 256], F32) for hf in range(2)]
-        g_raw1 = tile("g_raw1", [P, 4, 512], F32)
-        g_bf = [tile("g_bf%d" % a, [P, 2048], BF16) for a in range(PASSES)]
+        g_raw00 = tile("g_raw00", [P, 4, 256], F32, tag="g_raw00_then_ub00")
+        g_raw01 = tile("g_raw01", [P, 4, 256], F32, tag="g_raw01_then_bias")
+        g_bf0 = tile("g_bf0", [P, 2048], BF16)
+        g_bf1 = tile("g_bf1", [P, 2048], BF16)
         gw = [tile("gw%d" % a, [P, 512], U32) for a in range(PASSES)]
         gs = [tile("gs%d" % a, [P, 512], U8) for a in range(PASSES)]
-        d_raw = [tile("d_raw%d" % a, [P, 4, N], F32) for a in range(PASSES)]
-        d_bf = [tile("d_bf%d" % a, [P, 4 * N], BF16) for a in range(PASSES)]
         dw = [tile("dw%d" % a, [P, N], U32) for a in range(PASSES)]
         ds = [tile("ds%d" % a, [P, N], U8) for a in range(PASSES)]
-        ub = [tile("ub%d" % a, [P, 4 * J], F32) for a in range(PASSES)]
-        widths = [CHUNK * (c1 - c0) for c0, c1 in Y_GROUPS]
-        h_bf = [tile("h_bf%d" % g, [P, PASSES * 4 * w], BF16) for g, w in enumerate(widths)]
-        hw = [tile("hw%d" % g, [P, PASSES * w], U32) for g, w in enumerate(widths)]
-        hs = [tile("hs%d" % g, [P, PASSES * w], U8) for g, w in enumerate(widths)]
-        group_of = [g for g, (c0, c1) in enumerate(Y_GROUPS) for c in range(c0, c1)]
+        h_bf = [tile("h_bf%d" % a, [P, 4 * J], BF16) for a in range(PASSES)]
+        hw = [tile("hw%d" % a, [P, J], U32) for a in range(PASSES)]
+        hs = [tile("hs%d" % a, [P, J], U8) for a in range(PASSES)]
         y_sb = [tile("y_sb%d" % g, [P, 4, CHUNK * (c1 - c0)], F32) for g, (c0, c1) in enumerate(Y_GROUPS)]
+        ub = {}
 
-        nc.vector.memset(ts[:], 0)
-        nc.gpsimd.memset(us_raw[:], 0)
-        nc.sync.dma_start(offsets[:], offs)
-        nc.sync.dma_start(uw_raw[:], wu_words[0].bitcast(I32))
-        ts_rows = tab_scales[0].bitcast(I32)
+        nc.vector.memset(ts[0:ROW0, :], 0)
+        nc.gpsimd.memset(us[:], 0)
+        nc.gpsimd.memset(vs[:].bitcast(I32), 0)
         us_rows = wu_scales[0].bitcast(I32)
         wg_rows = wg.rearrange("(p i) r -> p i r", i=4)
-        nc.sync.dma_start(g_raw0[0][:], wg_rows[:, :, 0:256])
-        for r in range(4):
-            nc.sync.dma_start(ts[r:P:32, :], ts_rows[r:16:4, :])
-        nc.sync.dma_start(tw[:], tab_words[0].rearrange("p t i -> p (t i)").bitcast(I32))
+        nc.sync.dma_start(offsets[:], offs)
+        nc.sync.dma_start(ts[ROW0:P, :], tab_scales[0].bitcast(I32))
+        nc.sync.dma_start(uw_raw[:], wu_words[0].bitcast(I32))
         for r in range(4):
             nc.sync.dma_start(us_raw[r:P:32, :], us_rows[r:16:4, :])
-        nc.sync.dma_start(g_raw0[1][:], wg_rows[:, :, 256:512])
+        nc.sync.dma_start(tw[:], tab_words[0].rearrange("p t i -> p (t i)").bitcast(I32))
+        nc.sync.dma_start(g_raw00[:], wg_rows[:, :, 0:256])
+        nc.sync.dma_start(g_raw01[:], wg_rows[:, :, 256:512])
+
+        nc.vector.tensor_copy(vs_raw[:], ts[:].bitcast(U8).indirect(offsets[:]))
+        for r in range(4):
+            nc.sync.dma_start(vs[r:P:32, :].bitcast(I32), vs_raw[ROW0 + r : P : 4, :].bitcast(I32))
+        g_raw1 = tile("g_raw1", [P, 4, 512], F32, tag="ts_then_g_raw1")
         nc.sync.dma_start(g_raw1[:], wg_rows[:, :, 512:1024])
-        for a in range(PASSES):
-            rows = wd[512 * a : 512 * (a + 1), :].rearrange("(q t s) n -> t q s n", t=4, s=8)
-            for t in range(4):
-                nc.sync.dma_start(d_raw[a][:, t, :], rows[t])
-        with nc.allow_non_contiguous_dma(reason="one bias value to a partition"):
-            nc.sync.dma_start(bias[:], b.rearrange("(u p) -> p u", p=P))
 
         nc.vector.tensor_copy(
             uw[:].rearrange("p (a t q w) -> p a t q w", a=2, t=4, w=4),
             uw_raw[:].rearrange("p (a q t w) -> p a t q w", a=2, t=4, w=4),
         )
-        nc.vector.tensor_copy(vs[:], ts[:].bitcast(U8).indirect(offsets[:]))
-        nc.vector.tensor_copy(vw0[:], tw[:].bitcast(U32).indirect(offsets[:, 0:32]))
-        nc.vector.tensor_copy(
-            us[:].rearrange("p (a t q w) -> p a t q w", a=2, t=4, w=2),
-            us_raw[:].rearrange("p (a q t w) -> p a t q w", a=2, t=4, w=2),
-        )
-        vw1 = keep.tile([P, J // 2], U32, name="vw1", tag="shared", align_bytes=64)
-        nc.vector.tensor_copy(vw1[:], tw[:].bitcast(U32).indirect(offsets[:, 32:64]))
-        vw = (vw0, vw1)
+        for quad in range(4):
+            rows = slice(32 * quad, 32 * quad + 4)
+            nc.vector.tensor_copy(
+                us[rows, :].rearrange("p (a t q w) -> p a t q w", a=2, t=4, w=2),
+                us_raw[rows, :].rearrange("p (a q t w) -> p a t q w", a=2, t=4, w=2),
+            )
+        for hf in range(2):
+            nc.vector.tensor_copy(vw[hf][:], tw[:].bitcast(U32).indirect(offsets[:, 32 * hf : 32 * (hf + 1)]))
 
-        def cast_wg(copy, a, raw, q0, q1):
-            dst = g_bf[a][:].rearrange("p (t q u v i) -> p u q t i v", t=4, q=16, u=2, v=4, i=4)
+        d_raw = [tile("d_raw0", [P, 4, N], F32, tag="us_raw_then_d_raw0"), tile("d_raw1", [P, 4, N], F32, tag="tw_then_d_raw1")]
+        for a in range(PASSES):
+            rows = wd[512 * a : 512 * (a + 1), :].rearrange("(q t s) n -> t q s n", t=4, s=8)
+            for t in range(4):
+                nc.sync.dma_start(d_raw[a][:, t, :], rows[t])
+
+        def cast_wg(copy, dst_tile, raw, q0, q1):
+            dst = dst_tile[:].rearrange("p (t q u v i) -> p u q t i v", t=4, q=16, u=2, v=4, i=4)
             src = raw.rearrange("p i (q t u v) -> p u q t i v", t=4, u=2, v=4)
             for u in range(2):
                 copy(dst[:, u, q0:q1], src[:, u])
@@ -119,8 +120,9 @@ def tile_list_gmlpt_relu_bias_kernel(tc, tab_words, tab_scales, wg, wu_words, wu
                     start=True,
                     stop=True,
                 )
+            ub[a, c] = tile("ub%d%d" % (a, c), [P, 4 * CHUNK], F32, tag="g_raw00_then_ub00" if (a, c) == (0, 0) else None)
             nc.scalar.activation(
-                ub[a][:, 512 * c : 512 * (c + 1)].rearrange("p (j t) -> p j t", t=4),
+                ub[a, c][:].rearrange("p (j t) -> p j t", t=4),
                 bank[:].rearrange("p t j -> p j t"),
                 ACT.Copy,
             )
@@ -138,139 +140,109 @@ def tile_list_gmlpt_relu_bias_kernel(tc, tab_words, tab_scales, wg, wu_words, wu
                     start=True,
                     stop=True,
                 )
-            g = group_of[c]
-            first = 4 * (widths[g] * a + CHUNK * (c - Y_GROUPS[g][0]))
             nc.vector.scalar_tensor_tensor(
-                out=h_bf[g][:, first : first + 512].rearrange("p (j t) -> p j t", t=4),
+                out=h_bf[a][:, 512 * c : 512 * (c + 1)].rearrange("p (j t) -> p j t", t=4),
                 in0=bank[:].rearrange("p t j -> p j t"),
                 scalar=0.0,
-                in1=ub[a][:, 512 * c : 512 * (c + 1)].rearrange("p (j t) -> p j t", t=4),
+                in1=ub[a, c][:].rearrange("p (j t) -> p j t", t=4),
                 op0=ALU.max,
                 op1=ALU.mult,
             )
 
-        def quantize_h(g, a0, a1):
-            cols = slice(widths[g] * a0, widths[g] * a1)
-            quantize(hw[g][:, cols], hs[g][:, cols], h_bf[g][:, 4 * cols.start : 4 * cols.stop])
+        def quantize_h(a, c0, c1):
+            cols = slice(CHUNK * c0, CHUNK * c1)
+            quantize(hw[a][:, cols], hs[a][:, cols], h_bf[a][:, 4 * cols.start : 4 * cols.stop])
 
-        def cast_wd(copy, a, n0, n1):
-            dst = d_bf[a][:, 4 * n0 : 4 * n1].rearrange("p (c v t) -> p c t v", t=4, v=4)
+        def cast_wd(copy, dst_tile, a, n0, n1):
+            dst = dst_tile[:, 4 * n0 : 4 * n1].rearrange("p (c v t) -> p c t v", t=4, v=4)
             src = d_raw[a][:, :, n0:n1].rearrange("p t (c v) -> p c t v", v=4)
             copy(dst, src)
 
-        def down(g, u0, on_vector):
+        def down_pass(bank, g, u, a):
             c0, c1 = Y_GROUPS[g]
             cols = slice(CHUNK * c0, CHUNK * c1)
-            width = CHUNK * (c1 - c0)
-            per_bank = 1 if width == 512 else 2
-            out_rows = out.rearrange("(u p) j -> p u j", p=P)
-            if True:
-                if on_vector:
-                    bank = ps_v.tile([P, per_bank, width], F32, name="bank_v")
-                else:
-                    bank = ps_s.tile([P, per_bank, width], F32, name="bank_s")
-                for e in range(per_bank):
-                    u = u0 + e
-                    for a in range(PASSES):
-                        nc.tensor.matmul_mx(
-                            out=bank[:, e, :],
-                            lhsT=dw[a][:, 128 * u : 128 * (u + 1)].bitcast(FP8X4),
-                            lhsT_scale=ds[a][:, 128 * u : 128 * (u + 1)],
-                            rhs=hw[g][:, width * a : width * (a + 1)].bitcast(FP8X4),
-                            rhs_scale=hs[g][:, width * a : width * (a + 1)],
-                            start=(a == 0),
-                            stop=(a == PASSES - 1),
-                        )
-                if on_vector:
-                    nc.vector.tensor_tensor(
-                        y_sb[g][:, u0 : u0 + 2, :],
-                        bank[:],
-                        bias[:, u0 : u0 + 2].unsqueeze(2).to_broadcast([P, 2, width]),
-                        ALU.add,
-                    )
-                else:
-                    for e in range(per_bank):
-                        u = u0 + e
-                        nc.scalar.activation(y_sb[g][:, u, :], bank[:, e, :], ACT.Identity, bias=bias[:, u : u + 1])
-
-        def down_pass(bank, g, u, a):
-            width = widths[g]
             nc.tensor.matmul_mx(
-                out=bank[:],
+                out=bank,
                 lhsT=dw[a][:, 128 * u : 128 * (u + 1)].bitcast(FP8X4),
                 lhsT_scale=ds[a][:, 128 * u : 128 * (u + 1)],
-                rhs=hw[g][:, width * a : width * (a + 1)].bitcast(FP8X4),
-                rhs_scale=hs[g][:, width * a : width * (a + 1)],
+                rhs=hw[a][:, cols].bitcast(FP8X4),
+                rhs_scale=hs[a][:, cols],
                 start=(a == 0),
                 stop=(a == PASSES - 1),
             )
+
+        def down(g, u0, on_vector):
+            c0, c1 = Y_GROUPS[g]
+            width = CHUNK * (c1 - c0)
+            per_bank = 1 if width == 512 else 2
+            if on_vector:
+                bank = ps_v.tile([P, per_bank, width], F32, name="bank_v")
+            else:
+                bank = ps_s.tile([P, per_bank, width], F32, name="bank_s")
+            for e in range(per_bank):
+                for a in range(PASSES):
+                    down_pass(bank[:, e, :], g, u0 + e, a)
+            if on_vector:
+                nc.vector.tensor_tensor(
+                    y_sb[g][:, u0 : u0 + 2, :],
+                    bank[:],
+                    bias[:, u0 : u0 + 2].unsqueeze(2).to_broadcast([P, 2, width]),
+                    ALU.add,
+                )
+            else:
+                for e in range(per_bank):
+                    u = u0 + e
+                    nc.scalar.activation(y_sb[g][:, u, :], bank[:, e, :], ACT.Identity, bias=bias[:, u : u + 1])
 
         def store(g, u0, u1):
             c0, c1 = Y_GROUPS[g]
             out_rows = out.rearrange("(u p) j -> p u j", p=P)
             nc.sync.dma_start(out_rows[:, u0:u1, CHUNK * c0 : CHUNK * c1], y_sb[g][:, u0:u1, :])
 
-        cast_wg(nc.scalar.copy, 0, g_raw0[0][:], 0, 8)
-        cast_wg(nc.scalar.copy, 0, g_raw0[1][:], 8, 16)
-        quantize(gw[0][:, 0:256], gs[0][:, 0:256], g_bf[0][:, 0:1024])
-        quantize(gw[0][:, 256:512], gs[0][:, 256:512], g_bf[0][:, 1024:2048])
-        up(0, 0)
-        gate(0, 0)
-        up(0, 1)
-        gate(0, 1)
-        up(0, 2)
-        cast_wg(nc.vector.tensor_copy, 1, g_raw1[:], 0, 16)
-        up(0, 3)
-        gate(0, 2)
-        quantize(gw[1][:], gs[1][:], g_bf[1][:])
-        up(1, 0)
-        gate(0, 3)
-        up(1, 1)
-        gate(1, 0)
-        up(1, 2)
-        quantize_h(0, 0, 1)
-        up(1, 3)
-        cast_wd(nc.scalar.copy, 0, 0, 512)
-        gate(1, 1)
-        gate(1, 2)
-        up(0, 4)
-        quantize(dw[0][:], ds[0][:], d_bf[0][:])
-        gate(1, 3)
-        cast_wd(nc.vector.tensor_copy, 1, 0, 192)
-        cast_wd(nc.scalar.copy, 1, 192, 512)
-        up(1, 4)
-        up(0, 5)
-        gate(0, 4)
-        quantize_h(0, 1, 2)
-        quantize(dw[1][:], ds[1][:], d_bf[1][:])
-        up(1, 5)
+        cast_wg(nc.scalar.copy, g_bf0, g_raw00[:], 0, 8)
+        cast_wg(nc.vector.tensor_copy, g_bf0, g_raw01[:], 8, 16)
+        bias = tile("bias", [P, 4], F32, tag="g_raw01_then_bias")
+        with nc.allow_non_contiguous_dma(reason="one bias value to a partition"):
+            nc.sync.dma_start(bias[:], b.rearrange("(u p) -> p u", p=P))
+        quantize(gw[0][:, 0:256], gs[0][:, 0:256], g_bf0[:, 0:1024])
+        quantize(gw[0][:, 256:512], gs[0][:, 256:512], g_bf0[:, 1024:2048])
+        for c in range(CHUNKS):
+            up(0, c)
+            gate(0, c)
+            if c == 5:
+                cast_wg(nc.vector.tensor_copy, g_bf1, g_raw1[:], 0, 16)
+            if c == 6:
+                quantize(gw[1][:], gs[1][:], g_bf1[:])
+        d_bf0 = tile("d_bf0", [P, 4 * N], BF16)
+        d_bf1 = tile("d_bf1", [P, 4 * N], BF16)
+        for c in range(4):
+            up(1, c)
+            gate(1, c)
+            if c == 1:
+                cast_wd(nc.scalar.copy, d_bf0, 0, 160, N)
+        cast_wd(nc.vector.tensor_copy, d_bf0, 0, 0, 160)
+        cast_wd(nc.scalar.copy, d_bf1, 1, 0, N)
+        quantize_h(0, 0, 4)
+        quantize(dw[0][:], ds[0][:], d_bf0[:])
+        quantize_h(1, 0, 4)
+        quantize(dw[1][:], ds[1][:], d_bf1[:])
+        for c in range(4, CHUNKS):
+            up(1, c)
         gate(1, 4)
-        down(0, 0, False)
-        store(0, 0, 1)
-        up(0, 6)
-        gate(0, 5)
-        down(0, 1, False)
-        store(0, 1, 2)
-        up(1, 6)
+        quantize_h(0, 4, 8)
         gate(1, 5)
-        down(0, 2, False)
-        store(0, 2, 3)
-        up(0, 7)
-        up(1, 7)
-        gate(0, 6)
-        down(0, 3, False)
-        store(0, 3, 4)
-        quantize_h(1, 0, 2)
         gate(1, 6)
-        gate(0, 7)
-        quantize_h(2, 0, 2)
+        quantize_h(1, 4, 6)
         gate(1, 7)
-        quantize_h(3, 0, 1)
+        quantize_h(1, 6, 7)
+        quantize_h(1, 7, 8)
+        for u in range(4):
+            down(0, u, False)
+            store(0, u, u + 1)
         down(1, 0, False)
         store(1, 0, 2)
         down(1, 2, False)
         store(1, 2, 4)
-        quantize_h(3, 1, 2)
         down(2, 0, False)
         down(2, 2, True)
         store(2, 0, 4)
@@ -278,7 +250,7 @@ def tile_list_gmlpt_relu_bias_kernel(tc, tab_words, tab_scales, wg, wu_words, wu
         last_banks += [ps_v.tile([P, CHUNK], F32, name="bank_v") for u in range(2)]
         for a in range(PASSES):
             for u in (0, 2, 1, 3):
-                down_pass(last_banks[u], 3, u, a)
+                down_pass(last_banks[u][:], 3, u, a)
         for u in range(2):
             nc.scalar.activation(y_sb[3][:, u, :], last_banks[u][:], ACT.Identity, bias=bias[:, u : u + 1])
         for u in range(2, 4):

@@ -103,6 +103,19 @@ def tile_list_gmlpt_relu_bias_kernel(tc, tab_words, tab_scales, wg, wu_words, wu
             for u in range(2):
                 copy(dst[:, u, q0:q1], src[:, u])
 
+        def pool_round(dst, src):
+            nc.gpsimd.tensor_scalar(dst, src, 1.0, 0.0, ALU.mult, ALU.add)
+
+        def cast_wg_pool(dst_tile, raw):
+            dst = dst_tile[:].rearrange("p (t q s i) -> p t q s i", t=4, q=16, s=8, i=4)
+            src = raw.rearrange("p i (q t s) -> p t q s i", t=4, s=8)
+            for t in range(4):
+                pool_round(dst[:, t], src[:, t])
+
+        def cast_wd_pool(dst_tile, a, n0, n1):
+            dst = dst_tile[:, 4 * n0 : 4 * n1].rearrange("p (c t) -> p c t", t=4)
+            pool_round(dst, d_raw[a][:, :, n0:n1].rearrange("p t c -> p c t"))
+
         def quantize(words, scales, src):
             nc.vector.quantize_mx(out=words.bitcast(FP8X4), scales=scales, in_=src)
 
@@ -206,21 +219,18 @@ def tile_list_gmlpt_relu_bias_kernel(tc, tab_words, tab_scales, wg, wu_words, wu
             nc.sync.dma_start(bias[:], b.rearrange("(u p) -> p u", p=P))
         quantize(gw[0][:, 0:256], gs[0][:, 0:256], g_bf0[:, 0:1024])
         quantize(gw[0][:, 256:512], gs[0][:, 256:512], g_bf0[:, 1024:2048])
+        cast_wg_pool(g_bf1, g_raw1[:])
+        d_bf0 = tile("d_bf0", [P, 4 * N], BF16)
+        d_bf1 = tile("d_bf1", [P, 4 * N], BF16)
+        for n0 in range(0, N, 128):
+            cast_wd_pool(d_bf0, 0, n0, n0 + 128)
         for c in range(CHUNKS):
             up(0, c)
             gate(0, c)
-            if c == 5:
-                cast_wg(nc.vector.tensor_copy, g_bf1, g_raw1[:], 0, 16)
-            if c == 6:
-                quantize(gw[1][:], gs[1][:], g_bf1[:])
-        d_bf0 = tile("d_bf0", [P, 4 * N], BF16)
-        d_bf1 = tile("d_bf1", [P, 4 * N], BF16)
+        quantize(gw[1][:], gs[1][:], g_bf1[:])
         for c in range(4):
             up(1, c)
             gate(1, c)
-            if c == 1:
-                cast_wd(nc.scalar.copy, d_bf0, 0, 160, N)
-        cast_wd(nc.vector.tensor_copy, d_bf0, 0, 0, 160)
         cast_wd(nc.scalar.copy, d_bf1, 1, 0, N)
         quantize_h(0, 0, 4)
         quantize(dw[0][:], ds[0][:], d_bf0[:])

@@ -36,16 +36,14 @@ def tile_list_gmlpt_relu_bias_kernel(tc, tab_words, tab_scales, wg, wu_words, wu
 
         offsets = keep.tile([P, J // 16], U16, name="offsets")
         tw = tile("tw", [P, T], I32, tag="tw_then_d_raw1")
-        ts = tile("ts", [P, T // 4], I32, tag="ts_then_g_raw1")
+        ts = tile("ts", [P, T // 4], I32, tag="ts_then_g_raw")
         uw_raw = tile("uw_raw", [P, R // 2], I32)
-        us_raw = tile("us_raw", [P, R // 4], I32, tag="us_raw_then_d_raw0")
+        us_raw = tile("us_raw", [P, R // 4], I32)
         uw = tile("uw", [P, R // 2], I32)
         us = tile("us", [P, R // 4], I32)
         vw = [tile("vw%d" % hf, [P, J // 2], U32) for hf in range(2)]
-        vs_raw = tile("vs_raw", [P, J], U8)
+        vs_raw = tile("vs_raw", [P, J], U8, tag="vs_raw_then_d_raw0")
         vs = tile("vs", [P, J], U8)
-        g_raw00 = tile("g_raw00", [P, 4, 256], F32, tag="g_raw00_then_ub00")
-        g_raw01 = tile("g_raw01", [P, 4, 256], F32, tag="g_raw01_then_bias")
         g_bf0 = tile("g_bf0", [P, 2048], BF16)
         g_bf1 = tile("g_bf1", [P, 2048], BF16)
         gw = [tile("gw%d" % a, [P, 512], U32) for a in range(PASSES)]
@@ -69,14 +67,15 @@ def tile_list_gmlpt_relu_bias_kernel(tc, tab_words, tab_scales, wg, wu_words, wu
         for r in range(4):
             nc.sync.dma_start(us_raw[r:P:32, :], us_rows[r:16:4, :])
         nc.sync.dma_start(tw[:], tab_words[0].rearrange("p t i -> p (t i)").bitcast(I32))
-        nc.sync.dma_start(g_raw00[:], wg_rows[:, :, 0:256])
-        nc.sync.dma_start(g_raw01[:], wg_rows[:, :, 256:512])
 
         nc.vector.tensor_copy(vs_raw[:], ts[:].bitcast(U8).indirect(offsets[:]))
         for r in range(4):
             nc.sync.dma_start(vs[r:P:32, :].bitcast(I32), vs_raw[ROW0 + r : P : 4, :].bitcast(I32))
-        g_raw1 = tile("g_raw1", [P, 4, 512], F32, tag="ts_then_g_raw1")
-        nc.sync.dma_start(g_raw1[:], wg_rows[:, :, 512:1024])
+        g_raw = tile("g_raw", [P, 4 * R], F32, tag="ts_then_g_raw")
+        g_parts = []
+        for r0, r1 in ((0, 256), (256, 512), (512, 1024)):
+            g_parts.append(g_raw[:, 4 * r0 : 4 * r1].rearrange("p (i r) -> p i r", i=4))
+            nc.sync.dma_start(g_parts[-1], wg_rows[:, :, r0:r1])
 
         nc.vector.tensor_copy(
             uw[:].rearrange("p (a t q w) -> p a t q w", a=2, t=4, w=4),
@@ -91,7 +90,7 @@ def tile_list_gmlpt_relu_bias_kernel(tc, tab_words, tab_scales, wg, wu_words, wu
         for hf in range(2):
             nc.vector.tensor_copy(vw[hf][:], tw[:].bitcast(U32).indirect(offsets[:, 32 * hf : 32 * (hf + 1)]))
 
-        d_raw = [tile("d_raw0", [P, 4, N], F32, tag="us_raw_then_d_raw0"), tile("d_raw1", [P, 4, N], F32, tag="tw_then_d_raw1")]
+        d_raw = [tile("d_raw0", [P, 4, N], F32, tag="vs_raw_then_d_raw0"), tile("d_raw1", [P, 4, N], F32, tag="tw_then_d_raw1")]
         for a in range(PASSES):
             rows = wd[512 * a : 512 * (a + 1), :].rearrange("(q t s) n -> t q s n", t=4, s=8)
             for t in range(4):
@@ -133,9 +132,9 @@ def tile_list_gmlpt_relu_bias_kernel(tc, tab_words, tab_scales, wg, wu_words, wu
                     start=True,
                     stop=True,
                 )
-            ub[a, c] = tile("ub%d%d" % (a, c), [P, 4 * CHUNK], F32, tag="g_raw00_then_ub00" if (a, c) == (0, 0) else None)
+            ub[a, c] = g_raw[:, 512 * c : 512 * (c + 1)] if a == 0 and c < 4 else tile("ub%d%d" % (a, c), [P, 4 * CHUNK], F32)[:]
             nc.scalar.activation(
-                ub[a, c][:].rearrange("p (j t) -> p j t", t=4),
+                ub[a, c].rearrange("p (j t) -> p j t", t=4),
                 bank[:].rearrange("p t j -> p j t"),
                 ACT.Copy,
             )
@@ -157,7 +156,7 @@ def tile_list_gmlpt_relu_bias_kernel(tc, tab_words, tab_scales, wg, wu_words, wu
                 out=h_bf[a][:, 512 * c : 512 * (c + 1)].rearrange("p (j t) -> p j t", t=4),
                 in0=bank[:].rearrange("p t j -> p j t"),
                 scalar=0.0,
-                in1=ub[a, c][:].rearrange("p (j t) -> p j t", t=4),
+                in1=ub[a, c].rearrange("p (j t) -> p j t", t=4),
                 op0=ALU.max,
                 op1=ALU.mult,
             )
@@ -212,14 +211,14 @@ def tile_list_gmlpt_relu_bias_kernel(tc, tab_words, tab_scales, wg, wu_words, wu
             out_rows = out.rearrange("(u p) j -> p u j", p=P)
             nc.sync.dma_start(out_rows[:, u0:u1, CHUNK * c0 : CHUNK * c1], y_sb[g][:, u0:u1, :])
 
-        cast_wg(nc.scalar.copy, g_bf0, g_raw00[:], 0, 8)
-        cast_wg(nc.vector.tensor_copy, g_bf0, g_raw01[:], 8, 16)
-        bias = tile("bias", [P, 4], F32, tag="g_raw01_then_bias")
-        with nc.allow_non_contiguous_dma(reason="one bias value to a partition"):
-            nc.sync.dma_start(bias[:], b.rearrange("(u p) -> p u", p=P))
+        cast_wg(nc.scalar.copy, g_bf0, g_parts[0], 0, 8)
+        cast_wg(nc.vector.tensor_copy, g_bf0, g_parts[1], 8, 16)
         quantize(gw[0][:, 0:256], gs[0][:, 0:256], g_bf0[:, 0:1024])
         quantize(gw[0][:, 256:512], gs[0][:, 256:512], g_bf0[:, 1024:2048])
-        cast_wg_pool(g_bf1, g_raw1[:])
+        cast_wg_pool(g_bf1, g_parts[2])
+        bias = g_raw[:, 2048:2052]
+        with nc.allow_non_contiguous_dma(reason="one bias value to a partition"):
+            nc.sync.dma_start(bias, b.rearrange("(u p) -> p u", p=P))
         d_bf0 = tile("d_bf0", [P, 4 * N], BF16)
         d_bf1 = tile("d_bf1", [P, 4 * N], BF16)
         for n0 in range(0, N, 128):

@@ -21,7 +21,8 @@ PASSES = 2
 CHUNK = 128
 CHUNKS = J // CHUNK
 ROW0 = P - 16
-Y_GROUPS = ((0, 4), (4, 6), (6, 7), (7, 8))
+PAIR = 2 * CHUNK
+LATE = ((1, 5), (0, 6), (1, 6), (0, 7))
 
 
 def tile_list_gmlpt_relu_bias_kernel(tc, tab_words, tab_scales, wg, wu_words, wu_scales, wd, b, offs, out):
@@ -29,31 +30,37 @@ def tile_list_gmlpt_relu_bias_kernel(tc, tab_words, tab_scales, wg, wu_words, wu
     with ExitStack() as ctx:
         keep = ctx.enter_context(tc.tile_pool(name="keep", bufs=1))
         ps_s = ctx.enter_context(tc.psum_pool(name="ps_s", bufs=4))
-        ps_v = ctx.enter_context(tc.psum_pool(name="ps_v", bufs=4))
+        ps_v = ctx.enter_context(tc.psum_pool(name="ps_v", bufs=1))
+        v_turn = list(range(4)) * 8
 
         def tile(name, shape, dtype, tag=None):
             return keep.tile(shape, dtype, name=name, tag=tag or name, align_bytes=64)
 
+        def vector_bank(shape):
+            return ps_v.tile(shape, F32, name="bank_v%d" % v_turn.pop(0))
+
         offsets = keep.tile([P, J // 16], U16, name="offsets")
         tw = tile("tw", [P, T], I32, tag="tw_then_d_raw1")
-        ts = tile("ts", [P, T // 4], I32, tag="ts_then_g_raw")
+        ts = tile("ts", [P, T // 4], I32, tag="ts_then_g_late")
         uw_raw = tile("uw_raw", [P, R // 2], I32)
-        us_raw = tile("us_raw", [P, R // 4], I32)
+        us_raw = tile("us_raw", [P, R // 4], I32, tag="us_raw_then_d_raw0")
         uw = tile("uw", [P, R // 2], I32)
         us = tile("us", [P, R // 4], I32)
         vw = [tile("vw%d" % hf, [P, J // 2], U32) for hf in range(2)]
-        vs_raw = tile("vs_raw", [P, J], U8, tag="vs_raw_then_d_raw0")
+        vs_raw = tile("vs_raw", [P, J], U8)
         vs = tile("vs", [P, J], U8)
-        g_bf0 = tile("g_bf0", [P, 2048], BF16)
-        g_bf1 = tile("g_bf1", [P, 2048], BF16)
+        g_early = tile("g_early", [P, 4 * 256], F32)
+        g_bf = [tile("g_bf0", [P, 2048], BF16), tile("g_bf1", [P, 2048], BF16, tag="g_bf1_then_hw0")]
         gw = [tile("gw%d" % a, [P, 512], U32) for a in range(PASSES)]
         gs = [tile("gs%d" % a, [P, 512], U8) for a in range(PASSES)]
+        h0_flat = tile("h0_flat", [P, 1024 + 4 * J], BF16)
+        d_bf1 = tile("d_bf1", [P, 4 * N], BF16)
+        d_bf = [h0_flat[:, 0 : 4 * N], d_bf1[:]]
         dw = [tile("dw%d" % a, [P, N], U32) for a in range(PASSES)]
         ds = [tile("ds%d" % a, [P, N], U8) for a in range(PASSES)]
-        h_bf = [tile("h_bf%d" % a, [P, 4 * J], BF16) for a in range(PASSES)]
-        hw = [tile("hw%d" % a, [P, J], U32) for a in range(PASSES)]
+        h_bf = [h0_flat[:, 1024 : 1024 + 4 * J], tile("h_bf1", [P, 4 * J], BF16)[:]]
+        hw = {1: tile("hw1", [P, J], U32)}
         hs = [tile("hs%d" % a, [P, J], U8) for a in range(PASSES)]
-        y_sb = [tile("y_sb%d" % g, [P, 4, CHUNK * (c1 - c0)], F32) for g, (c0, c1) in enumerate(Y_GROUPS)]
         ub = {}
 
         nc.vector.memset(ts[0:ROW0, :], 0)
@@ -67,14 +74,15 @@ def tile_list_gmlpt_relu_bias_kernel(tc, tab_words, tab_scales, wg, wu_words, wu
         for r in range(4):
             nc.sync.dma_start(us_raw[r:P:32, :], us_rows[r:16:4, :])
         nc.sync.dma_start(tw[:], tab_words[0].rearrange("p t i -> p (t i)").bitcast(I32))
+        g_parts = [g_early[:].rearrange("p (i r) -> p i r", i=4)]
+        nc.sync.dma_start(g_parts[0], wg_rows[:, :, 0:256])
 
         nc.vector.tensor_copy(vs_raw[:], ts[:].bitcast(U8).indirect(offsets[:]))
         for r in range(4):
             nc.sync.dma_start(vs[r:P:32, :].bitcast(I32), vs_raw[ROW0 + r : P : 4, :].bitcast(I32))
-        g_raw = tile("g_raw", [P, 4 * R], F32, tag="ts_then_g_raw")
-        g_parts = []
-        for r0, r1 in ((0, 256), (256, 512), (512, 1024)):
-            g_parts.append(g_raw[:, 4 * r0 : 4 * r1].rearrange("p (i r) -> p i r", i=4))
+        g_late = tile("g_late", [P, 4 * (R - 256)], F32, tag="ts_then_g_late")
+        for r0, r1 in ((256, 512), (512, 1024)):
+            g_parts.append(g_late[:, 4 * (r0 - 256) : 4 * (r1 - 256)].rearrange("p (i r) -> p i r", i=4))
             nc.sync.dma_start(g_parts[-1], wg_rows[:, :, r0:r1])
 
         nc.vector.tensor_copy(
@@ -90,14 +98,19 @@ def tile_list_gmlpt_relu_bias_kernel(tc, tab_words, tab_scales, wg, wu_words, wu
         for hf in range(2):
             nc.vector.tensor_copy(vw[hf][:], tw[:].bitcast(U32).indirect(offsets[:, 32 * hf : 32 * (hf + 1)]))
 
-        d_raw = [tile("d_raw0", [P, 4, N], F32, tag="vs_raw_then_d_raw0"), tile("d_raw1", [P, 4, N], F32, tag="tw_then_d_raw1")]
+        d_raw0 = tile("d_raw0", [P, 4 * N], F32, tag="us_raw_then_d_raw0")
+        d_last = tile("d_last", [P, 4 * N + 16], F32, tag="tw_then_d_raw1")
+        d_raw = [flat[:, 0 : 4 * N].rearrange("p (t n) -> p t n", t=4) for flat in (d_raw0, d_last)]
+        bias = d_last[:, 4 * N : 4 * N + 4]
         for a in range(PASSES):
             rows = wd[512 * a : 512 * (a + 1), :].rearrange("(q t s) n -> t q s n", t=4, s=8)
             for t in range(4):
                 nc.sync.dma_start(d_raw[a][:, t, :], rows[t])
+        with nc.allow_non_contiguous_dma(reason="one bias value to a partition"):
+            nc.sync.dma_start(bias, b.rearrange("(u p) -> p u", p=P))
 
-        def cast_wg(copy, dst_tile, raw, q0, q1):
-            dst = dst_tile[:].rearrange("p (t q u v i) -> p u q t i v", t=4, q=16, u=2, v=4, i=4)
+        def cast_wg(copy, raw, q0, q1):
+            dst = g_bf[0][:].rearrange("p (t q u v i) -> p u q t i v", t=4, q=16, u=2, v=4, i=4)
             src = raw.rearrange("p i (q t u v) -> p u q t i v", t=4, u=2, v=4)
             for u in range(2):
                 copy(dst[:, u, q0:q1], src[:, u])
@@ -105,15 +118,19 @@ def tile_list_gmlpt_relu_bias_kernel(tc, tab_words, tab_scales, wg, wu_words, wu
         def pool_round(dst, src):
             nc.gpsimd.tensor_scalar(dst, src, 1.0, 0.0, ALU.mult, ALU.add)
 
-        def cast_wg_pool(dst_tile, raw):
-            dst = dst_tile[:].rearrange("p (t q s i) -> p t q s i", t=4, q=16, s=8, i=4)
+        def cast_wg_pool(raw):
+            dst = g_bf[1][:].rearrange("p (t q s i) -> p t q s i", t=4, q=16, s=8, i=4)
             src = raw.rearrange("p i (q t s) -> p t q s i", t=4, s=8)
             for t in range(4):
                 pool_round(dst[:, t], src[:, t])
 
-        def cast_wd_pool(dst_tile, a, n0, n1):
-            dst = dst_tile[:, 4 * n0 : 4 * n1].rearrange("p (c t) -> p c t", t=4)
+        def cast_wd_pool(a, n0, n1):
+            dst = d_bf[a][:, 4 * n0 : 4 * n1].rearrange("p (c t) -> p c t", t=4)
             pool_round(dst, d_raw[a][:, :, n0:n1].rearrange("p t c -> p c t"))
+
+        def cast_wd_scalar(a, n0, n1):
+            dst = d_bf[a][:, 4 * n0 : 4 * n1].rearrange("p (c v t) -> p c t v", t=4, v=4)
+            nc.scalar.copy(dst, d_raw[a][:, :, n0:n1].rearrange("p t (c v) -> p c t v", v=4))
 
         def quantize(words, scales, src):
             nc.vector.quantize_mx(out=words.bitcast(FP8X4), scales=scales, in_=src)
@@ -132,7 +149,17 @@ def tile_list_gmlpt_relu_bias_kernel(tc, tab_words, tab_scales, wg, wu_words, wu
                     start=True,
                     stop=True,
                 )
-            ub[a, c] = g_raw[:, 512 * c : 512 * (c + 1)] if a == 0 and c < 4 else tile("ub%d%d" % (a, c), [P, 4 * CHUNK], F32)[:]
+            if a == 0 and c < 2:
+                ub[a, c] = g_early[:, 512 * c : 512 * (c + 1)]
+            elif a == 0 and c < 4:
+                ub[a, c] = g_late[:, 512 * (c - 2) : 512 * (c - 1)]
+            elif (a, c) in LATE:
+                k = LATE.index((a, c))
+                ub[a, c] = d_last[:, 512 * k : 512 * (k + 1)]
+            elif (a, c) == (1, 7):
+                ub[a, c] = d_bf1[:].bitcast(F32)[:, 0:512]
+            else:
+                ub[a, c] = tile("ub%d%d" % (a, c), [P, 4 * CHUNK], F32)[:]
             nc.scalar.activation(
                 ub[a, c].rearrange("p (j t) -> p j t", t=4),
                 bank[:].rearrange("p t j -> p j t"),
@@ -141,7 +168,7 @@ def tile_list_gmlpt_relu_bias_kernel(tc, tab_words, tab_scales, wg, wu_words, wu
 
         def gate(a, c):
             cols = slice(CHUNK * c, CHUNK * (c + 1))
-            bank = ps_v.tile([P, 4, CHUNK], F32, name="bank_v")
+            bank = vector_bank([P, 4, CHUNK])
             for t in range(4):
                 nc.tensor.matmul_mx(
                     out=bank[:, t, :],
@@ -165,13 +192,7 @@ def tile_list_gmlpt_relu_bias_kernel(tc, tab_words, tab_scales, wg, wu_words, wu
             cols = slice(CHUNK * c0, CHUNK * c1)
             quantize(hw[a][:, cols], hs[a][:, cols], h_bf[a][:, 4 * cols.start : 4 * cols.stop])
 
-        def cast_wd(copy, dst_tile, a, n0, n1):
-            dst = dst_tile[:, 4 * n0 : 4 * n1].rearrange("p (c v t) -> p c t v", t=4, v=4)
-            src = d_raw[a][:, :, n0:n1].rearrange("p t (c v) -> p c t v", v=4)
-            copy(dst, src)
-
-        def down_pass(bank, g, u, a):
-            c0, c1 = Y_GROUPS[g]
+        def down_pass(bank, c0, c1, u, a):
             cols = slice(CHUNK * c0, CHUNK * c1)
             nc.tensor.matmul_mx(
                 out=bank,
@@ -183,85 +204,102 @@ def tile_list_gmlpt_relu_bias_kernel(tc, tab_words, tab_scales, wg, wu_words, wu
                 stop=(a == PASSES - 1),
             )
 
-        def down(g, u0, on_vector):
-            c0, c1 = Y_GROUPS[g]
+        def down(y, c0, c1, u0, on_vector):
             width = CHUNK * (c1 - c0)
-            per_bank = 1 if width == 512 else 2
             if on_vector:
-                bank = ps_v.tile([P, per_bank, width], F32, name="bank_v")
+                bank = vector_bank([P, 2, width])
             else:
-                bank = ps_s.tile([P, per_bank, width], F32, name="bank_s")
-            for e in range(per_bank):
+                bank = ps_s.tile([P, 2, width], F32, name="bank_s")
+            for e in range(2):
                 for a in range(PASSES):
-                    down_pass(bank[:, e, :], g, u0 + e, a)
+                    down_pass(bank[:, e, :], c0, c1, u0 + e, a)
             if on_vector:
                 nc.vector.tensor_tensor(
-                    y_sb[g][:, u0 : u0 + 2, :],
+                    y[:, u0 : u0 + 2, :],
                     bank[:],
                     bias[:, u0 : u0 + 2].unsqueeze(2).to_broadcast([P, 2, width]),
                     ALU.add,
                 )
             else:
-                for e in range(per_bank):
+                for e in range(2):
                     u = u0 + e
-                    nc.scalar.activation(y_sb[g][:, u, :], bank[:, e, :], ACT.Identity, bias=bias[:, u : u + 1])
+                    nc.scalar.activation(y[:, u, :], bank[:, e, :], ACT.Identity, bias=bias[:, u : u + 1])
 
-        def store(g, u0, u1):
-            c0, c1 = Y_GROUPS[g]
-            out_rows = out.rearrange("(u p) j -> p u j", p=P)
-            nc.sync.dma_start(out_rows[:, u0:u1, CHUNK * c0 : CHUNK * c1], y_sb[g][:, u0:u1, :])
+        out_rows = out.rearrange("(u p) j -> p u j", p=P)
 
-        cast_wg(nc.scalar.copy, g_bf0, g_parts[0], 0, 8)
-        cast_wg(nc.vector.tensor_copy, g_bf0, g_parts[1], 8, 16)
-        quantize(gw[0][:, 0:256], gs[0][:, 0:256], g_bf0[:, 0:1024])
-        quantize(gw[0][:, 256:512], gs[0][:, 256:512], g_bf0[:, 1024:2048])
-        cast_wg_pool(g_bf1, g_parts[2])
-        bias = g_raw[:, 2048:2052]
-        with nc.allow_non_contiguous_dma(reason="one bias value to a partition"):
-            nc.sync.dma_start(bias, b.rearrange("(u p) -> p u", p=P))
-        d_bf0 = tile("d_bf0", [P, 4 * N], BF16)
-        d_bf1 = tile("d_bf1", [P, 4 * N], BF16)
-        for n0 in range(0, N, 128):
-            cast_wd_pool(d_bf0, 0, n0, n0 + 128)
-        for c in range(CHUNKS):
+        def store(y, c0, c1, u0, u1):
+            nc.sync.dma_start(out_rows[:, u0:u1, CHUNK * c0 : CHUNK * c1], y[:, u0:u1, :])
+
+        def output_wide(y, u):
+            bank = ps_s.tile([P, 4 * CHUNK], F32, name="bank_s")
+            for a in range(PASSES):
+                down_pass(bank[:], 0, 4, u, a)
+            nc.scalar.activation(y[:, u, :], bank[:], ACT.Identity, bias=bias[:, u : u + 1])
+            store(y, 0, 4, u, u + 1)
+
+        def outputs(g, share):
+            y = tile("y%d" % g, [P, 4, PAIR], F32)
+            for u0 in (0, 2):
+                down(y, 2 * g, 2 * g + 2, u0, share and u0 == 2)
+                store(y, 2 * g, 2 * g + 2, u0, u0 + 2)
+
+        cast_wg(nc.scalar.copy, g_parts[0], 0, 8)
+        cast_wg(nc.vector.tensor_copy, g_parts[1], 8, 16)
+        quantize(gw[0][:, 0:256], gs[0][:, 0:256], g_bf[0][:, 0:1024])
+        quantize(gw[0][:, 256:512], gs[0][:, 256:512], g_bf[0][:, 1024:2048])
+        cast_wg_pool(g_parts[2])
+        for c in range(6):
             up(0, c)
             gate(0, c)
-        quantize(gw[1][:], gs[1][:], g_bf1[:])
+        quantize(gw[1][:], gs[1][:], g_bf[1][:])
+        hw[0] = tile("hw0", [P, J], U32, tag="g_bf1_then_hw0")
+        quantize_h(0, 0, 4)
+        for n0 in (256, 384):
+            cast_wd_pool(0, n0, n0 + 128)
+        cast_wd_scalar(0, 0, 256)
         for c in range(4):
             up(1, c)
             gate(1, c)
-        cast_wd(nc.scalar.copy, d_bf1, 1, 0, N)
-        quantize_h(0, 0, 4)
-        quantize(dw[0][:], ds[0][:], d_bf0[:])
+        up(1, 4)
+        cast_wd_scalar(1, 0, N)
+        quantize(dw[1][:], ds[1][:], d_bf[1])
         quantize_h(1, 0, 4)
-        quantize(dw[1][:], ds[1][:], d_bf1[:])
-        for c in range(4, CHUNKS):
-            up(1, c)
+        quantize(dw[0][:], ds[0][:], d_bf[0])
+        y0 = tile("y0", [P, 4, 4 * CHUNK], F32)
+        up(1, 5)
+        up(0, 6)
         gate(1, 4)
-        quantize_h(0, 4, 8)
+        output_wide(y0, 0)
+        up(1, 6)
         gate(1, 5)
-        gate(1, 6)
+        output_wide(y0, 1)
+        up(0, 7)
+        output_wide(y0, 2)
+        quantize_h(0, 4, 6)
         quantize_h(1, 4, 6)
-        gate(1, 7)
+        up(1, 7)
+        output_wide(y0, 3)
+        gate(0, 6)
+        gate(1, 6)
+        outputs(2, False)
+        quantize_h(0, 6, 7)
+        gate(0, 7)
         quantize_h(1, 6, 7)
+        gate(1, 7)
+        y6 = tile("y6", [P, 4, CHUNK], F32)
+        down(y6, 6, 7, 0, False)
+        down(y6, 6, 7, 2, False)
+        store(y6, 6, 7, 0, 4)
+        quantize_h(0, 7, 8)
         quantize_h(1, 7, 8)
-        for u in range(4):
-            down(0, u, False)
-            store(0, u, u + 1)
-        down(1, 0, False)
-        store(1, 0, 2)
-        down(1, 2, False)
-        store(1, 2, 4)
-        down(2, 0, False)
-        down(2, 2, True)
-        store(2, 0, 4)
+        y7 = tile("y7", [P, 4, CHUNK], F32)
         last_banks = [ps_s.tile([P, CHUNK], F32, name="bank_s") for u in range(2)]
-        last_banks += [ps_v.tile([P, CHUNK], F32, name="bank_v") for u in range(2)]
+        last_banks += [vector_bank([P, CHUNK]) for u in range(2)]
         for a in range(PASSES):
             for u in (0, 2, 1, 3):
-                down_pass(last_banks[u][:], 3, u, a)
+                down_pass(last_banks[u][:], 7, 8, u, a)
         for u in range(2):
-            nc.scalar.activation(y_sb[3][:, u, :], last_banks[u][:], ACT.Identity, bias=bias[:, u : u + 1])
+            nc.scalar.activation(y7[:, u, :], last_banks[u][:], ACT.Identity, bias=bias[:, u : u + 1])
         for u in range(2, 4):
-            nc.vector.tensor_scalar_add(y_sb[3][:, u, :], last_banks[u][:], bias[:, u : u + 1])
-        store(3, 0, 4)
+            nc.vector.tensor_scalar_add(y7[:, u, :], last_banks[u][:], bias[:, u : u + 1])
+        store(y7, 7, 8, 0, 4)

@@ -18,20 +18,26 @@ ACT = mybir.ActivationFunctionType
 
 P = 128
 PASSES = 2
+PASS = R // PASSES
 CHUNK = 128
-CHUNKS = J // CHUNK
-ROW0 = P - 16
-PAIR = 2 * CHUNK
-LATE = ((1, 5), (0, 6), (1, 6), (0, 7))
+BANK = 4 * CHUNK
+BANKS = 4
+SCALE_ROWS = 16
+ROW0 = P - SCALE_ROWS
+WG_FIRST = 256
+WD_SCALAR = 256
+AHEAD = 6
+WIDE = 4
+AFTER_WD = ((1, 5), (0, 6), (1, 6), (0, 7))
 
 
 def tile_list_gmlpt_relu_bias_kernel(tc, tab_words, tab_scales, wg, wu_words, wu_scales, wd, b, offs, out):
     nc = tc.nc
     with ExitStack() as ctx:
         keep = ctx.enter_context(tc.tile_pool(name="keep", bufs=1))
-        ps_s = ctx.enter_context(tc.psum_pool(name="ps_s", bufs=4))
+        ps_s = ctx.enter_context(tc.psum_pool(name="ps_s", bufs=BANKS))
         ps_v = ctx.enter_context(tc.psum_pool(name="ps_v", bufs=1))
-        v_turn = list(range(4)) * 8
+        v_turn = list(range(BANKS)) * 5
 
         def tile(name, shape, dtype, tag=None):
             return keep.tile(shape, dtype, name=name, tag=tag or name, align_bytes=64)
@@ -44,122 +50,132 @@ def tile_list_gmlpt_relu_bias_kernel(tc, tab_words, tab_scales, wg, wu_words, wu
         ts = tile("ts", [P, T // 4], I32, tag="ts_then_g_late")
         uw_raw = tile("uw_raw", [P, R // 2], I32)
         us_raw = tile("us_raw", [P, R // 4], I32, tag="us_raw_then_d_raw0")
-        uw = tile("uw", [P, R // 2], I32)
-        us = tile("us", [P, R // 4], I32)
-        vw = [tile("vw%d" % hf, [P, J // 2], U32) for hf in range(2)]
+        us_all = tile("us_all", [P, R // 4], I32)
+        uw = [tile("uw%d" % a, [P, 2 * PASS], U8) for a in range(PASSES)]
+        us = [tile("us%d" % a, [P, PASS], U8) for a in range(PASSES)]
+        vw = [tile("vw%d" % half, [P, J // 2], U32) for half in range(2)]
         vs_raw = tile("vs_raw", [P, J], U8)
         vs = tile("vs", [P, J], U8)
-        g_early = tile("g_early", [P, 4 * 256], F32)
-        g_bf = [tile("g_bf0", [P, 2048], BF16), tile("g_bf1", [P, 2048], BF16, tag="g_bf1_then_hw0")]
-        gw = [tile("gw%d" % a, [P, 512], U32) for a in range(PASSES)]
-        gs = [tile("gs%d" % a, [P, 512], U8) for a in range(PASSES)]
-        h0_flat = tile("h0_flat", [P, 1024 + 4 * J], BF16)
+        g_early = tile("g_early", [P, 4 * WG_FIRST], F32)
+        g_bf = [tile("g_bf0", [P, 4 * PASS], BF16), tile("g_bf1", [P, 4 * PASS], BF16, tag="g_bf1_then_hw0")]
+        gw = [tile("gw%d" % a, [P, PASS], U32) for a in range(PASSES)]
+        gs = [tile("gs%d" % a, [P, PASS], U8) for a in range(PASSES)]
+        h0_flat = tile("h0_flat", [P, 4 * WD_SCALAR + 4 * J], BF16)
         d_bf1 = tile("d_bf1", [P, 4 * N], BF16)
         d_bf = [h0_flat[:, 0 : 4 * N], d_bf1[:]]
         dw = [tile("dw%d" % a, [P, N], U32) for a in range(PASSES)]
         ds = [tile("ds%d" % a, [P, N], U8) for a in range(PASSES)]
-        h_bf = [h0_flat[:, 1024 : 1024 + 4 * J], tile("h_bf1", [P, 4 * J], BF16)[:]]
+        h_bf = [h0_flat[:, 4 * WD_SCALAR : 4 * WD_SCALAR + 4 * J], tile("h_bf1", [P, 4 * J], BF16)[:]]
         hw = {1: tile("hw1", [P, J], U32)}
         hs = [tile("hs%d" % a, [P, J], U8) for a in range(PASSES)]
         ub = {}
 
         nc.vector.memset(ts[0:ROW0, :], 0)
-        nc.gpsimd.memset(us[:], 0)
+        nc.gpsimd.memset(us_all[:], 0)
         nc.gpsimd.memset(vs[:].bitcast(I32), 0)
+
         us_rows = wu_scales[0].bitcast(I32)
         wg_rows = wg.rearrange("(p i) r -> p i r", i=4)
         nc.sync.dma_start(offsets[:], offs)
         nc.sync.dma_start(ts[ROW0:P, :], tab_scales[0].bitcast(I32))
         nc.sync.dma_start(uw_raw[:], wu_words[0].bitcast(I32))
-        for r in range(4):
-            nc.sync.dma_start(us_raw[r:P:32, :], us_rows[r:16:4, :])
+        for e in range(4):
+            nc.sync.dma_start(us_raw[e:P:32, :], us_rows[e:SCALE_ROWS:4, :])
         nc.sync.dma_start(tw[:], tab_words[0].rearrange("p t i -> p (t i)").bitcast(I32))
         g_parts = [g_early[:].rearrange("p (i r) -> p i r", i=4)]
-        nc.sync.dma_start(g_parts[0], wg_rows[:, :, 0:256])
+        nc.sync.dma_start(g_parts[0], wg_rows[:, :, 0:WG_FIRST])
 
         nc.vector.tensor_copy(vs_raw[:], ts[:].bitcast(U8).indirect(offsets[:]))
-        for r in range(4):
-            nc.sync.dma_start(vs[r:P:32, :].bitcast(I32), vs_raw[ROW0 + r : P : 4, :].bitcast(I32))
-        g_late = tile("g_late", [P, 4 * (R - 256)], F32, tag="ts_then_g_late")
-        for r0, r1 in ((256, 512), (512, 1024)):
-            g_parts.append(g_late[:, 4 * (r0 - 256) : 4 * (r1 - 256)].rearrange("p (i r) -> p i r", i=4))
+        for e in range(4):
+            nc.sync.dma_start(vs[e:P:32, :].bitcast(I32), vs_raw[ROW0 + e : P : 4, :].bitcast(I32))
+        g_late = tile("g_late", [P, 4 * (R - WG_FIRST)], F32, tag="ts_then_g_late")
+        for r0, r1 in ((WG_FIRST, PASS), (PASS, R)):
+            g_parts.append(g_late[:, 4 * (r0 - WG_FIRST) : 4 * (r1 - WG_FIRST)].rearrange("p (i r) -> p i r", i=4))
             nc.sync.dma_start(g_parts[-1], wg_rows[:, :, r0:r1])
 
         nc.vector.tensor_copy(
-            uw[:].rearrange("p (a t q w) -> p a t q w", a=2, t=4, w=4),
-            uw_raw[:].rearrange("p (a q t w) -> p a t q w", a=2, t=4, w=4),
+            uw[0][:].rearrange("p (t m b) -> p t m b", t=4, b=2),
+            uw_raw[:, 0 : PASS // 2].bitcast(U8).rearrange("p (m t b) -> p t m b", t=4, b=2),
         )
-        for quad in range(4):
-            rows = slice(32 * quad, 32 * quad + 4)
-            nc.vector.tensor_copy(
-                us[rows, :].rearrange("p (a t q w) -> p a t q w", a=2, t=4, w=2),
-                us_raw[rows, :].rearrange("p (a q t w) -> p a t q w", a=2, t=4, w=2),
-            )
-        for hf in range(2):
-            nc.vector.tensor_copy(vw[hf][:], tw[:].bitcast(U32).indirect(offsets[:, 32 * hf : 32 * (hf + 1)]))
+        nc.vector.tensor_copy(
+            uw[1][:].bitcast(I32).rearrange("p (t q w) -> p t q w", t=4, w=4),
+            uw_raw[:, PASS // 2 : PASS].rearrange("p (q t w) -> p t q w", t=4, w=4),
+        )
+        for quadrant in range(4):
+            live = slice(32 * quadrant, 32 * quadrant + 4)
+            nc.vector.tensor_copy(us_all[live, :], us_raw[live, :])
+        nc.vector.tensor_copy(
+            us[0][:].rearrange("p (t m) -> p t m", t=4),
+            us_all[:, 0 : PASS // 4].bitcast(U8).rearrange("p (m t) -> p t m", t=4),
+        )
+        nc.vector.tensor_copy(
+            us[1][:].bitcast(I32).rearrange("p (t q w) -> p t q w", t=4, w=2),
+            us_all[:, PASS // 4 : PASS // 2].rearrange("p (q t w) -> p t q w", t=4, w=2),
+        )
+        for half in range(2):
+            nc.vector.tensor_copy(vw[half][:], tw[:].bitcast(U32).indirect(offsets[:, 32 * half : 32 * (half + 1)]))
 
         d_raw0 = tile("d_raw0", [P, 4 * N], F32, tag="us_raw_then_d_raw0")
         d_last = tile("d_last", [P, 4 * N + 16], F32, tag="tw_then_d_raw1")
         d_raw = [flat[:, 0 : 4 * N].rearrange("p (t n) -> p t n", t=4) for flat in (d_raw0, d_last)]
         bias = d_last[:, 4 * N : 4 * N + 4]
-        for a in range(PASSES):
-            rows = wd[512 * a : 512 * (a + 1), :].rearrange("(q t s) n -> t q s n", t=4, s=8)
-            for t in range(4):
-                nc.sync.dma_start(d_raw[a][:, t, :], rows[t])
+        nc.sync.dma_start(d_raw[0], wd[0:PASS, :].rearrange("(p t) n -> p t n", t=4))
+        wd_rows = wd[PASS:R, :].rearrange("(q t s) n -> t q s n", t=4, s=8)
+        for t in range(4):
+            nc.sync.dma_start(d_raw[1][:, t, :], wd_rows[t])
         with nc.allow_non_contiguous_dma(reason="one bias value to a partition"):
             nc.sync.dma_start(bias, b.rearrange("(u p) -> p u", p=P))
 
-        def cast_wg(copy, raw, q0, q1):
-            dst = g_bf[0][:].rearrange("p (t q u v i) -> p u q t i v", t=4, q=16, u=2, v=4, i=4)
-            src = raw.rearrange("p i (q t u v) -> p u q t i v", t=4, u=2, v=4)
-            for u in range(2):
-                copy(dst[:, u, q0:q1], src[:, u])
+        def round_wg0(copy, raw, r0, r1):
+            dst = g_bf[0][:].rearrange("p (h e m i) -> p h m i e", h=2, e=2, i=4)
+            copy(dst[:, :, r0 // 4 : r1 // 4], raw.rearrange("p i (m h e) -> p h m i e", h=2, e=2))
 
-        def pool_round(dst, src):
+        def round_on_gpsimd(dst, src):
             nc.gpsimd.tensor_scalar(dst, src, 1.0, 0.0, ALU.mult, ALU.add)
 
-        def cast_wg_pool(raw):
+        def round_wg1(raw):
             dst = g_bf[1][:].rearrange("p (t q s i) -> p t q s i", t=4, q=16, s=8, i=4)
             src = raw.rearrange("p i (q t s) -> p t q s i", t=4, s=8)
             for t in range(4):
-                pool_round(dst[:, t], src[:, t])
+                round_on_gpsimd(dst[:, t], src[:, t])
 
-        def cast_wd_pool(a, n0, n1):
-            dst = d_bf[a][:, 4 * n0 : 4 * n1].rearrange("p (c t) -> p c t", t=4)
-            pool_round(dst, d_raw[a][:, :, n0:n1].rearrange("p t c -> p c t"))
+        def round_wd_gpsimd(a, n0, n1):
+            dst = d_bf[a][:, 4 * n0 : 4 * n1].rearrange("p (n t) -> p n t", t=4)
+            round_on_gpsimd(dst, d_raw[a][:, :, n0:n1].rearrange("p t n -> p n t"))
 
-        def cast_wd_scalar(a, n0, n1):
-            dst = d_bf[a][:, 4 * n0 : 4 * n1].rearrange("p (c v t) -> p c t v", t=4, v=4)
-            nc.scalar.copy(dst, d_raw[a][:, :, n0:n1].rearrange("p t (c v) -> p c t v", v=4))
+        def round_wd_scalar(a, n0, n1):
+            dst = d_bf[a][:, 4 * n0 : 4 * n1].rearrange("p (w v t) -> p w t v", t=4, v=4)
+            nc.scalar.copy(dst, d_raw[a][:, :, n0:n1].rearrange("p t (w v) -> p w t v", v=4))
 
         def quantize(words, scales, src):
             nc.vector.quantize_mx(out=words.bitcast(FP8X4), scales=scales, in_=src)
+
+        def ub_buffer(a, c):
+            if a == 0 and c < 2:
+                return g_early[:, BANK * c : BANK * (c + 1)]
+            if a == 0 and c < 4:
+                return g_late[:, BANK * (c - 2) : BANK * (c - 1)]
+            if (a, c) in AFTER_WD:
+                place = AFTER_WD.index((a, c))
+                return d_last[:, BANK * place : BANK * (place + 1)]
+            if (a, c) == (1, 7):
+                return d_bf1[:].bitcast(F32)[:, 0:BANK]
+            return tile("ub%d%d" % (a, c), [P, BANK], F32)[:]
 
         def up(a, c):
             cols = slice(CHUNK * c, CHUNK * (c + 1))
             bank = ps_s.tile([P, 4, CHUNK], F32, name="bank_s")
             for t in range(4):
-                m = 4 * a + t
                 nc.tensor.matmul_mx(
                     out=bank[:, t, :],
-                    lhsT=uw[:].bitcast(U8)[:, 256 * m : 256 * (m + 1)].bitcast(FP4X4),
-                    lhsT_scale=us[:].bitcast(U8)[:, 128 * m : 128 * (m + 1)],
+                    lhsT=uw[a][:, 2 * P * t : 2 * P * (t + 1)].bitcast(FP4X4),
+                    lhsT_scale=us[a][:, P * t : P * (t + 1)],
                     rhs=vw[c // 4][:, CHUNK * (c % 4) : CHUNK * (c % 4 + 1)].bitcast(FP8X4),
                     rhs_scale=vs[:, cols],
                     start=True,
                     stop=True,
                 )
-            if a == 0 and c < 2:
-                ub[a, c] = g_early[:, 512 * c : 512 * (c + 1)]
-            elif a == 0 and c < 4:
-                ub[a, c] = g_late[:, 512 * (c - 2) : 512 * (c - 1)]
-            elif (a, c) in LATE:
-                k = LATE.index((a, c))
-                ub[a, c] = d_last[:, 512 * k : 512 * (k + 1)]
-            elif (a, c) == (1, 7):
-                ub[a, c] = d_bf1[:].bitcast(F32)[:, 0:512]
-            else:
-                ub[a, c] = tile("ub%d%d" % (a, c), [P, 4 * CHUNK], F32)[:]
+            ub[a, c] = ub_buffer(a, c)
             nc.scalar.activation(
                 ub[a, c].rearrange("p (j t) -> p j t", t=4),
                 bank[:].rearrange("p t j -> p j t"),
@@ -172,15 +188,15 @@ def tile_list_gmlpt_relu_bias_kernel(tc, tab_words, tab_scales, wg, wu_words, wu
             for t in range(4):
                 nc.tensor.matmul_mx(
                     out=bank[:, t, :],
-                    lhsT=gw[a][:, 128 * t : 128 * (t + 1)].bitcast(FP8X4),
-                    lhsT_scale=gs[a][:, 128 * t : 128 * (t + 1)],
+                    lhsT=gw[a][:, P * t : P * (t + 1)].bitcast(FP8X4),
+                    lhsT_scale=gs[a][:, P * t : P * (t + 1)],
                     rhs=vw[c // 4][:, CHUNK * (c % 4) : CHUNK * (c % 4 + 1)].bitcast(FP8X4),
                     rhs_scale=vs[:, cols],
                     start=True,
                     stop=True,
                 )
             nc.vector.scalar_tensor_tensor(
-                out=h_bf[a][:, 512 * c : 512 * (c + 1)].rearrange("p (j t) -> p j t", t=4),
+                out=h_bf[a][:, BANK * c : BANK * (c + 1)].rearrange("p (j t) -> p j t", t=4),
                 in0=bank[:].rearrange("p t j -> p j t"),
                 scalar=0.0,
                 in1=ub[a, c].rearrange("p (j t) -> p j t", t=4),
@@ -196,34 +212,24 @@ def tile_list_gmlpt_relu_bias_kernel(tc, tab_words, tab_scales, wg, wu_words, wu
             cols = slice(CHUNK * c0, CHUNK * c1)
             nc.tensor.matmul_mx(
                 out=bank,
-                lhsT=dw[a][:, 128 * u : 128 * (u + 1)].bitcast(FP8X4),
-                lhsT_scale=ds[a][:, 128 * u : 128 * (u + 1)],
+                lhsT=dw[a][:, P * u : P * (u + 1)].bitcast(FP8X4),
+                lhsT_scale=ds[a][:, P * u : P * (u + 1)],
                 rhs=hw[a][:, cols].bitcast(FP8X4),
                 rhs_scale=hs[a][:, cols],
                 start=(a == 0),
                 stop=(a == PASSES - 1),
             )
 
-        def down(y, c0, c1, u0, on_vector):
-            width = CHUNK * (c1 - c0)
-            if on_vector:
-                bank = vector_bank([P, 2, width])
-            else:
-                bank = ps_s.tile([P, 2, width], F32, name="bank_s")
+        def add_bias(y, u, sums):
+            nc.scalar.activation(y[:, u, :], sums, ACT.Identity, bias=bias[:, u : u + 1])
+
+        def down_two(y, c0, c1, u0):
+            bank = ps_s.tile([P, 2, CHUNK * (c1 - c0)], F32, name="bank_s")
             for e in range(2):
                 for a in range(PASSES):
                     down_pass(bank[:, e, :], c0, c1, u0 + e, a)
-            if on_vector:
-                nc.vector.tensor_tensor(
-                    y[:, u0 : u0 + 2, :],
-                    bank[:],
-                    bias[:, u0 : u0 + 2].unsqueeze(2).to_broadcast([P, 2, width]),
-                    ALU.add,
-                )
-            else:
-                for e in range(2):
-                    u = u0 + e
-                    nc.scalar.activation(y[:, u, :], bank[:, e, :], ACT.Identity, bias=bias[:, u : u + 1])
+            for e in range(2):
+                add_bias(y, u0 + e, bank[:, e, :])
 
         out_rows = out.rearrange("(u p) j -> p u j", p=P)
 
@@ -231,67 +237,68 @@ def tile_list_gmlpt_relu_bias_kernel(tc, tab_words, tab_scales, wg, wu_words, wu
             nc.sync.dma_start(out_rows[:, u0:u1, CHUNK * c0 : CHUNK * c1], y[:, u0:u1, :])
 
         def output_wide(y, u):
-            bank = ps_s.tile([P, 4 * CHUNK], F32, name="bank_s")
+            bank = ps_s.tile([P, WIDE * CHUNK], F32, name="bank_s")
             for a in range(PASSES):
-                down_pass(bank[:], 0, 4, u, a)
-            nc.scalar.activation(y[:, u, :], bank[:], ACT.Identity, bias=bias[:, u : u + 1])
-            store(y, 0, 4, u, u + 1)
+                down_pass(bank[:], 0, WIDE, u, a)
+            add_bias(y, u, bank[:])
+            store(y, 0, WIDE, u, u + 1)
 
-        def outputs(g, share):
-            y = tile("y%d" % g, [P, 4, PAIR], F32)
-            for u0 in (0, 2):
-                down(y, 2 * g, 2 * g + 2, u0, share and u0 == 2)
-                store(y, 2 * g, 2 * g + 2, u0, u0 + 2)
+        round_wg0(nc.scalar.copy, g_parts[0], 0, WG_FIRST)
+        round_wg0(nc.vector.tensor_copy, g_parts[1], WG_FIRST, PASS)
+        for half in range(2):
+            cols = slice(2 * P * half, 2 * P * (half + 1))
+            quantize(gw[0][:, cols], gs[0][:, cols], g_bf[0][:, 4 * cols.start : 4 * cols.stop])
 
-        cast_wg(nc.scalar.copy, g_parts[0], 0, 8)
-        cast_wg(nc.vector.tensor_copy, g_parts[1], 8, 16)
-        quantize(gw[0][:, 0:256], gs[0][:, 0:256], g_bf[0][:, 0:1024])
-        quantize(gw[0][:, 256:512], gs[0][:, 256:512], g_bf[0][:, 1024:2048])
-        cast_wg_pool(g_parts[2])
-        for c in range(6):
+        round_wg1(g_parts[2])
+        for c in range(AHEAD):
             up(0, c)
             gate(0, c)
+
         quantize(gw[1][:], gs[1][:], g_bf[1][:])
         hw[0] = tile("hw0", [P, J], U32, tag="g_bf1_then_hw0")
-        quantize_h(0, 0, 4)
-        for n0 in (256, 384):
-            cast_wd_pool(0, n0, n0 + 128)
-        cast_wd_scalar(0, 0, 256)
-        for c in range(4):
+        quantize_h(0, 0, WIDE)
+        for n0 in range(WD_SCALAR, N, P):
+            round_wd_gpsimd(0, n0, n0 + P)
+        round_wd_scalar(0, 0, WD_SCALAR)
+        for c in range(WIDE):
             up(1, c)
             gate(1, c)
         up(1, 4)
-        cast_wd_scalar(1, 0, N)
+        round_wd_scalar(1, 0, N)
         quantize(dw[1][:], ds[1][:], d_bf[1])
-        quantize_h(1, 0, 4)
+        quantize_h(1, 0, WIDE)
         quantize(dw[0][:], ds[0][:], d_bf[0])
-        y0 = tile("y0", [P, 4, 4 * CHUNK], F32)
+
+        y_wide = tile("y0", [P, 4, WIDE * CHUNK], F32)
         up(1, 5)
         up(0, 6)
         gate(1, 4)
-        output_wide(y0, 0)
+        output_wide(y_wide, 0)
         up(1, 6)
         gate(1, 5)
-        output_wide(y0, 1)
+        output_wide(y_wide, 1)
         up(0, 7)
-        output_wide(y0, 2)
-        quantize_h(0, 4, 6)
-        quantize_h(1, 4, 6)
+        output_wide(y_wide, 2)
+        for a in range(PASSES):
+            quantize_h(a, 4, 6)
         up(1, 7)
-        output_wide(y0, 3)
-        gate(0, 6)
-        gate(1, 6)
-        outputs(2, False)
-        quantize_h(0, 6, 7)
-        gate(0, 7)
-        quantize_h(1, 6, 7)
-        gate(1, 7)
+        output_wide(y_wide, 3)
+        for a in range(PASSES):
+            gate(a, 6)
+        y_pair = tile("y2", [P, 4, 2 * CHUNK], F32)
+        for u0 in (0, 2):
+            down_two(y_pair, 4, 6, u0)
+            store(y_pair, 4, 6, u0, u0 + 2)
+        for a in range(PASSES):
+            quantize_h(a, 6, 7)
+            gate(a, 7)
         y6 = tile("y6", [P, 4, CHUNK], F32)
-        down(y6, 6, 7, 0, False)
-        down(y6, 6, 7, 2, False)
+        for u0 in (0, 2):
+            down_two(y6, 6, 7, u0)
         store(y6, 6, 7, 0, 4)
-        quantize_h(0, 7, 8)
-        quantize_h(1, 7, 8)
+
+        for a in range(PASSES):
+            quantize_h(a, 7, 8)
         y7 = tile("y7", [P, 4, CHUNK], F32)
         last_banks = [ps_s.tile([P, CHUNK], F32, name="bank_s") for u in range(2)]
         last_banks += [vector_bank([P, CHUNK]) for u in range(2)]
@@ -299,7 +306,7 @@ def tile_list_gmlpt_relu_bias_kernel(tc, tab_words, tab_scales, wg, wu_words, wu
             for u in (0, 2, 1, 3):
                 down_pass(last_banks[u][:], 7, 8, u, a)
         for u in range(2):
-            nc.scalar.activation(y7[:, u, :], last_banks[u][:], ACT.Identity, bias=bias[:, u : u + 1])
+            add_bias(y7, u, last_banks[u][:])
         for u in range(2, 4):
             nc.vector.tensor_scalar_add(y7[:, u, :], last_banks[u][:], bias[:, u : u + 1])
         store(y7, 7, 8, 0, 4)

@@ -16,6 +16,7 @@ FP4X4 = mybir.dt.float4_e2m1fn_x4
 ALU = mybir.AluOpType
 ACT = mybir.ActivationFunctionType
 
+
 P = 128
 PASSES = 2
 PASS = R // PASSES
@@ -25,146 +26,128 @@ BANKS = 4
 SCALE_ROWS = 16
 ROW0 = P - SCALE_ROWS
 WG_FIRST = 256
-WD_SCALAR = 256
-AHEAD = 6
-WIDE = 4
-AFTER_WD = ((1, 5), (0, 6), (1, 6), (0, 7))
 
 
 def tile_list_gmlpt_relu_bias_kernel(tc, tab_words, tab_scales, wg, wu_words, wu_scales, wd, b, offs, out):
     nc = tc.nc
     with ExitStack() as ctx:
         keep = ctx.enter_context(tc.tile_pool(name="keep", bufs=1))
-        ps_s = ctx.enter_context(tc.psum_pool(name="ps_s", bufs=BANKS))
-        ps_v = ctx.enter_context(tc.psum_pool(name="ps_v", bufs=1))
-        v_turn = list(range(BANKS)) * 5
+        ps = ctx.enter_context(tc.psum_pool(name="ps", bufs=1))
+        turn = {"s": list(range(BANKS)) * 7, "v": list(range(BANKS)) * 5}
 
         def tile(name, shape, dtype, tag=None):
             return keep.tile(shape, dtype, name=name, tag=tag or name, align_bytes=64)
 
-        def vector_bank(shape):
-            return ps_v.tile(shape, F32, name="bank_v%d" % v_turn.pop(0))
+        def bank_of(reader, shape):
+            return ps.tile(shape, F32, name="bank_%s%d" % (reader, turn[reader].pop(0)))
 
         offsets = keep.tile([P, J // 16], U16, name="offsets")
-        tw = tile("tw", [P, T], I32, tag="tw_then_d_raw1")
+        tw = tile("tw", [P, T], I32)
         ts = tile("ts", [P, T // 4], I32, tag="ts_then_g_late")
         uw_raw = tile("uw_raw", [P, R // 2], I32)
-        us_raw = tile("us_raw", [P, R // 4], I32, tag="us_raw_then_d_raw0")
-        us_all = tile("us_all", [P, R // 4], I32)
+        us_raw = tile("us_raw", [P, R // 4], I32)
         uw = [tile("uw%d" % a, [P, 2 * PASS], U8) for a in range(PASSES)]
         us = [tile("us%d" % a, [P, PASS], U8) for a in range(PASSES)]
         vw = [tile("vw%d" % half, [P, J // 2], U32) for half in range(2)]
         vs_raw = tile("vs_raw", [P, J], U8)
         vs = tile("vs", [P, J], U8)
-        g_early = tile("g_early", [P, 4 * WG_FIRST], F32)
-        g_bf = [tile("g_bf0", [P, 4 * PASS], BF16), tile("g_bf1", [P, 4 * PASS], BF16, tag="g_bf1_then_hw0")]
+        early = tile("early", [P, 4 * BANK], F32)
+        g_bf0 = tile("g_bf0", [P, 4 * PASS], BF16)
         gw = [tile("gw%d" % a, [P, PASS], U32) for a in range(PASSES)]
         gs = [tile("gs%d" % a, [P, PASS], U8) for a in range(PASSES)]
-        h0_flat = tile("h0_flat", [P, 4 * WD_SCALAR + 4 * J], BF16)
-        d_bf1 = tile("d_bf1", [P, 4 * N], BF16)
-        d_bf = [h0_flat[:, 0 : 4 * N], d_bf1[:]]
         dw = [tile("dw%d" % a, [P, N], U32) for a in range(PASSES)]
         ds = [tile("ds%d" % a, [P, N], U8) for a in range(PASSES)]
-        h_bf = [h0_flat[:, 4 * WD_SCALAR : 4 * WD_SCALAR + 4 * J], tile("h_bf1", [P, 4 * J], BF16)[:]]
-        hw = {1: tile("hw1", [P, J], U32)}
         hs = [tile("hs%d" % a, [P, J], U8) for a in range(PASSES)]
-        ub = {}
+        d_raw = [tile("d_raw%d" % a, [P, 4 * N], F32) for a in range(PASSES)]
+        d_rows = [flat[:].rearrange("p (t n) -> p t n", t=4) for flat in d_raw]
+        bias = tile("bias", [P, 4], F32)
+        ub, h_bf, hw, y = {}, {}, {}, {}
+        groups = ((0, 4), (4, 6), (6, 8))
+        for a in range(PASSES):
+            for c0, c1 in groups:
+                h_bf[a, c0] = tile("h_bf%d%d" % (a, c0), [P, BANK * (c1 - c0)], BF16)
 
+        def group_of(c):
+            return [g for g in groups if g[0] <= c < g[1]][0]
+
+        nc.gpsimd.memset(us_raw[:], 0)
         nc.vector.memset(ts[0:ROW0, :], 0)
-        nc.gpsimd.memset(us_all[:], 0)
         nc.gpsimd.memset(vs[:].bitcast(I32), 0)
 
         us_rows = wu_scales[0].bitcast(I32)
         wg_rows = wg.rearrange("(p i) r -> p i r", i=4)
         nc.sync.dma_start(offsets[:], offs)
+        for e in range(4):
+            nc.scalar.dma_start(us_raw[e:P:32, :], us_rows[e:SCALE_ROWS:4, :])
         nc.sync.dma_start(ts[ROW0:P, :], tab_scales[0].bitcast(I32))
         nc.sync.dma_start(uw_raw[:], wu_words[0].bitcast(I32))
-        for e in range(4):
-            nc.sync.dma_start(us_raw[e:P:32, :], us_rows[e:SCALE_ROWS:4, :])
         nc.sync.dma_start(tw[:], tab_words[0].rearrange("p t i -> p (t i)").bitcast(I32))
-        g_parts = [g_early[:].rearrange("p (i r) -> p i r", i=4)]
+        g_parts = [early[:].rearrange("p (i x) -> p i x", i=4)[:, :, 0:WG_FIRST]]
         nc.sync.dma_start(g_parts[0], wg_rows[:, :, 0:WG_FIRST])
 
         nc.vector.tensor_copy(vs_raw[:], ts[:].bitcast(U8).indirect(offsets[:]))
         for e in range(4):
-            nc.sync.dma_start(vs[e:P:32, :].bitcast(I32), vs_raw[ROW0 + e : P : 4, :].bitcast(I32))
+            nc.scalar.dma_start(vs[e:P:32, :].bitcast(I32), vs_raw[ROW0 + e : P : 4, :].bitcast(I32))
         g_late = tile("g_late", [P, 4 * (R - WG_FIRST)], F32, tag="ts_then_g_late")
         for r0, r1 in ((WG_FIRST, PASS), (PASS, R)):
             g_parts.append(g_late[:, 4 * (r0 - WG_FIRST) : 4 * (r1 - WG_FIRST)].rearrange("p (i r) -> p i r", i=4))
             nc.sync.dma_start(g_parts[-1], wg_rows[:, :, r0:r1])
+        nc.sync.dma_start(d_rows[0], wd[0:PASS, :].rearrange("(p t) n -> p t n", t=4))
+        wd_rows = wd[PASS:R, :].rearrange("(q t s) n -> t q s n", t=4, s=8)
+        for t in range(4):
+            nc.sync.dma_start(d_rows[1][:, t, :], wd_rows[t])
+        with nc.allow_non_contiguous_dma(reason="one bias value to a partition"):
+            nc.sync.dma_start(bias[:], b.rearrange("(u p) -> p u", p=P))
 
         nc.vector.tensor_copy(
             uw[0][:].rearrange("p (t m b) -> p t m b", t=4, b=2),
             uw_raw[:, 0 : PASS // 2].bitcast(U8).rearrange("p (m t b) -> p t m b", t=4, b=2),
         )
         nc.vector.tensor_copy(
+            us[0][:].rearrange("p (t m) -> p t m", t=4),
+            us_raw[:, 0 : PASS // 4].bitcast(U8).rearrange("p (m t) -> p t m", t=4),
+        )
+        nc.vector.tensor_copy(
             uw[1][:].bitcast(I32).rearrange("p (t q w) -> p t q w", t=4, w=4),
             uw_raw[:, PASS // 2 : PASS].rearrange("p (q t w) -> p t q w", t=4, w=4),
         )
-        for quadrant in range(4):
-            live = slice(32 * quadrant, 32 * quadrant + 4)
-            nc.vector.tensor_copy(us_all[live, :], us_raw[live, :])
-        nc.vector.tensor_copy(
-            us[0][:].rearrange("p (t m) -> p t m", t=4),
-            us_all[:, 0 : PASS // 4].bitcast(U8).rearrange("p (m t) -> p t m", t=4),
-        )
         nc.vector.tensor_copy(
             us[1][:].bitcast(I32).rearrange("p (t q w) -> p t q w", t=4, w=2),
-            us_all[:, PASS // 4 : PASS // 2].rearrange("p (q t w) -> p t q w", t=4, w=2),
+            us_raw[:, PASS // 4 : PASS // 2].rearrange("p (q t w) -> p t q w", t=4, w=2),
         )
         for half in range(2):
             nc.vector.tensor_copy(vw[half][:], tw[:].bitcast(U32).indirect(offsets[:, 32 * half : 32 * (half + 1)]))
 
-        d_raw0 = tile("d_raw0", [P, 4 * N], F32, tag="us_raw_then_d_raw0")
-        d_last = tile("d_last", [P, 4 * N + 16], F32, tag="tw_then_d_raw1")
-        d_raw = [flat[:, 0 : 4 * N].rearrange("p (t n) -> p t n", t=4) for flat in (d_raw0, d_last)]
-        bias = d_last[:, 4 * N : 4 * N + 4]
-        nc.sync.dma_start(d_raw[0], wd[0:PASS, :].rearrange("(p t) n -> p t n", t=4))
-        wd_rows = wd[PASS:R, :].rearrange("(q t s) n -> t q s n", t=4, s=8)
-        for t in range(4):
-            nc.sync.dma_start(d_raw[1][:, t, :], wd_rows[t])
-        with nc.allow_non_contiguous_dma(reason="one bias value to a partition"):
-            nc.sync.dma_start(bias, b.rearrange("(u p) -> p u", p=P))
-
         def round_wg0(copy, raw, r0, r1):
-            dst = g_bf[0][:].rearrange("p (h e m i) -> p h m i e", h=2, e=2, i=4)
+            dst = g_bf0[:].rearrange("p (h e m i) -> p h m i e", h=2, e=2, i=4)
             copy(dst[:, :, r0 // 4 : r1 // 4], raw.rearrange("p i (m h e) -> p h m i e", h=2, e=2))
 
         def round_on_gpsimd(dst, src):
             nc.gpsimd.tensor_scalar(dst, src, 1.0, 0.0, ALU.mult, ALU.add)
 
-        def round_wg1(raw):
-            dst = g_bf[1][:].rearrange("p (t q s i) -> p t q s i", t=4, q=16, s=8, i=4)
-            src = raw.rearrange("p i (q t s) -> p t q s i", t=4, s=8)
-            for t in range(4):
-                round_on_gpsimd(dst[:, t], src[:, t])
+        def round_wg1_gpsimd(dst, t):
+            src = g_parts[2].rearrange("p i (q t s) -> p t q s i", t=4, s=8)
+            round_on_gpsimd(dst.rearrange("p (q s i) -> p q s i", s=8, i=4), src[:, t])
 
-        def round_wd_gpsimd(a, n0, n1):
-            dst = d_bf[a][:, 4 * n0 : 4 * n1].rearrange("p (n t) -> p n t", t=4)
-            round_on_gpsimd(dst, d_raw[a][:, :, n0:n1].rearrange("p t n -> p n t"))
+        def round_wg1_scalar(dst, t):
+            src = g_parts[2].rearrange("p i (q t w v) -> p t q w i v", t=4, w=2, v=4)
+            nc.scalar.copy(dst.rearrange("p (q w v i) -> p q w i v", w=2, v=4, i=4), src[:, t])
 
-        def round_wd_scalar(a, n0, n1):
-            dst = d_bf[a][:, 4 * n0 : 4 * n1].rearrange("p (w v t) -> p w t v", t=4, v=4)
-            nc.scalar.copy(dst, d_raw[a][:, :, n0:n1].rearrange("p t (w v) -> p w t v", v=4))
+        def round_wd_gpsimd(dst, a, n0, n1):
+            round_on_gpsimd(dst.rearrange("p (n t) -> p n t", t=4), d_rows[a][:, :, n0:n1].rearrange("p t n -> p n t"))
+
+        def round_wd(copy, dst, a, n0, n1):
+            copy(dst.rearrange("p (w v t) -> p w t v", t=4, v=4), d_rows[a][:, :, n0:n1].rearrange("p t (w v) -> p w t v", v=4))
 
         def quantize(words, scales, src):
             nc.vector.quantize_mx(out=words.bitcast(FP8X4), scales=scales, in_=src)
 
-        def ub_buffer(a, c):
-            if a == 0 and c < 2:
-                return g_early[:, BANK * c : BANK * (c + 1)]
-            if a == 0 and c < 4:
-                return g_late[:, BANK * (c - 2) : BANK * (c - 1)]
-            if (a, c) in AFTER_WD:
-                place = AFTER_WD.index((a, c))
-                return d_last[:, BANK * place : BANK * (place + 1)]
-            if (a, c) == (1, 7):
-                return d_bf1[:].bitcast(F32)[:, 0:BANK]
-            return tile("ub%d%d" % (a, c), [P, BANK], F32)[:]
+        def halves(flat):
+            return flat.rearrange("p (h j t) -> p h j t", h=2, t=4)
 
-        def up(a, c):
+        def up(a, c, place=None, tag=None):
             cols = slice(CHUNK * c, CHUNK * (c + 1))
-            bank = ps_s.tile([P, 4, CHUNK], F32, name="bank_s")
+            bank = bank_of("s", [P, 4, CHUNK])
             for t in range(4):
                 nc.tensor.matmul_mx(
                     out=bank[:, t, :],
@@ -175,16 +158,14 @@ def tile_list_gmlpt_relu_bias_kernel(tc, tab_words, tab_scales, wg, wu_words, wu
                     start=True,
                     stop=True,
                 )
-            ub[a, c] = ub_buffer(a, c)
-            nc.scalar.activation(
-                ub[a, c].rearrange("p (j t) -> p j t", t=4),
-                bank[:].rearrange("p t j -> p j t"),
-                ACT.Copy,
-            )
+            if place is None:
+                place = halves(tile("ub%d%d" % (a, c), [P, BANK], F32, tag=tag)[:])
+            ub[a, c] = place
+            nc.scalar.activation(place, bank[:].rearrange("p t (h j) -> p h j t", h=2), ACT.Copy)
 
         def gate(a, c):
             cols = slice(CHUNK * c, CHUNK * (c + 1))
-            bank = vector_bank([P, 4, CHUNK])
+            bank = bank_of("v", [P, 4, CHUNK])
             for t in range(4):
                 nc.tensor.matmul_mx(
                     out=bank[:, t, :],
@@ -195,118 +176,117 @@ def tile_list_gmlpt_relu_bias_kernel(tc, tab_words, tab_scales, wg, wu_words, wu
                     start=True,
                     stop=True,
                 )
+            c0 = group_of(c)[0]
             nc.vector.scalar_tensor_tensor(
-                out=h_bf[a][:, BANK * c : BANK * (c + 1)].rearrange("p (j t) -> p j t", t=4),
-                in0=bank[:].rearrange("p t j -> p j t"),
+                out=h_bf[a, c0][:, BANK * (c - c0) : BANK * (c - c0 + 1)].rearrange("p (h j t) -> p h j t", h=2, t=4),
+                in0=bank[:].rearrange("p t (h j) -> p h j t", h=2),
                 scalar=0.0,
-                in1=ub[a, c].rearrange("p (j t) -> p j t", t=4),
+                in1=ub[a, c],
                 op0=ALU.max,
                 op1=ALU.mult,
             )
 
-        def quantize_h(a, c0, c1):
-            cols = slice(CHUNK * c0, CHUNK * c1)
-            quantize(hw[a][:, cols], hs[a][:, cols], h_bf[a][:, 4 * cols.start : 4 * cols.stop])
+        def quantize_h(a, c0, c1, tag=None):
+            hw[a, c0] = tile("hw%d%d" % (a, c0), [P, CHUNK * (c1 - c0)], U32, tag=tag)
+            g0 = group_of(c0)[0]
+            quantize(hw[a, c0][:], hs[a][:, CHUNK * c0 : CHUNK * c1], h_bf[a, g0][:, BANK * (c0 - g0) : BANK * (c1 - g0)])
+
+        def quantize_wd(a, n0, n1, src):
+            quantize(dw[a][:, n0:n1], ds[a][:, n0:n1], src)
 
         def down_pass(bank, c0, c1, u, a):
-            cols = slice(CHUNK * c0, CHUNK * c1)
             nc.tensor.matmul_mx(
                 out=bank,
                 lhsT=dw[a][:, P * u : P * (u + 1)].bitcast(FP8X4),
                 lhsT_scale=ds[a][:, P * u : P * (u + 1)],
-                rhs=hw[a][:, cols].bitcast(FP8X4),
-                rhs_scale=hs[a][:, cols],
+                rhs=hw[a, c0][:].bitcast(FP8X4),
+                rhs_scale=hs[a][:, CHUNK * c0 : CHUNK * c1],
                 start=(a == 0),
                 stop=(a == PASSES - 1),
             )
 
-        def add_bias(y, u, sums):
-            nc.scalar.activation(y[:, u, :], sums, ACT.Identity, bias=bias[:, u : u + 1])
-
-        def down_two(y, c0, c1, u0):
-            bank = ps_s.tile([P, 2, CHUNK * (c1 - c0)], F32, name="bank_s")
-            for e in range(2):
-                for a in range(PASSES):
-                    down_pass(bank[:, e, :], c0, c1, u0 + e, a)
-            for e in range(2):
-                add_bias(y, u0 + e, bank[:, e, :])
+        def add_bias(reader, c0, c1, u, sums):
+            if c0 not in y:
+                y[c0] = tile("y%d" % c0, [P, 4, CHUNK * (c1 - c0)], F32)
+            if reader == "s":
+                nc.scalar.activation(y[c0][:, u, :], sums, ACT.Identity, bias=bias[:, u : u + 1])
+            else:
+                nc.vector.tensor_scalar_add(y[c0][:, u, :], sums, bias[:, u : u + 1])
 
         out_rows = out.rearrange("(u p) j -> p u j", p=P)
 
-        def store(y, c0, c1, u0, u1):
-            nc.sync.dma_start(out_rows[:, u0:u1, CHUNK * c0 : CHUNK * c1], y[:, u0:u1, :])
+        def store(c0, c1, u0, u1):
+            nc.sync.dma_start(out_rows[:, u0:u1, CHUNK * c0 : CHUNK * c1], y[c0][:, u0:u1, :])
 
-        def output_wide(y, u):
-            bank = ps_s.tile([P, WIDE * CHUNK], F32, name="bank_s")
+        def output(reader, c0, c1, u0, u1):
+            bank = bank_of(reader, [P, u1 - u0, CHUNK * (c1 - c0)])
+            for u in range(u0, u1):
+                for a in range(PASSES):
+                    down_pass(bank[:, u - u0, :], c0, c1, u, a)
+            for u in range(u0, u1):
+                add_bias(reader, c0, c1, u, bank[:, u - u0, :])
+            store(c0, c1, u0, u1)
+
+        def last(c0, c1, readers, stores):
+            banks = [bank_of(reader, [P, CHUNK * (c1 - c0)]) for reader in readers]
             for a in range(PASSES):
-                down_pass(bank[:], 0, WIDE, u, a)
-            add_bias(y, u, bank[:])
-            store(y, 0, WIDE, u, u + 1)
+                for u in range(4):
+                    down_pass(banks[u][:], c0, c1, u, a)
+            for u in range(4):
+                add_bias(readers[u], c0, c1, u, banks[u][:])
+            for u0, u1 in stores:
+                store(c0, c1, u0, u1)
+
 
         round_wg0(nc.scalar.copy, g_parts[0], 0, WG_FIRST)
         round_wg0(nc.vector.tensor_copy, g_parts[1], WG_FIRST, PASS)
         for half in range(2):
             cols = slice(2 * P * half, 2 * P * (half + 1))
-            quantize(gw[0][:, cols], gs[0][:, cols], g_bf[0][:, 4 * cols.start : 4 * cols.stop])
-
-        round_wg1(g_parts[2])
-        for c in range(AHEAD):
-            up(0, c)
+            quantize(gw[0][:, cols], gs[0][:, cols], g_bf0[:, 4 * cols.start : 4 * cols.stop])
+        g_bf1 = [tile("g_bf1a", [P, 2 * PASS], BF16), None]
+        for t in range(2):
+            round_wg1_gpsimd(g_bf1[0][:, BANK * t : BANK * (t + 1)], t)
+        for c in range(4):
+            up(0, c, halves(early[:, BANK * c : BANK * (c + 1)]))
             gate(0, c)
-
-        quantize(gw[1][:], gs[1][:], g_bf[1][:])
-        hw[0] = tile("hw0", [P, J], U32, tag="g_bf1_then_hw0")
-        quantize_h(0, 0, WIDE)
-        for n0 in range(WD_SCALAR, N, P):
-            round_wd_gpsimd(0, n0, n0 + P)
-        round_wd_scalar(0, 0, WD_SCALAR)
-        for c in range(WIDE):
+        up(0, 4)
+        gate(0, 4)
+        up(0, 5)
+        g_bf1[1] = early[:, 0:BANK].bitcast(BF16)
+        for t in range(2):
+            round_wg1_scalar(g_bf1[1][:, BANK * t : BANK * (t + 1)], 2 + t)
+        quantize(gw[1][:, 0 : 2 * P], gs[1][:, 0 : 2 * P], g_bf1[0][:])
+        quantize(gw[1][:, 2 * P : 4 * P], gs[1][:, 2 * P : 4 * P], g_bf1[1])
+        quantize_h(0, 0, 4, tag="g_bf1a")
+        d_bf0 = tile("d_bf0", [P, 4 * N], BF16, tag="h_bf00")
+        for n0 in (0, N // 2):
+            round_wd_gpsimd(d_bf0[:, 4 * n0 : 4 * n0 + 2 * N], 0, n0, n0 + N // 2)
+        gate(0, 5)
+        for c in range(6):
             up(1, c)
             gate(1, c)
-        up(1, 4)
-        round_wd_scalar(1, 0, N)
-        quantize(dw[1][:], ds[1][:], d_bf[1])
-        quantize_h(1, 0, WIDE)
-        quantize(dw[0][:], ds[0][:], d_bf[0])
-
-        y_wide = tile("y0", [P, 4, WIDE * CHUNK], F32)
-        up(1, 5)
         up(0, 6)
-        gate(1, 4)
-        output_wide(y_wide, 0)
         up(1, 6)
-        gate(1, 5)
-        output_wide(y_wide, 1)
-        up(0, 7)
-        output_wide(y_wide, 2)
+        d_bf1 = [tile("d_bf1a", [P, 2 * N], BF16, tag="ub11"), tile("d_bf1b", [P, N], BF16, tag="ub12"), tile("d_bf1c", [P, N], BF16, tag="d_raw0")]
+        round_wd(nc.scalar.copy, d_bf1[0][:], 1, 0, 2 * P)
+        round_wd(nc.scalar.copy, d_bf1[1][:], 1, 2 * P, 3 * P)
         for a in range(PASSES):
-            quantize_h(a, 4, 6)
-        up(1, 7)
-        output_wide(y_wide, 3)
-        for a in range(PASSES):
-            gate(a, 6)
-        y_pair = tile("y2", [P, 4, 2 * CHUNK], F32)
+            up(a, 7, d_rows[1][:, 2 * a : 2 * a + 2, 0 : 2 * P].rearrange("p h (j t) -> p h j t", t=4))
+        quantize_wd(0, 0, N, d_bf0[:])
+        quantize_wd(1, 0, 2 * P, d_bf1[0][:])
+        quantize_h(1, 0, 4, tag="h_bf00")
+        round_wd(nc.vector.tensor_copy, d_bf1[2][:], 1, 3 * P, N)
+        quantize_wd(1, 2 * P, 3 * P, d_bf1[1][:])
+        quantize_h(0, 4, 6, tag="ub11")
+        quantize_wd(1, 3 * P, N, d_bf1[2][:])
+        quantize_h(1, 4, 6, tag="ub12")
+        for c in (6, 7):
+            for a in range(PASSES):
+                gate(a, c)
+        for u in range(4):
+            output("s", 0, 4, u, u + 1)
         for u0 in (0, 2):
-            down_two(y_pair, 4, 6, u0)
-            store(y_pair, 4, 6, u0, u0 + 2)
+            output("s", 4, 6, u0, u0 + 2)
         for a in range(PASSES):
-            quantize_h(a, 6, 7)
-            gate(a, 7)
-        y6 = tile("y6", [P, 4, CHUNK], F32)
-        for u0 in (0, 2):
-            down_two(y6, 6, 7, u0)
-        store(y6, 6, 7, 0, 4)
-
-        for a in range(PASSES):
-            quantize_h(a, 7, 8)
-        y7 = tile("y7", [P, 4, CHUNK], F32)
-        last_banks = [ps_s.tile([P, CHUNK], F32, name="bank_s") for u in range(2)]
-        last_banks += [vector_bank([P, CHUNK]) for u in range(2)]
-        for a in range(PASSES):
-            for u in (0, 2, 1, 3):
-                down_pass(last_banks[u][:], 7, 8, u, a)
-        for u in range(2):
-            add_bias(y7, u, last_banks[u][:])
-        for u in range(2, 4):
-            nc.vector.tensor_scalar_add(y7[:, u, :], last_banks[u][:], bias[:, u : u + 1])
-        store(y7, 7, 8, 0, 4)
+            quantize_h(a, 6, 8)
+        last(6, 8, "svsv", ((0, 2), (2, 4)))

@@ -77,17 +77,17 @@ def tile_list_gmlpt_relu_bias_kernel(tc, tab_words, tab_scales, wg, wu_words, wu
         us_rows = wu_scales[0].bitcast(I32)
         wg_rows = wg.rearrange("(p i) r -> p i r", i=4)
         nc.sync.dma_start(offsets[:], offs)
-        for e in range(4):
-            nc.scalar.dma_start(us_raw[e:P:32, :], us_rows[e:SCALE_ROWS:4, :])
         nc.sync.dma_start(ts[ROW0:P, :], tab_scales[0].bitcast(I32))
         nc.sync.dma_start(uw_raw[:], wu_words[0].bitcast(I32))
+        for e in range(4):
+            nc.sync.dma_start(us_raw[e:P:32, :], us_rows[e:SCALE_ROWS:4, :])
         nc.sync.dma_start(tw[:], tab_words[0].rearrange("p t i -> p (t i)").bitcast(I32))
         g_parts = [early[:].rearrange("p (i x) -> p i x", i=4)[:, :, 0:WG_FIRST]]
         nc.sync.dma_start(g_parts[0], wg_rows[:, :, 0:WG_FIRST])
 
         nc.vector.tensor_copy(vs_raw[:], ts[:].bitcast(U8).indirect(offsets[:]))
         for e in range(4):
-            nc.scalar.dma_start(vs[e:P:32, :].bitcast(I32), vs_raw[ROW0 + e : P : 4, :].bitcast(I32))
+            nc.sync.dma_start(vs[e:P:32, :].bitcast(I32), vs_raw[ROW0 + e : P : 4, :].bitcast(I32))
         g_late = tile("g_late", [P, 4 * (R - WG_FIRST)], F32, tag="ts_then_g_late")
         for r0, r1 in ((WG_FIRST, PASS), (PASS, R)):
             g_parts.append(g_late[:, 4 * (r0 - WG_FIRST) : 4 * (r1 - WG_FIRST)].rearrange("p (i r) -> p i r", i=4))

@@ -46,7 +46,7 @@ def tile_list_gmlpt_relu_bias_kernel(tc, tab_words, tab_scales, wg, wu_words, wu
         ts = tile("ts", [P, T // 4], I32, tag="ts_then_g_late")
         uw_raw = tile("uw_raw", [P, R // 2], I32)
         us_raw = tile("us_raw", [P, R // 4], I32)
-        uw = [tile("uw%d" % a, [P, 2 * PASS], U8) for a in range(PASSES)]
+        uw = [tile("uw0", [P, 2 * PASS], U8)]
         us = [tile("us%d" % a, [P, PASS], U8) for a in range(PASSES)]
         vw = [tile("vw%d" % half, [P, J // 2], U32) for half in range(2)]
         vs_raw = tile("vs_raw", [P, J], U8)
@@ -108,10 +108,6 @@ def tile_list_gmlpt_relu_bias_kernel(tc, tab_words, tab_scales, wg, wu_words, wu
             us_raw[:, 0 : PASS // 4].bitcast(U8).rearrange("p (m t) -> p t m", t=4),
         )
         nc.vector.tensor_copy(
-            uw[1][:].bitcast(I32).rearrange("p (t q w) -> p t q w", t=4, w=4),
-            uw_raw[:, PASS // 2 : PASS].rearrange("p (q t w) -> p t q w", t=4, w=4),
-        )
-        nc.vector.tensor_copy(
             us[1][:].bitcast(I32).rearrange("p (t q w) -> p t q w", t=4, w=2),
             us_raw[:, PASS // 4 : PASS // 2].rearrange("p (q t w) -> p t q w", t=4, w=2),
         )
@@ -125,13 +121,15 @@ def tile_list_gmlpt_relu_bias_kernel(tc, tab_words, tab_scales, wg, wu_words, wu
         def round_on_gpsimd(dst, src):
             nc.gpsimd.tensor_scalar(dst, src, 1.0, 0.0, ALU.mult, ALU.add)
 
-        def round_wg1_gpsimd(dst, t):
+        def round_wg1_gpsimd(t, q0, q1):
             src = g_parts[2].rearrange("p i (q t s) -> p t q s i", t=4, s=8)
-            round_on_gpsimd(dst.rearrange("p (q s i) -> p q s i", s=8, i=4), src[:, t])
+            dst = g_bf1[:].rearrange("p (t q s i) -> p t q s i", t=4, s=8, i=4)
+            round_on_gpsimd(dst[:, t, q0:q1], src[:, t, q0:q1])
 
-        def round_wg1_scalar(dst, t):
+        def round_wg1_scalar(t, q0, q1):
             src = g_parts[2].rearrange("p i (q t w v) -> p t q w i v", t=4, w=2, v=4)
-            nc.scalar.copy(dst.rearrange("p (q w v i) -> p q w i v", w=2, v=4, i=4), src[:, t])
+            dst = g_bf1[:].rearrange("p (t q w v i) -> p t q w i v", t=4, w=2, v=4, i=4)
+            nc.scalar.copy(dst[:, t, q0:q1], src[:, t, q0:q1])
 
         def round_wd_gpsimd(dst, a, n0, n1):
             round_on_gpsimd(dst.rearrange("p (n t) -> p n t", t=4), d_rows[a][:, :, n0:n1].rearrange("p t n -> p n t"))
@@ -187,9 +185,10 @@ def tile_list_gmlpt_relu_bias_kernel(tc, tab_words, tab_scales, wg, wu_words, wu
             )
 
         def quantize_h(a, c0, c1, tag=None):
-            hw[a, c0] = tile("hw%d%d" % (a, c0), [P, CHUNK * (c1 - c0)], U32, tag=tag)
-            g0 = group_of(c0)[0]
-            quantize(hw[a, c0][:], hs[a][:, CHUNK * c0 : CHUNK * c1], h_bf[a, g0][:, BANK * (c0 - g0) : BANK * (c1 - g0)])
+            g0, g1 = group_of(c0)
+            if c0 == g0:
+                hw[a, g0] = tile("hw%d%d" % (a, g0), [P, CHUNK * (g1 - g0)], U32, tag=tag)
+            quantize(hw[a, g0][:, CHUNK * (c0 - g0) : CHUNK * (c1 - g0)], hs[a][:, CHUNK * c0 : CHUNK * c1], h_bf[a, g0][:, BANK * (c0 - g0) : BANK * (c1 - g0)])
 
         def quantize_wd(a, n0, n1, src):
             quantize(dw[a][:, n0:n1], ds[a][:, n0:n1], src)
@@ -243,50 +242,54 @@ def tile_list_gmlpt_relu_bias_kernel(tc, tab_words, tab_scales, wg, wu_words, wu
         for half in range(2):
             cols = slice(2 * P * half, 2 * P * (half + 1))
             quantize(gw[0][:, cols], gs[0][:, cols], g_bf0[:, 4 * cols.start : 4 * cols.stop])
-        g_bf1 = [tile("g_bf1a", [P, 2 * PASS], BF16), None]
-        for t in range(2):
-            round_wg1_gpsimd(g_bf1[0][:, BANK * t : BANK * (t + 1)], t)
+        uw.append(tile("uw1", [P, 2 * PASS], U8, tag="g_bf0"))
+        nc.vector.tensor_copy(
+            uw[1][:].bitcast(I32).rearrange("p (t q w) -> p t q w", t=4, w=4),
+            uw_raw[:, PASS // 2 : PASS].rearrange("p (q t w) -> p t q w", t=4, w=4),
+        )
+        g_bf1 = tile("g_bf1", [P, 4 * PASS], BF16)
+        for t, q1 in ((0, 16), (1, 16), (2, 8)):
+            round_wg1_gpsimd(t, 0, q1)
         for c in range(4):
             up(0, c, halves(early[:, BANK * c : BANK * (c + 1)]))
             gate(0, c)
         up(0, 4)
         gate(0, 4)
-        up(0, 5)
-        g_bf1[1] = early[:, 0:BANK].bitcast(BF16)
-        for t in range(2):
-            round_wg1_scalar(g_bf1[1][:, BANK * t : BANK * (t + 1)], 2 + t)
-        quantize(gw[1][:, 0 : 2 * P], gs[1][:, 0 : 2 * P], g_bf1[0][:])
-        quantize(gw[1][:, 2 * P : 4 * P], gs[1][:, 2 * P : 4 * P], g_bf1[1])
-        quantize_h(0, 0, 4, tag="g_bf1a")
-        d_bf0 = tile("d_bf0", [P, 4 * N], BF16, tag="h_bf00")
+        for t, q0 in ((3, 0), (2, 8)):
+            round_wg1_scalar(t, q0, 16)
+        for a, c in ((1, 0), (1, 1), (0, 5), (0, 6)):
+            up(a, c)
+        quantize(gw[1][:], gs[1][:], g_bf1[:])
+        d_bf0 = tile("d_bf0", [P, 4 * N], BF16, tag="g_bf1")
         for n0 in (0, N // 2):
             round_wd_gpsimd(d_bf0[:, 4 * n0 : 4 * n0 + 2 * N], 0, n0, n0 + N // 2)
-        gate(0, 5)
-        for c in range(6):
+        for a, c in ((0, 5), (0, 6), (1, 0), (1, 1)):
+            gate(a, c)
+        for c in range(2, 6):
             up(1, c)
-            gate(1, c)
-        up(0, 6)
-        up(1, 6)
-        d_bf1 = [tile("d_bf1a", [P, 2 * N], BF16, tag="ub11"), tile("d_bf1b", [P, N], BF16, tag="ub12"), tile("d_bf1c", [P, N], BF16, tag="d_raw0")]
-        round_wd(nc.scalar.copy, d_bf1[0][:], 1, 0, 2 * P)
-        round_wd(nc.scalar.copy, d_bf1[1][:], 1, 2 * P, 3 * P)
-        for a in range(PASSES):
-            up(a, 7, d_rows[1][:, 2 * a : 2 * a + 2, 0 : 2 * P].rearrange("p h (j t) -> p h j t", t=4))
+            if c < 5:
+                gate(1, c)
+        d_bf1 = [tile("d_bf1a", [P, 2 * N], BF16, tag="ub10"), tile("d_bf1b", [P, 2 * N], BF16, tag="ub11")]
+        for half in range(2):
+            round_wd(nc.scalar.copy, d_bf1[half][:], 1, 2 * P * half, 2 * P * (half + 1))
+        for a, c, t in ((0, 7, 0), (1, 6, 1), (1, 7, 2)):
+            up(a, c, halves(d_rows[1][:, t, :]))
+        quantize_h(0, 0, 4, tag="d_raw0")
         quantize_wd(0, 0, N, d_bf0[:])
-        quantize_wd(1, 0, 2 * P, d_bf1[0][:])
         quantize_h(1, 0, 4, tag="h_bf00")
-        round_wd(nc.vector.tensor_copy, d_bf1[2][:], 1, 3 * P, N)
-        quantize_wd(1, 2 * P, 3 * P, d_bf1[1][:])
-        quantize_h(0, 4, 6, tag="ub11")
-        quantize_wd(1, 3 * P, N, d_bf1[2][:])
-        quantize_h(1, 4, 6, tag="ub12")
-        for c in (6, 7):
-            for a in range(PASSES):
-                gate(a, c)
+        quantize_wd(1, 0, 2 * P, d_bf1[0][:])
+        gate(1, 5)
+        quantize_h(0, 4, 6, tag="g_bf1")
+        quantize_wd(1, 2 * P, N, d_bf1[1][:])
+        quantize_h(1, 4, 6, tag="ub13")
+        gate(0, 7)
+        gate(1, 6)
+        quantize_h(0, 6, 8)
+        gate(1, 7)
         for u in range(4):
             output("s", 0, 4, u, u + 1)
         for u0 in (0, 2):
             output("s", 4, 6, u0, u0 + 2)
-        for a in range(PASSES):
-            quantize_h(a, 6, 8)
+        quantize_h(1, 6, 7, tag="h_bf06")
+        quantize_h(1, 7, 8)
         last(6, 8, "svsv", ((0, 2), (2, 4)))

@@ -33,7 +33,7 @@ def tile_list_gmlpt_relu_bias_kernel(tc, tab_words, tab_scales, wg, wu_words, wu
     with ExitStack() as ctx:
         keep = ctx.enter_context(tc.tile_pool(name="keep", bufs=1))
         ps = ctx.enter_context(tc.psum_pool(name="ps", bufs=1))
-        turn = {"s": list(range(BANKS)) * 7, "v": list(range(BANKS)) * 5}
+        turn = {"s": [0, 1, 2, 3, 0] + [3, 0, 1, 2] * 6, "v": list(range(BANKS)) * 5}
 
         def tile(name, shape, dtype, tag=None):
             return keep.tile(shape, dtype, name=name, tag=tag or name, align_bytes=64)
@@ -140,26 +140,37 @@ def tile_list_gmlpt_relu_bias_kernel(tc, tab_words, tab_scales, wg, wu_words, wu
         def quantize(words, scales, src):
             nc.vector.quantize_mx(out=words.bitcast(FP8X4), scales=scales, in_=src)
 
-        def halves(flat):
-            return flat.rearrange("p (h j t) -> p h j t", h=2, t=4)
+        def up_product(dst, a, t, c0, c1):
+            nc.tensor.matmul_mx(
+                out=dst,
+                lhsT=uw[a][:, 2 * P * t : 2 * P * (t + 1)].bitcast(FP4X4),
+                lhsT_scale=us[a][:, P * t : P * (t + 1)],
+                rhs=vw[c0 // 4][:, CHUNK * (c0 % 4) : CHUNK * (c0 % 4 + c1 - c0)].bitcast(FP8X4),
+                rhs_scale=vs[:, CHUNK * c0 : CHUNK * c1],
+                start=True,
+                stop=True,
+            )
 
-        def up(a, c, place=None, tag=None):
-            cols = slice(CHUNK * c, CHUNK * (c + 1))
+        def up_one(a, c, place=None):
             bank = bank_of("s", [P, 4, CHUNK])
             for t in range(4):
-                nc.tensor.matmul_mx(
-                    out=bank[:, t, :],
-                    lhsT=uw[a][:, 2 * P * t : 2 * P * (t + 1)].bitcast(FP4X4),
-                    lhsT_scale=us[a][:, P * t : P * (t + 1)],
-                    rhs=vw[c // 4][:, CHUNK * (c % 4) : CHUNK * (c % 4 + 1)].bitcast(FP8X4),
-                    rhs_scale=vs[:, cols],
-                    start=True,
-                    stop=True,
-                )
+                up_product(bank[:, t, :], a, t, c, c + 1)
             if place is None:
-                place = halves(tile("ub%d%d" % (a, c), [P, BANK], F32, tag=tag)[:])
-            ub[a, c] = place
-            nc.scalar.activation(place, bank[:].rearrange("p t (h j) -> p h j t", h=2), ACT.Copy)
+                place = tile("ub%d%d" % (a, c), [P, BANK], F32)[:]
+            ub[a, c] = place.rearrange("p (j e r) -> p j e r", e=2, r=2)
+            nc.scalar.activation(place.rearrange("p (j t) -> p j t", t=4), bank[:].rearrange("p t j -> p j t"), ACT.Copy)
+
+        def up(a, c, place=None):
+            if place is None:
+                place = tile("ub%d%d" % (a, c), [P, 2 * BANK], F32)[:]
+            both = place.rearrange("p (r j e) -> p r j e", r=2, e=2)
+            for r in range(2):
+                bank = bank_of("s", [P, 2, 2 * CHUNK])
+                for e in range(2):
+                    up_product(bank[:, e, :], a, 2 * e + r, c, c + 2)
+                nc.scalar.activation(both[:, r], bank[:].rearrange("p e j -> p j e"), ACT.Copy)
+            for half in range(2):
+                ub[a, c + half] = both[:, :, CHUNK * half : CHUNK * (half + 1), :].rearrange("p r j e -> p j e r")
 
         def gate(a, c):
             cols = slice(CHUNK * c, CHUNK * (c + 1))
@@ -176,8 +187,8 @@ def tile_list_gmlpt_relu_bias_kernel(tc, tab_words, tab_scales, wg, wu_words, wu
                 )
             c0 = group_of(c)[0]
             nc.vector.scalar_tensor_tensor(
-                out=h_bf[a, c0][:, BANK * (c - c0) : BANK * (c - c0 + 1)].rearrange("p (h j t) -> p h j t", h=2, t=4),
-                in0=bank[:].rearrange("p t (h j) -> p h j t", h=2),
+                out=h_bf[a, c0][:, BANK * (c - c0) : BANK * (c - c0 + 1)].rearrange("p (j e r) -> p j e r", e=2, r=2),
+                in0=bank[:].rearrange("p (e r) j -> p j e r", r=2),
                 scalar=0.0,
                 in1=ub[a, c],
                 op0=ALU.max,
@@ -250,30 +261,32 @@ def tile_list_gmlpt_relu_bias_kernel(tc, tab_words, tab_scales, wg, wu_words, wu
         g_bf1 = tile("g_bf1", [P, 4 * PASS], BF16)
         for t, q1 in ((0, 16), (1, 16), (2, 8)):
             round_wg1_gpsimd(t, 0, q1)
-        for c in range(4):
-            up(0, c, halves(early[:, BANK * c : BANK * (c + 1)]))
+        for c in (0, 2):
+            up(0, c, early[:, BANK * c : BANK * (c + 2)])
             gate(0, c)
-        up(0, 4)
+            gate(0, c + 1)
+        up_one(0, 4)
         gate(0, 4)
         for t, q0 in ((3, 0), (2, 8)):
             round_wg1_scalar(t, q0, 16)
-        for a, c in ((1, 0), (1, 1), (0, 5), (0, 6)):
-            up(a, c)
+        up(0, 5)
+        up(1, 0)
         quantize(gw[1][:], gs[1][:], g_bf1[:])
         d_bf0 = tile("d_bf0", [P, 4 * N], BF16, tag="g_bf1")
         for n0 in (0, N // 2):
             round_wd_gpsimd(d_bf0[:, 4 * n0 : 4 * n0 + 2 * N], 0, n0, n0 + N // 2)
         for a, c in ((0, 5), (0, 6), (1, 0), (1, 1)):
             gate(a, c)
-        for c in range(2, 6):
-            up(1, c)
-            if c < 5:
-                gate(1, c)
-        d_bf1 = [tile("d_bf1a", [P, 2 * N], BF16, tag="ub10"), tile("d_bf1b", [P, 2 * N], BF16, tag="ub11")]
+        up(1, 2)
+        gate(1, 2)
+        gate(1, 3)
+        up(1, 4)
+        gate(1, 4)
+        d_bf1 = [tile("d_bf1a", [P, 2 * N], BF16, tag="ub10"), tile("d_bf1b", [P, 2 * N], BF16, tag="ub12")]
         for half in range(2):
             round_wd(nc.scalar.copy, d_bf1[half][:], 1, 2 * P * half, 2 * P * (half + 1))
-        for a, c, t in ((0, 7, 0), (1, 6, 1), (1, 7, 2)):
-            up(a, c, halves(d_rows[1][:, t, :]))
+        up_one(0, 7, d_raw[1][:, 0:BANK])
+        up(1, 6, d_raw[1][:, BANK : 3 * BANK])
         quantize_h(0, 0, 4, tag="d_raw0")
         quantize_wd(0, 0, N, d_bf0[:])
         quantize_h(1, 0, 4, tag="h_bf00")
@@ -281,7 +294,7 @@ def tile_list_gmlpt_relu_bias_kernel(tc, tab_words, tab_scales, wg, wu_words, wu
         gate(1, 5)
         quantize_h(0, 4, 6, tag="g_bf1")
         quantize_wd(1, 2 * P, N, d_bf1[1][:])
-        quantize_h(1, 4, 6, tag="ub13")
+        quantize_h(1, 4, 6, tag="ub10")
         gate(0, 7)
         gate(1, 6)
         quantize_h(0, 6, 8)

@@ -215,35 +215,35 @@ def tile_list_gmlpt_relu_bias_kernel(tc, tab_words, tab_scales, wg, wu_words, wu
                 stop=(a == PASSES - 1),
             )
 
-        def add_bias(reader, c0, c1, u, sums):
-            if c0 not in y:
-                y[c0] = tile("y%d" % c0, [P, 4, CHUNK * (c1 - c0)], F32)
+        def add_bias(reader, dst, u, sums):
             if reader == "s":
-                nc.scalar.activation(y[c0][:, u, :], sums, ACT.Identity, bias=bias[:, u : u + 1])
+                nc.scalar.activation(dst, sums, ACT.Identity, bias=bias[:, u : u + 1])
             else:
-                nc.vector.tensor_scalar_add(y[c0][:, u, :], sums, bias[:, u : u + 1])
+                nc.vector.tensor_scalar_add(dst, sums, bias[:, u : u + 1])
 
         out_rows = out.rearrange("(u p) j -> p u j", p=P)
 
         def store(c0, c1, u0, u1):
             nc.sync.dma_start(out_rows[:, u0:u1, CHUNK * c0 : CHUNK * c1], y[c0][:, u0:u1, :])
 
-        def output(reader, c0, c1, u0, u1):
+        def output(reader, c0, c1, u0, u1, tag=None):
             bank = bank_of(reader, [P, u1 - u0, CHUNK * (c1 - c0)])
             for u in range(u0, u1):
                 for a in range(PASSES):
                     down_pass(bank[:, u - u0, :], c0, c1, u, a)
+            rows = tile("y%d%d" % (c0, u0), [P, u1 - u0, CHUNK * (c1 - c0)], F32, tag=tag)
             for u in range(u0, u1):
-                add_bias(reader, c0, c1, u, bank[:, u - u0, :])
-            store(c0, c1, u0, u1)
+                add_bias(reader, rows[:, u - u0, :], u, bank[:, u - u0, :])
+            nc.sync.dma_start(out_rows[:, u0:u1, CHUNK * c0 : CHUNK * c1], rows[:])
 
         def last(c0, c1, readers, stores):
             banks = [bank_of(reader, [P, CHUNK * (c1 - c0)]) for reader in readers]
+            y[c0] = tile("y%d" % c0, [P, 4, CHUNK * (c1 - c0)], F32)
             for a in range(PASSES):
                 for u in range(4):
                     down_pass(banks[u][:], c0, c1, u, a)
             for u in range(4):
-                add_bias(readers[u], c0, c1, u, banks[u][:])
+                add_bias(readers[u], y[c0][:, u, :], u, banks[u][:])
             for u0, u1 in stores:
                 store(c0, c1, u0, u1)
 
@@ -259,7 +259,7 @@ def tile_list_gmlpt_relu_bias_kernel(tc, tab_words, tab_scales, wg, wu_words, wu
             uw_raw[:, PASS // 2 : PASS].rearrange("p (q t w) -> p t q w", t=4, w=4),
         )
         g_bf1 = tile("g_bf1", [P, 4 * PASS], BF16)
-        for t, q1 in ((0, 16), (1, 16), (2, 8)):
+        for t, q1 in ((0, 16), (1, 16), (2, 16)):
             round_wg1_gpsimd(t, 0, q1)
         for c in (0, 2):
             up(0, c, early[:, BANK * c : BANK * (c + 2)])
@@ -267,7 +267,7 @@ def tile_list_gmlpt_relu_bias_kernel(tc, tab_words, tab_scales, wg, wu_words, wu
             gate(0, c + 1)
         up_one(0, 4)
         gate(0, 4)
-        for t, q0 in ((3, 0), (2, 8)):
+        for t, q0 in ((3, 0),):
             round_wg1_scalar(t, q0, 16)
         up(0, 5)
         up(1, 0)
@@ -282,10 +282,10 @@ def tile_list_gmlpt_relu_bias_kernel(tc, tab_words, tab_scales, wg, wu_words, wu
         gate(1, 3)
         up(1, 4)
         gate(1, 4)
+        up_one(0, 7)
         d_bf1 = [tile("d_bf1a", [P, 2 * N], BF16, tag="ub10"), tile("d_bf1b", [P, 2 * N], BF16, tag="ub12")]
         for half in range(2):
             round_wd(nc.scalar.copy, d_bf1[half][:], 1, 2 * P * half, 2 * P * (half + 1))
-        up_one(0, 7, d_raw[1][:, 0:BANK])
         up(1, 6, d_raw[1][:, BANK : 3 * BANK])
         quantize_h(0, 0, 4, tag="d_raw0")
         quantize_wd(0, 0, N, d_bf0[:])

@@ -26,6 +26,8 @@ BANKS = 4
 SCALE_ROWS = 16
 ROW0 = P - SCALE_ROWS
 WG_FIRST = 256
+WG_SCALAR = 256
+ROW = BANK + WG_FIRST - WG_SCALAR
 
 
 def tile_list_gmlpt_relu_bias_kernel(tc, tab_words, tab_scales, wg, wu_words, wu_scales, wd, b, offs, out):
@@ -33,25 +35,25 @@ def tile_list_gmlpt_relu_bias_kernel(tc, tab_words, tab_scales, wg, wu_words, wu
     with ExitStack() as ctx:
         keep = ctx.enter_context(tc.tile_pool(name="keep", bufs=1))
         ps = ctx.enter_context(tc.psum_pool(name="ps", bufs=1))
-        turn = {"s": [0, 1, 2, 3, 0] + [3, 0, 1, 2] * 6, "v": list(range(BANKS)) * 5}
+        turn = {"s": [0, 1, 2, 3, 0] + [3, 0, 1, 2] * 6, "v": [4, 1, 2] + [5, 6, 7, 4] * 5}
 
         def tile(name, shape, dtype, tag=None):
             return keep.tile(shape, dtype, name=name, tag=tag or name, align_bytes=64)
 
         def bank_of(reader, shape):
-            return ps.tile(shape, F32, name="bank_%s%d" % (reader, turn[reader].pop(0)))
+            return ps.tile(shape, F32, name="bank%d" % turn[reader].pop(0))
 
         offsets = keep.tile([P, J // 16], U16, name="offsets")
         tw = tile("tw", [P, T], I32)
         ts = tile("ts", [P, T // 4], I32, tag="ts_then_g_late")
         uw_raw = tile("uw_raw", [P, R // 2], I32)
         us_raw = tile("us_raw", [P, R // 4], I32)
-        uw = [tile("uw0", [P, 2 * PASS], U8)]
+        uw = [tile("uw%d" % a, [P, 2 * PASS], U8) for a in range(PASSES)]
         us = [tile("us%d" % a, [P, PASS], U8) for a in range(PASSES)]
         vw = [tile("vw%d" % half, [P, J // 2], U32) for half in range(2)]
         vs_raw = tile("vs_raw", [P, J], U8)
         vs = tile("vs", [P, J], U8)
-        early = tile("early", [P, 4 * BANK], F32)
+        early = tile("early", [P, 4 * ROW], F32)
         g_bf0 = tile("g_bf0", [P, 4 * PASS], BF16)
         gw = [tile("gw%d" % a, [P, PASS], U32) for a in range(PASSES)]
         gs = [tile("gs%d" % a, [P, PASS], U8) for a in range(PASSES)]
@@ -82,7 +84,7 @@ def tile_list_gmlpt_relu_bias_kernel(tc, tab_words, tab_scales, wg, wu_words, wu
         for e in range(4):
             nc.sync.dma_start(us_raw[e:P:32, :], us_rows[e:SCALE_ROWS:4, :])
         nc.sync.dma_start(tw[:], tab_words[0].rearrange("p t i -> p (t i)").bitcast(I32))
-        g_parts = [early[:].rearrange("p (i x) -> p i x", i=4)[:, :, 0:WG_FIRST]]
+        g_parts = [early[:].rearrange("p (i x) -> p i x", i=4)[:, :, ROW - WG_FIRST : ROW]]
         nc.sync.dma_start(g_parts[0], wg_rows[:, :, 0:WG_FIRST])
 
         nc.vector.tensor_copy(vs_raw[:], ts[:].bitcast(U8).indirect(offsets[:]))
@@ -106,6 +108,10 @@ def tile_list_gmlpt_relu_bias_kernel(tc, tab_words, tab_scales, wg, wu_words, wu
         nc.vector.tensor_copy(
             us[0][:].rearrange("p (t m) -> p t m", t=4),
             us_raw[:, 0 : PASS // 4].bitcast(U8).rearrange("p (m t) -> p t m", t=4),
+        )
+        nc.vector.tensor_copy(
+            uw[1][:].bitcast(I32).rearrange("p (t q w) -> p t q w", t=4, w=4),
+            uw_raw[:, PASS // 2 : PASS].rearrange("p (q t w) -> p t q w", t=4, w=4),
         )
         nc.vector.tensor_copy(
             us[1][:].bitcast(I32).rearrange("p (t q w) -> p t q w", t=4, w=2),
@@ -162,8 +168,8 @@ def tile_list_gmlpt_relu_bias_kernel(tc, tab_words, tab_scales, wg, wu_words, wu
 
         def up(a, c, place=None):
             if place is None:
-                place = tile("ub%d%d" % (a, c), [P, 2 * BANK], F32)[:]
-            both = place.rearrange("p (r j e) -> p r j e", r=2, e=2)
+                place = tile("ub%d%d" % (a, c), [P, 2, BANK], F32)[:]
+            both = place.rearrange("p r (j e) -> p r j e", e=2)
             for r in range(2):
                 bank = bank_of("s", [P, 2, 2 * CHUNK])
                 for e in range(2):
@@ -248,31 +254,26 @@ def tile_list_gmlpt_relu_bias_kernel(tc, tab_words, tab_scales, wg, wu_words, wu
                 store(c0, c1, u0, u1)
 
 
-        round_wg0(nc.scalar.copy, g_parts[0], 0, WG_FIRST)
+        round_wg0(nc.scalar.copy, g_parts[0][:, :, 0:WG_SCALAR], 0, WG_SCALAR)
         round_wg0(nc.vector.tensor_copy, g_parts[1], WG_FIRST, PASS)
         for half in range(2):
             cols = slice(2 * P * half, 2 * P * (half + 1))
             quantize(gw[0][:, cols], gs[0][:, cols], g_bf0[:, 4 * cols.start : 4 * cols.stop])
-        uw.append(tile("uw1", [P, 2 * PASS], U8, tag="g_bf0"))
-        nc.vector.tensor_copy(
-            uw[1][:].bitcast(I32).rearrange("p (t q w) -> p t q w", t=4, w=4),
-            uw_raw[:, PASS // 2 : PASS].rearrange("p (q t w) -> p t q w", t=4, w=4),
-        )
-        g_bf1 = tile("g_bf1", [P, 4 * PASS], BF16)
-        for t, q1 in ((0, 16), (1, 16), (2, 16)):
+        g_bf1 = tile("g_bf1", [P, 4 * PASS], BF16, tag="g_bf0")
+        for t, q1 in ((0, 16), (1, 16), (2, 8)):
             round_wg1_gpsimd(t, 0, q1)
         for c in (0, 2):
-            up(0, c, early[:, BANK * c : BANK * (c + 2)])
+            up(0, c, early[:].rearrange("p (i x) -> p i x", i=4)[:, c : c + 2, 0:BANK])
             gate(0, c)
             gate(0, c + 1)
         up_one(0, 4)
         gate(0, 4)
-        for t, q0 in ((3, 0),):
+        for t, q0 in ((3, 0), (2, 8)):
             round_wg1_scalar(t, q0, 16)
         up(0, 5)
         up(1, 0)
         quantize(gw[1][:], gs[1][:], g_bf1[:])
-        d_bf0 = tile("d_bf0", [P, 4 * N], BF16, tag="g_bf1")
+        d_bf0 = tile("d_bf0", [P, 4 * N], BF16, tag="g_bf0")
         for n0 in (0, N // 2):
             round_wd_gpsimd(d_bf0[:, 4 * n0 : 4 * n0 + 2 * N], 0, n0, n0 + N // 2)
         for a, c in ((0, 5), (0, 6), (1, 0), (1, 1)):
@@ -286,13 +287,13 @@ def tile_list_gmlpt_relu_bias_kernel(tc, tab_words, tab_scales, wg, wu_words, wu
         d_bf1 = [tile("d_bf1a", [P, 2 * N], BF16, tag="ub10"), tile("d_bf1b", [P, 2 * N], BF16, tag="ub12")]
         for half in range(2):
             round_wd(nc.scalar.copy, d_bf1[half][:], 1, 2 * P * half, 2 * P * (half + 1))
-        up(1, 6, d_raw[1][:, BANK : 3 * BANK])
+        up(1, 6, d_rows[1][:, 0:2, :])
         quantize_h(0, 0, 4, tag="d_raw0")
         quantize_wd(0, 0, N, d_bf0[:])
         quantize_h(1, 0, 4, tag="h_bf00")
         quantize_wd(1, 0, 2 * P, d_bf1[0][:])
         gate(1, 5)
-        quantize_h(0, 4, 6, tag="g_bf1")
+        quantize_h(0, 4, 6, tag="g_bf0")
         quantize_wd(1, 2 * P, N, d_bf1[1][:])
         quantize_h(1, 4, 6, tag="ub10")
         gate(0, 7)

@@ -62,7 +62,8 @@ def tile_list_gmlpt_relu_bias_kernel(tc, tab_words, tab_scales, wg, wu_words, wu
         hs = [tile("hs%d" % a, [P, J], U8) for a in range(PASSES)]
         d_raw = [tile("d_raw%d" % a, [P, 4 * N], F32) for a in range(PASSES)]
         d_rows = [flat[:].rearrange("p (t n) -> p t n", t=4) for flat in d_raw]
-        bias = tile("bias", [P, 4], F32)
+        bias_rows = tile("bias_rows", [P, 32], F32)
+        bias = tile("bias", [P, 32], F32)
         ub, h_bf, hw, y = {}, {}, {}, {}
         groups = ((0, 4), (4, 6), (6, 8))
         for a in range(PASSES):
@@ -75,6 +76,7 @@ def tile_list_gmlpt_relu_bias_kernel(tc, tab_words, tab_scales, wg, wu_words, wu
         nc.gpsimd.memset(us_raw[:], 0)
         nc.vector.memset(ts[0:ROW0, :], 0)
         nc.gpsimd.memset(vs[:].bitcast(I32), 0)
+        nc.gpsimd.memset(bias_rows[:], 0.0)
 
         us_rows = wu_scales[0].bitcast(I32)
         wg_rows = wg.rearrange("(p i) r -> p i r", i=4)
@@ -98,8 +100,9 @@ def tile_list_gmlpt_relu_bias_kernel(tc, tab_words, tab_scales, wg, wu_words, wu
         wd_rows = wd[PASS:R, :].rearrange("(q t s) n -> t q s n", t=4, s=8)
         for t in range(4):
             nc.sync.dma_start(d_rows[1][:, t, :], wd_rows[t])
-        with nc.allow_non_contiguous_dma(reason="one bias value to a partition"):
-            nc.sync.dma_start(bias[:], b.rearrange("(u p) -> p u", p=P))
+        b_rows = b.rearrange("(u q r) -> q u r", u=4, q=4)
+        for q in range(4):
+            nc.sync.dma_start(bias_rows[32 * q : 32 * q + 4, :], b_rows[q])
 
         nc.vector.tensor_copy(
             uw[0][:].rearrange("p (t m b) -> p t m b", t=4, b=2),
@@ -289,6 +292,7 @@ def tile_list_gmlpt_relu_bias_kernel(tc, tab_words, tab_scales, wg, wu_words, wu
             round_wd(nc.scalar.copy, d_bf1[half][:], 1, 2 * P * half, 2 * P * (half + 1))
         up(1, 6, d_rows[1][:, 0:2, :])
         quantize_h(0, 0, 4, tag="d_raw0")
+        nc.vector.transpose(bias[:], bias_rows[:])
         quantize_wd(0, 0, N, d_bf0[:])
         quantize_h(1, 0, 4, tag="h_bf00")
         quantize_wd(1, 0, 2 * P, d_bf1[0][:])

@@ -130,10 +130,10 @@ def tile_list_gmlpt_relu_bias_kernel(tc, tab_words, tab_scales, wg, wu_words, wu
         def round_on_gpsimd(dst, src):
             nc.gpsimd.tensor_scalar(dst, src, 1.0, 0.0, ALU.mult, ALU.add)
 
-        def round_wg1_gpsimd(t, q0, q1):
-            src = g_parts[2].rearrange("p i (q t s) -> p t q s i", t=4, s=8)
-            dst = g_bf1[:].rearrange("p (t q s i) -> p t q s i", t=4, s=8, i=4)
-            round_on_gpsimd(dst[:, t, q0:q1], src[:, t, q0:q1])
+        def round_wg1_gpsimd(t0, t1, q1):
+            src = g_parts[2].rearrange("p i (q t s) -> p q t s i", t=4, s=8)
+            dst = g_bf1[:].rearrange("p (t q s i) -> p q t s i", t=4, s=8, i=4)
+            round_on_gpsimd(dst[:, 0:q1, t0:t1], src[:, 0:q1, t0:t1])
 
         def round_wg1_scalar(t, q0, q1):
             src = g_parts[2].rearrange("p i (q t w v) -> p t q w i v", t=4, w=2, v=4)
@@ -263,8 +263,8 @@ def tile_list_gmlpt_relu_bias_kernel(tc, tab_words, tab_scales, wg, wu_words, wu
             cols = slice(2 * P * half, 2 * P * (half + 1))
             quantize(gw[0][:, cols], gs[0][:, cols], g_bf0[:, 4 * cols.start : 4 * cols.stop])
         g_bf1 = tile("g_bf1", [P, 4 * PASS], BF16, tag="g_bf0")
-        for t, q1 in ((0, 16), (1, 16), (2, 8)):
-            round_wg1_gpsimd(t, 0, q1)
+        round_wg1_gpsimd(0, 2, 16)
+        round_wg1_gpsimd(2, 3, 8)
         for c in (0, 2):
             up(0, c, early[:].rearrange("p (i x) -> p i x", i=4)[:, c : c + 2, 0:BANK])
             gate(0, c)
@@ -277,8 +277,7 @@ def tile_list_gmlpt_relu_bias_kernel(tc, tab_words, tab_scales, wg, wu_words, wu
         up(1, 0)
         quantize(gw[1][:], gs[1][:], g_bf1[:])
         d_bf0 = tile("d_bf0", [P, 4 * N], BF16, tag="g_bf0")
-        for n0 in (0, N // 2):
-            round_wd_gpsimd(d_bf0[:, 4 * n0 : 4 * n0 + 2 * N], 0, n0, n0 + N // 2)
+        round_wd_gpsimd(d_bf0[:], 0, 0, N)
         for a, c in ((0, 5), (0, 6), (1, 0), (1, 1)):
             gate(a, c)
         up(1, 2)

@@ -286,10 +286,10 @@ def tile_list_gmlpt_relu_bias_kernel(tc, tab_words, tab_scales, wg, wu_words, wu
         up(1, 4)
         gate(1, 4)
         up_one(0, 7)
+        up(1, 6)
         d_bf1 = [tile("d_bf1a", [P, 2 * N], BF16, tag="ub10"), tile("d_bf1b", [P, 2 * N], BF16, tag="ub12")]
         for half in range(2):
             round_wd(nc.scalar.copy, d_bf1[half][:], 1, 2 * P * half, 2 * P * (half + 1))
-        up(1, 6, d_rows[1][:, 0:2, :])
         quantize_h(0, 0, 4, tag="d_raw0")
         nc.vector.transpose(bias[:], bias_rows[:])
         quantize_wd(0, 0, N, d_bf0[:])

@@ -96,13 +96,12 @@ def tile_list_gmlpt_relu_bias_kernel(tc, tab_words, tab_scales, wg, wu_words, wu
         for r0, r1 in ((WG_FIRST, PASS), (PASS, R)):
             g_parts.append(g_late[:, 4 * (r0 - WG_FIRST) : 4 * (r1 - WG_FIRST)].rearrange("p (i r) -> p i r", i=4))
             nc.sync.dma_start(g_parts[-1], wg_rows[:, :, r0:r1])
+            if r1 == PASS:
+                nc.sync.dma_start(bias_rows[0:P:8, :], b.rearrange("(u z c) -> z u c", u=4, z=4))
         nc.sync.dma_start(d_rows[0], wd[0:PASS, :].rearrange("(p t) n -> p t n", t=4))
         wd_rows = wd[PASS:R, :].rearrange("(q t s) n -> t q s n", t=4, s=8)
         for t in range(4):
             nc.sync.dma_start(d_rows[1][:, t, :], wd_rows[t])
-        b_rows = b.rearrange("(u q r) -> q u r", u=4, q=4)
-        for q in range(4):
-            nc.sync.dma_start(bias_rows[32 * q : 32 * q + 4, :], b_rows[q])
 
         nc.vector.tensor_copy(
             uw[0][:].rearrange("p (t m b) -> p t m b", t=4, b=2),
@@ -226,9 +225,9 @@ def tile_list_gmlpt_relu_bias_kernel(tc, tab_words, tab_scales, wg, wu_words, wu
 
         def add_bias(reader, dst, u, sums):
             if reader == "s":
-                nc.scalar.activation(dst, sums, ACT.Identity, bias=bias[:, u : u + 1])
+                nc.scalar.activation(dst, sums, ACT.Identity, bias=bias[:, 8 * u : 8 * u + 1])
             else:
-                nc.vector.tensor_scalar_add(dst, sums, bias[:, u : u + 1])
+                nc.vector.tensor_scalar_add(dst, sums, bias[:, 8 * u : 8 * u + 1])
 
         out_rows = out.rearrange("(u p) j -> p u j", p=P)
 
@@ -246,13 +245,25 @@ def tile_list_gmlpt_relu_bias_kernel(tc, tab_words, tab_scales, wg, wu_words, wu
             nc.sync.dma_start(out_rows[:, u0:u1, CHUNK * c0 : CHUNK * c1], rows[:])
 
         def last(c0, c1, readers, stores):
-            banks = [bank_of(reader, [P, CHUNK * (c1 - c0)]) for reader in readers]
             y[c0] = tile("y%d" % c0, [P, 4, CHUNK * (c1 - c0)], F32)
-            for a in range(PASSES):
-                for u in range(4):
-                    down_pass(banks[u][:], c0, c1, u, a)
-            for u in range(4):
-                add_bias(readers[u], y[c0][:, u, :], u, banks[u][:])
+            for c in range(c0, c1):
+                cols = slice(CHUNK * (c - c0), CHUNK * (c - c0 + 1))
+                for reader in "sv":
+                    rows = [u for u in range(4) if readers[u] == reader]
+                    bank = bank_of(reader, [P, len(rows), CHUNK])
+                    for a in range(PASSES):
+                        for place, u in enumerate(rows):
+                            nc.tensor.matmul_mx(
+                                out=bank[:, place, :],
+                                lhsT=dw[a][:, P * u : P * (u + 1)].bitcast(FP8X4),
+                                lhsT_scale=ds[a][:, P * u : P * (u + 1)],
+                                rhs=hw[a, c0][:, cols].bitcast(FP8X4),
+                                rhs_scale=hs[a][:, CHUNK * c : CHUNK * (c + 1)],
+                                start=(a == 0 and place == 0),
+                                stop=(a == PASSES - 1 and place == len(rows) - 1),
+                            )
+                    for place, u in enumerate(rows):
+                        add_bias(reader, y[c0][:, u, cols], u, bank[:, place, :])
             for u0, u1 in stores:
                 store(c0, c1, u0, u1)
 
@@ -262,6 +273,7 @@ def tile_list_gmlpt_relu_bias_kernel(tc, tab_words, tab_scales, wg, wu_words, wu
         for half in range(2):
             cols = slice(2 * P * half, 2 * P * (half + 1))
             quantize(gw[0][:, cols], gs[0][:, cols], g_bf0[:, 4 * cols.start : 4 * cols.stop])
+        nc.vector.transpose(bias[:], bias_rows[:])
         g_bf1 = tile("g_bf1", [P, 4 * PASS], BF16, tag="g_bf0")
         round_wg1_gpsimd(0, 2, 16)
         round_wg1_gpsimd(2, 3, 8)
@@ -291,7 +303,6 @@ def tile_list_gmlpt_relu_bias_kernel(tc, tab_words, tab_scales, wg, wu_words, wu
         for half in range(2):
             round_wd(nc.scalar.copy, d_bf1[half][:], 1, 2 * P * half, 2 * P * (half + 1))
         quantize_h(0, 0, 4, tag="d_raw0")
-        nc.vector.transpose(bias[:], bias_rows[:])
         quantize_wd(0, 0, N, d_bf0[:])
         quantize_h(1, 0, 4, tag="h_bf00")
         quantize_wd(1, 0, 2 * P, d_bf1[0][:])
@@ -309,4 +320,4 @@ def tile_list_gmlpt_relu_bias_kernel(tc, tab_words, tab_scales, wg, wu_words, wu
             output("s", 4, 6, u0, u0 + 2)
         quantize_h(1, 6, 7, tag="h_bf06")
         quantize_h(1, 7, 8)
-        last(6, 8, "svsv", ((0, 2), (2, 4)))
+        last(6, 8, "ssvv", ((0, 2), (2, 4)))

@@ -96,12 +96,13 @@ def tile_list_gmlpt_relu_bias_kernel(tc, tab_words, tab_scales, wg, wu_words, wu
         for r0, r1 in ((WG_FIRST, PASS), (PASS, R)):
             g_parts.append(g_late[:, 4 * (r0 - WG_FIRST) : 4 * (r1 - WG_FIRST)].rearrange("p (i r) -> p i r", i=4))
             nc.sync.dma_start(g_parts[-1], wg_rows[:, :, r0:r1])
-            if r1 == PASS:
-                nc.sync.dma_start(bias_rows[0:P:8, :], b.rearrange("(u z c) -> z u c", u=4, z=4))
         nc.sync.dma_start(d_rows[0], wd[0:PASS, :].rearrange("(p t) n -> p t n", t=4))
         wd_rows = wd[PASS:R, :].rearrange("(q t s) n -> t q s n", t=4, s=8)
         for t in range(4):
             nc.sync.dma_start(d_rows[1][:, t, :], wd_rows[t])
+        b_rows = b.rearrange("(u q r) -> q u r", u=4, q=4)
+        for q in range(4):
+            nc.sync.dma_start(bias_rows[32 * q : 32 * q + 4, :], b_rows[q])
 
         nc.vector.tensor_copy(
             uw[0][:].rearrange("p (t m b) -> p t m b", t=4, b=2),
@@ -225,9 +226,9 @@ def tile_list_gmlpt_relu_bias_kernel(tc, tab_words, tab_scales, wg, wu_words, wu
 
         def add_bias(reader, dst, u, sums):
             if reader == "s":
-                nc.scalar.activation(dst, sums, ACT.Identity, bias=bias[:, 8 * u : 8 * u + 1])
+                nc.scalar.activation(dst, sums, ACT.Identity, bias=bias[:, u : u + 1])
             else:
-                nc.vector.tensor_scalar_add(dst, sums, bias[:, 8 * u : 8 * u + 1])
+                nc.vector.tensor_scalar_add(dst, sums, bias[:, u : u + 1])
 
         out_rows = out.rearrange("(u p) j -> p u j", p=P)
 
@@ -273,7 +274,6 @@ def tile_list_gmlpt_relu_bias_kernel(tc, tab_words, tab_scales, wg, wu_words, wu
         for half in range(2):
             cols = slice(2 * P * half, 2 * P * (half + 1))
             quantize(gw[0][:, cols], gs[0][:, cols], g_bf0[:, 4 * cols.start : 4 * cols.stop])
-        nc.vector.transpose(bias[:], bias_rows[:])
         g_bf1 = tile("g_bf1", [P, 4 * PASS], BF16, tag="g_bf0")
         round_wg1_gpsimd(0, 2, 16)
         round_wg1_gpsimd(2, 3, 8)
@@ -303,6 +303,7 @@ def tile_list_gmlpt_relu_bias_kernel(tc, tab_words, tab_scales, wg, wu_words, wu
         for half in range(2):
             round_wd(nc.scalar.copy, d_bf1[half][:], 1, 2 * P * half, 2 * P * (half + 1))
         quantize_h(0, 0, 4, tag="d_raw0")
+        nc.vector.transpose(bias[:], bias_rows[:])
         quantize_wd(0, 0, N, d_bf0[:])
         quantize_h(1, 0, 4, tag="h_bf00")
         quantize_wd(1, 0, 2 * P, d_bf1[0][:])

@@ -17,6 +17,7 @@ ALU = mybir.AluOpType
 ACT = mybir.ActivationFunctionType
 
 
+WD_GPSIMD = 448
 P = 128
 PASSES = 2
 PASS = R // PASSES
@@ -63,7 +64,6 @@ def tile_list_gmlpt_relu_bias_kernel(tc, tab_words, tab_scales, wg, wu_words, wu
         d_raw = [tile("d_raw%d" % a, [P, 4 * N], F32) for a in range(PASSES)]
         d_rows = [flat[:].rearrange("p (t n) -> p t n", t=4) for flat in d_raw]
         bias_rows = tile("bias_rows", [P, 32], F32)
-        bias = tile("bias", [P, 32], F32)
         ub, h_bf, hw, y = {}, {}, {}, {}
         groups = ((0, 4), (4, 6), (6, 8))
         for a in range(PASSES):
@@ -289,33 +289,36 @@ def tile_list_gmlpt_relu_bias_kernel(tc, tab_words, tab_scales, wg, wu_words, wu
         up(1, 0)
         quantize(gw[1][:], gs[1][:], g_bf1[:])
         d_bf0 = tile("d_bf0", [P, 4 * N], BF16, tag="g_bf0")
-        round_wd_gpsimd(d_bf0[:], 0, 0, N)
+        round_wd_gpsimd(d_bf0[:, 0 : 4 * WD_GPSIMD], 0, 0, WD_GPSIMD)
         for a, c in ((0, 5), (0, 6), (1, 0), (1, 1)):
             gate(a, c)
         up(1, 2)
+        round_wd(nc.scalar.copy, d_bf0[:, 4 * WD_GPSIMD : 4 * N], 0, WD_GPSIMD, N)
         gate(1, 2)
         gate(1, 3)
-        up(1, 4)
-        gate(1, 4)
-        up_one(0, 7)
-        up(1, 6)
         d_bf1 = [tile("d_bf1a", [P, 2 * N], BF16, tag="ub10"), tile("d_bf1b", [P, 2 * N], BF16, tag="ub12")]
-        for half in range(2):
-            round_wd(nc.scalar.copy, d_bf1[half][:], 1, 2 * P * half, 2 * P * (half + 1))
+        up(1, 4)
+        round_wd(nc.scalar.copy, d_bf1[0][:], 1, 0, 2 * P)
+        up_one(0, 7)
+        round_wd(nc.scalar.copy, d_bf1[1][:], 1, 2 * P, N)
         quantize_h(0, 0, 4, tag="d_raw0")
-        nc.vector.transpose(bias[:], bias_rows[:])
         quantize_wd(0, 0, N, d_bf0[:])
         quantize_h(1, 0, 4, tag="h_bf00")
         quantize_wd(1, 0, 2 * P, d_bf1[0][:])
+        bias = tile("bias", [P, 32], F32, tag="h_bf10")
+        nc.vector.transpose(bias[:], bias_rows[:])
+        output("s", 0, 4, 0, 1)
+        up(1, 6)
+        gate(1, 4)
         gate(1, 5)
-        quantize_h(0, 4, 6, tag="g_bf0")
         quantize_wd(1, 2 * P, N, d_bf1[1][:])
+        quantize_h(0, 4, 6, tag="g_bf0")
         quantize_h(1, 4, 6, tag="ub10")
         gate(0, 7)
         gate(1, 6)
         quantize_h(0, 6, 8)
         gate(1, 7)
-        for u in range(4):
+        for u in range(1, 4):
             output("s", 0, 4, u, u + 1)
         for u0 in (0, 2):
             output("s", 4, 6, u0, u0 + 2)

@@ -39,7 +39,7 @@ def tile_list_gmlpt_relu_bias_kernel(tc, tab_words, tab_scales, wg, wu_words, wu
         turn = {"s": [0, 1, 2, 3, 0] + [3, 0, 1, 2] * 6, "v": [4, 1, 2] + [5, 6, 7, 4] * 5}
 
         def tile(name, shape, dtype, tag=None):
-            return keep.tile(shape, dtype, name=name, tag=tag or name, align_bytes=64)
+            return keep.tile(shape, dtype, name=name, tag=tag or name, align_bytes=256)
 
         def bank_of(reader, shape):
             return ps.tile(shape, F32, name="bank%d" % turn[reader].pop(0))
@@ -73,7 +73,7 @@ def tile_list_gmlpt_relu_bias_kernel(tc, tab_words, tab_scales, wg, wu_words, wu
         def group_of(c):
             return [g for g in groups if g[0] <= c < g[1]][0]
 
-        nc.gpsimd.memset(us_raw[:], 0)
+        nc.vector.memset(us_raw[:], 0)
         nc.vector.memset(ts[0:ROW0, :], 0)
         nc.gpsimd.memset(vs[:].bitcast(I32), 0)
         nc.gpsimd.memset(bias_rows[:], 0.0)

@@ -48,7 +48,8 @@ def tile_list_gmlpt_relu_bias_kernel(tc, tab_words, tab_scales, wg, wu_words, wu
         tw = tile("tw", [P, T], I32)
         ts = tile("ts", [P, T // 4], I32, tag="ts_then_g_late")
         uw_raw = tile("uw_raw", [P, R // 2], I32)
-        us_raw = tile("us_raw", [P, R // 4], I32)
+        us_both = tile("us_raw", [P, 2, R // 4], I32)
+        us_raw = us_both[:, 0, :]
         uw = [tile("uw%d" % a, [P, 2 * PASS], U8) for a in range(PASSES)]
         us = [tile("us%d" % a, [P, PASS], U8) for a in range(PASSES)]
         vw = [tile("vw%d" % half, [P, J // 2], U32) for half in range(2)]
@@ -73,7 +74,7 @@ def tile_list_gmlpt_relu_bias_kernel(tc, tab_words, tab_scales, wg, wu_words, wu
         def group_of(c):
             return [g for g in groups if g[0] <= c < g[1]][0]
 
-        nc.vector.memset(us_raw[:], 0)
+        nc.vector.memset(us_raw, 0)
         nc.vector.memset(ts[0:ROW0, :], 0)
         nc.gpsimd.memset(vs[:].bitcast(I32), 0)
         nc.gpsimd.memset(bias_rows[:], 0.0)
@@ -83,8 +84,8 @@ def tile_list_gmlpt_relu_bias_kernel(tc, tab_words, tab_scales, wg, wu_words, wu
         nc.sync.dma_start(offsets[:], offs)
         nc.sync.dma_start(ts[ROW0:P, :], tab_scales[0].bitcast(I32))
         nc.sync.dma_start(uw_raw[:], wu_words[0].bitcast(I32))
-        for e in range(4):
-            nc.sync.dma_start(us_raw[e:P:32, :], us_rows[e:SCALE_ROWS:4, :])
+        for half in range(2):
+            nc.sync.dma_start(us_both[64 * half : 64 * half + 4], us_rows[8 * half : 8 * half + 8, :].rearrange("(q e) c -> e q c", q=2))
         nc.sync.dma_start(tw[:], tab_words[0].rearrange("p t i -> p (t i)").bitcast(I32))
         g_parts = [early[:].rearrange("p (i x) -> p i x", i=4)[:, :, ROW - WG_FIRST : ROW]]
         nc.sync.dma_start(g_parts[0], wg_rows[:, :, 0:WG_FIRST])
@@ -104,17 +105,19 @@ def tile_list_gmlpt_relu_bias_kernel(tc, tab_words, tab_scales, wg, wu_words, wu
         for q in range(4):
             nc.sync.dma_start(bias_rows[32 * q : 32 * q + 4, :], b_rows[q])
 
-        nc.vector.tensor_copy(
-            uw[0][:].rearrange("p (t m b) -> p t m b", t=4, b=2),
-            uw_raw[:, 0 : PASS // 2].bitcast(U8).rearrange("p (m t b) -> p t m b", t=4, b=2),
+        for half in range(2):
+            nc.vector.tensor_copy(us_both[64 * half + 32 : 64 * half + 36, 0, :], us_both[64 * half : 64 * half + 4, 1, :])
+        nc.scalar.copy(
+            uw[0][:].bitcast(U16).rearrange("p (t m) -> p t m", t=4),
+            uw_raw[:, 0 : PASS // 2].bitcast(U16).rearrange("p (m t) -> p t m", t=4),
         )
         nc.vector.tensor_copy(
             us[0][:].rearrange("p (t m) -> p t m", t=4),
             us_raw[:, 0 : PASS // 4].bitcast(U8).rearrange("p (m t) -> p t m", t=4),
         )
-        nc.vector.tensor_copy(
-            uw[1][:].bitcast(I32).rearrange("p (t q w) -> p t q w", t=4, w=4),
-            uw_raw[:, PASS // 2 : PASS].rearrange("p (q t w) -> p t q w", t=4, w=4),
+        nc.scalar.copy(
+            uw[1][:].bitcast(U32).rearrange("p (t q w) -> p t q w", t=4, w=4),
+            uw_raw[:, PASS // 2 : PASS].bitcast(U32).rearrange("p (q t w) -> p t q w", t=4, w=4),
         )
         nc.vector.tensor_copy(
             us[1][:].bitcast(I32).rearrange("p (t q w) -> p t q w", t=4, w=2),

from contextlib import ExitStack

import concourse.mybir as mybir

K, R, N, T, J = 512, 1024, 512, 4096, 1024
FLOPS = 2 * K * R * J * 2 + 2 * R * N * J

F32 = mybir.dt.float32
BF16 = mybir.dt.bfloat16
I32 = mybir.dt.int32
U32 = mybir.dt.uint32
U16 = mybir.dt.uint16
U8 = mybir.dt.uint8
FP8X4 = mybir.dt.float8_e4m3fn_x4
FP4X4 = mybir.dt.float4_e2m1fn_x4
ALU = mybir.AluOpType
ACT = mybir.ActivationFunctionType


WD_GPSIMD = 448
P = 128
PASSES = 2
PASS = R // PASSES
CHUNK = 128
BANK = 4 * CHUNK
BANKS = 4
SCALE_ROWS = 16
ROW0 = P - SCALE_ROWS
WG_FIRST = 256
WG_SCALAR = 256
ROW = BANK + WG_FIRST - WG_SCALAR


def tile_list_gmlpt_relu_bias_kernel(tc, tab_words, tab_scales, wg, wu_words, wu_scales, wd, b, offs, out):
    nc = tc.nc
    with ExitStack() as ctx:
        keep = ctx.enter_context(tc.tile_pool(name="keep", bufs=1))
        ps = ctx.enter_context(tc.psum_pool(name="ps", bufs=1))
        turn = {"s": [0, 1, 2, 3, 0] + [3, 0, 1, 2] * 6, "v": [4, 1, 2] + [5, 6, 7, 4] * 5}

        def tile(name, shape, dtype, tag=None):
            return keep.tile(shape, dtype, name=name, tag=tag or name, align_bytes=256)

        def bank_of(reader, shape):
            return ps.tile(shape, F32, name="bank%d" % turn[reader].pop(0))

        offsets = keep.tile([P, J // 16], U16, name="offsets")
        tw = tile("tw", [P, T], I32)
        ts = tile("ts", [P, T // 4], I32, tag="ts_then_g_late")
        uw_raw = tile("uw_raw", [P, R // 2], I32)
        us_both = tile("us_raw", [P, 2, R // 4], I32)
        us_raw = us_both[:, 0, :]
        uw = [tile("uw%d" % a, [P, 2 * PASS], U8) for a in range(PASSES)]
        us = [tile("us%d" % a, [P, PASS], U8) for a in range(PASSES)]
        vw = [tile("vw%d" % half, [P, J // 2], U32) for half in range(2)]
        vs_raw = tile("vs_raw", [P, J], U8)
        vs = tile("vs", [P, J], U8)
        early = tile("early", [P, 4 * ROW], F32)
        g_bf0 = tile("g_bf0", [P, 4 * PASS], BF16)
        gw = [tile("gw%d" % a, [P, PASS], U32) for a in range(PASSES)]
        gs = [tile("gs%d" % a, [P, PASS], U8) for a in range(PASSES)]
        dw = [tile("dw%d" % a, [P, N], U32) for a in range(PASSES)]
        ds = [tile("ds%d" % a, [P, N], U8) for a in range(PASSES)]
        hs = [tile("hs%d" % a, [P, J], U8) for a in range(PASSES)]
        d_raw = [tile("d_raw%d" % a, [P, 4 * N], F32) for a in range(PASSES)]
        d_rows = [flat[:].rearrange("p (t n) -> p t n", t=4) for flat in d_raw]
        bias_rows = tile("bias_rows", [P, 32], F32)
        ub, h_bf, hw, y = {}, {}, {}, {}
        groups = ((0, 4), (4, 6), (6, 8))
        for a in range(PASSES):
            for c0, c1 in groups:
                h_bf[a, c0] = tile("h_bf%d%d" % (a, c0), [P, BANK * (c1 - c0)], BF16)

        def group_of(c):
            return [g for g in groups if g[0] <= c < g[1]][0]

        nc.vector.memset(us_raw, 0)
        nc.vector.memset(ts[0:ROW0, :], 0)
        nc.gpsimd.memset(vs[:].bitcast(I32), 0)
        nc.gpsimd.memset(bias_rows[:], 0.0)

        us_rows = wu_scales[0].bitcast(I32)
        wg_rows = wg.rearrange("(p i) r -> p i r", i=4)
        nc.sync.dma_start(offsets[:], offs)
        nc.sync.dma_start(ts[ROW0:P, :], tab_scales[0].bitcast(I32))
        nc.sync.dma_start(uw_raw[:], wu_words[0].bitcast(I32))
        for half in range(2):
            nc.sync.dma_start(us_both[64 * half : 64 * half + 4], us_rows[8 * half : 8 * half + 8, :].rearrange("(q e) c -> e q c", q=2))
        nc.sync.dma_start(tw[:], tab_words[0].rearrange("p t i -> p (t i)").bitcast(I32))
        g_parts = [early[:].rearrange("p (i x) -> p i x", i=4)[:, :, ROW - WG_FIRST : ROW]]
        nc.sync.dma_start(g_parts[0], wg_rows[:, :, 0:WG_FIRST])

        nc.vector.tensor_copy(vs_raw[:], ts[:].bitcast(U8).indirect(offsets[:]))
        for e in range(4):
            nc.sync.dma_start(vs[e:P:32, :].bitcast(I32), vs_raw[ROW0 + e : P : 4, :].bitcast(I32))
        g_late = tile("g_late", [P, 4 * (R - WG_FIRST)], F32, tag="ts_then_g_late")
        for r0, r1 in ((WG_FIRST, PASS), (PASS, R)):
            g_parts.append(g_late[:, 4 * (r0 - WG_FIRST) : 4 * (r1 - WG_FIRST)].rearrange("p (i r) -> p i r", i=4))
            nc.sync.dma_start(g_parts[-1], wg_rows[:, :, r0:r1])
        nc.sync.dma_start(d_rows[0], wd[0:PASS, :].rearrange("(p t) n -> p t n", t=4))
        wd_rows = wd[PASS:R, :].rearrange("(q t s) n -> t q s n", t=4, s=8)
        for t in range(4):
            nc.sync.dma_start(d_rows[1][:, t, :], wd_rows[t])
        b_rows = b.rearrange("(u q r) -> q u r", u=4, q=4)
        for q in range(4):
            nc.sync.dma_start(bias_rows[32 * q : 32 * q + 4, :], b_rows[q])

        for half in range(2):
            nc.vector.tensor_copy(us_both[64 * half + 32 : 64 * half + 36, 0, :], us_both[64 * half : 64 * half + 4, 1, :])
        nc.scalar.copy(
            uw[0][:].bitcast(U16).rearrange("p (t m) -> p t m", t=4),
            uw_raw[:, 0 : PASS // 2].bitcast(U16).rearrange("p (m t) -> p t m", t=4),
        )
        nc.vector.tensor_copy(
            us[0][:].rearrange("p (t m) -> p t m", t=4),
            us_raw[:, 0 : PASS // 4].bitcast(U8).rearrange("p (m t) -> p t m", t=4),
        )
        nc.scalar.copy(
            uw[1][:].bitcast(U32).rearrange("p (t q w) -> p t q w", t=4, w=4),
            uw_raw[:, PASS // 2 : PASS].bitcast(U32).rearrange("p (q t w) -> p t q w", t=4, w=4),
        )
        nc.vector.tensor_copy(
            us[1][:].bitcast(I32).rearrange("p (t q w) -> p t q w", t=4, w=2),
            us_raw[:, PASS // 4 : PASS // 2].rearrange("p (q t w) -> p t q w", t=4, w=2),
        )
        for half in range(2):
            nc.vector.tensor_copy(vw[half][:], tw[:].bitcast(U32).indirect(offsets[:, 32 * half : 32 * (half + 1)]))

        def round_wg0(copy, raw, r0, r1):
            dst = g_bf0[:].rearrange("p (h e m i) -> p h m i e", h=2, e=2, i=4)
            copy(dst[:, :, r0 // 4 : r1 // 4], raw.rearrange("p i (m h e) -> p h m i e", h=2, e=2))

        def round_on_gpsimd(dst, src):
            nc.gpsimd.tensor_scalar(dst, src, 1.0, 0.0, ALU.mult, ALU.add)

        def round_wg1_gpsimd(t0, t1, q1):
            src = g_parts[2].rearrange("p i (q t s) -> p q t s i", t=4, s=8)
            dst = g_bf1[:].rearrange("p (t q s i) -> p q t s i", t=4, s=8, i=4)
            round_on_gpsimd(dst[:, 0:q1, t0:t1], src[:, 0:q1, t0:t1])

        def round_wg1_scalar(t, q0, q1):
            src = g_parts[2].rearrange("p i (q t w v) -> p t q w i v", t=4, w=2, v=4)
            dst = g_bf1[:].rearrange("p (t q w v i) -> p t q w i v", t=4, w=2, v=4, i=4)
            nc.scalar.copy(dst[:, t, q0:q1], src[:, t, q0:q1])

        def round_wd_gpsimd(dst, a, n0, n1):
            round_on_gpsimd(dst.rearrange("p (n t) -> p n t", t=4), d_rows[a][:, :, n0:n1].rearrange("p t n -> p n t"))

        def round_wd(copy, dst, a, n0, n1):
            copy(dst.rearrange("p (w v t) -> p w t v", t=4, v=4), d_rows[a][:, :, n0:n1].rearrange("p t (w v) -> p w t v", v=4))

        def quantize(words, scales, src):
            nc.vector.quantize_mx(out=words.bitcast(FP8X4), scales=scales, in_=src)

        def up_product(dst, a, t, c0, c1):
            nc.tensor.matmul_mx(
                out=dst,
                lhsT=uw[a][:, 2 * P * t : 2 * P * (t + 1)].bitcast(FP4X4),
                lhsT_scale=us[a][:, P * t : P * (t + 1)],
                rhs=vw[c0 // 4][:, CHUNK * (c0 % 4) : CHUNK * (c0 % 4 + c1 - c0)].bitcast(FP8X4),
                rhs_scale=vs[:, CHUNK * c0 : CHUNK * c1],
                start=True,
                stop=True,
            )

        def up_one(a, c, place=None):
            bank = bank_of("s", [P, 4, CHUNK])
            for t in range(4):
                up_product(bank[:, t, :], a, t, c, c + 1)
            if place is None:
                place = tile("ub%d%d" % (a, c), [P, BANK], F32)[:]
            ub[a, c] = place.rearrange("p (j e r) -> p j e r", e=2, r=2)
            nc.scalar.activation(place.rearrange("p (j t) -> p j t", t=4), bank[:].rearrange("p t j -> p j t"), ACT.Copy)

        def up(a, c, place=None):
            if place is None:
                place = tile("ub%d%d" % (a, c), [P, 2, BANK], F32)[:]
            both = place.rearrange("p r (j e) -> p r j e", e=2)
            for r in range(2):
                bank = bank_of("s", [P, 2, 2 * CHUNK])
                for e in range(2):
                    up_product(bank[:, e, :], a, 2 * e + r, c, c + 2)
                nc.scalar.activation(both[:, r], bank[:].rearrange("p e j -> p j e"), ACT.Copy)
            for half in range(2):
                ub[a, c + half] = both[:, :, CHUNK * half : CHUNK * (half + 1), :].rearrange("p r j e -> p j e r")

        def gate(a, c):
            cols = slice(CHUNK * c, CHUNK * (c + 1))
            bank = bank_of("v", [P, 4, CHUNK])
            for t in range(4):
                nc.tensor.matmul_mx(
                    out=bank[:, t, :],
                    lhsT=gw[a][:, P * t : P * (t + 1)].bitcast(FP8X4),
                    lhsT_scale=gs[a][:, P * t : P * (t + 1)],
                    rhs=vw[c // 4][:, CHUNK * (c % 4) : CHUNK * (c % 4 + 1)].bitcast(FP8X4),
                    rhs_scale=vs[:, cols],
                    start=True,
                    stop=True,
                )
            c0 = group_of(c)[0]
            nc.vector.scalar_tensor_tensor(
                out=h_bf[a, c0][:, BANK * (c - c0) : BANK * (c - c0 + 1)].rearrange("p (j e r) -> p j e r", e=2, r=2),
                in0=bank[:].rearrange("p (e r) j -> p j e r", r=2),
                scalar=0.0,
                in1=ub[a, c],
                op0=ALU.max,
                op1=ALU.mult,
            )

        def quantize_h(a, c0, c1, tag=None):
            g0, g1 = group_of(c0)
            if c0 == g0:
                hw[a, g0] = tile("hw%d%d" % (a, g0), [P, CHUNK * (g1 - g0)], U32, tag=tag)
            quantize(hw[a, g0][:, CHUNK * (c0 - g0) : CHUNK * (c1 - g0)], hs[a][:, CHUNK * c0 : CHUNK * c1], h_bf[a, g0][:, BANK * (c0 - g0) : BANK * (c1 - g0)])

        def quantize_wd(a, n0, n1, src):
            quantize(dw[a][:, n0:n1], ds[a][:, n0:n1], src)

        def down_pass(bank, c0, c1, u, a):
            nc.tensor.matmul_mx(
                out=bank,
                lhsT=dw[a][:, P * u : P * (u + 1)].bitcast(FP8X4),
                lhsT_scale=ds[a][:, P * u : P * (u + 1)],
                rhs=hw[a, c0][:].bitcast(FP8X4),
                rhs_scale=hs[a][:, CHUNK * c0 : CHUNK * c1],
                start=(a == 0),
                stop=(a == PASSES - 1),
            )

        def add_bias(reader, dst, u, sums):
            if reader == "s":
                nc.scalar.activation(dst, sums, ACT.Identity, bias=bias[:, u : u + 1])
            else:
                nc.vector.tensor_scalar_add(dst, sums, bias[:, u : u + 1])

        out_rows = out.rearrange("(u p) j -> p u j", p=P)

        def store(c0, c1, u0, u1):
            nc.sync.dma_start(out_rows[:, u0:u1, CHUNK * c0 : CHUNK * c1], y[c0][:, u0:u1, :])

        def output(reader, c0, c1, u0, u1, tag=None):
            bank = bank_of(reader, [P, u1 - u0, CHUNK * (c1 - c0)])
            for u in range(u0, u1):
                for a in range(PASSES):
                    down_pass(bank[:, u - u0, :], c0, c1, u, a)
            rows = tile("y%d%d" % (c0, u0), [P, u1 - u0, CHUNK * (c1 - c0)], F32, tag=tag)
            for u in range(u0, u1):
                add_bias(reader, rows[:, u - u0, :], u, bank[:, u - u0, :])
            nc.sync.dma_start(out_rows[:, u0:u1, CHUNK * c0 : CHUNK * c1], rows[:])

        def last(c0, c1, readers, stores):
            y[c0] = tile("y%d" % c0, [P, 4, CHUNK * (c1 - c0)], F32)
            for c in range(c0, c1):
                cols = slice(CHUNK * (c - c0), CHUNK * (c - c0 + 1))
                for reader in "sv":
                    rows = [u for u in range(4) if readers[u] == reader]
                    bank = bank_of(reader, [P, len(rows), CHUNK])
                    for a in range(PASSES):
                        for place, u in enumerate(rows):
                            nc.tensor.matmul_mx(
                                out=bank[:, place, :],
                                lhsT=dw[a][:, P * u : P * (u + 1)].bitcast(FP8X4),
                                lhsT_scale=ds[a][:, P * u : P * (u + 1)],
                                rhs=hw[a, c0][:, cols].bitcast(FP8X4),
                                rhs_scale=hs[a][:, CHUNK * c : CHUNK * (c + 1)],
                                start=(a == 0 and place == 0),
                                stop=(a == PASSES - 1 and place == len(rows) - 1),
                            )
                    for place, u in enumerate(rows):
                        add_bias(reader, y[c0][:, u, cols], u, bank[:, place, :])
            for u0, u1 in stores:
                store(c0, c1, u0, u1)


        round_wg0(nc.scalar.copy, g_parts[0][:, :, 0:WG_SCALAR], 0, WG_SCALAR)
        round_wg0(nc.vector.tensor_copy, g_parts[1], WG_FIRST, PASS)
        for half in range(2):
            cols = slice(2 * P * half, 2 * P * (half + 1))
            quantize(gw[0][:, cols], gs[0][:, cols], g_bf0[:, 4 * cols.start : 4 * cols.stop])
        g_bf1 = tile("g_bf1", [P, 4 * PASS], BF16, tag="g_bf0")
        round_wg1_gpsimd(0, 2, 16)
        round_wg1_gpsimd(2, 3, 8)
        for c in (0, 2):
            up(0, c, early[:].rearrange("p (i x) -> p i x", i=4)[:, c : c + 2, 0:BANK])
            gate(0, c)
            gate(0, c + 1)
        up_one(0, 4)
        gate(0, 4)
        for t, q0 in ((3, 0), (2, 8)):
            round_wg1_scalar(t, q0, 16)
        up(0, 5)
        up(1, 0)
        quantize(gw[1][:], gs[1][:], g_bf1[:])
        d_bf0 = tile("d_bf0", [P, 4 * N], BF16, tag="g_bf0")
        round_wd_gpsimd(d_bf0[:, 0 : 4 * WD_GPSIMD], 0, 0, WD_GPSIMD)
        for a, c in ((0, 5), (0, 6), (1, 0), (1, 1)):
            gate(a, c)
        up(1, 2)
        round_wd(nc.scalar.copy, d_bf0[:, 4 * WD_GPSIMD : 4 * N], 0, WD_GPSIMD, N)
        gate(1, 2)
        gate(1, 3)
        d_bf1 = [tile("d_bf1a", [P, 2 * N], BF16, tag="ub10"), tile("d_bf1b", [P, 2 * N], BF16, tag="ub12")]
        up(1, 4)
        round_wd(nc.scalar.copy, d_bf1[0][:], 1, 0, 2 * P)
        up_one(0, 7)
        round_wd(nc.scalar.copy, d_bf1[1][:], 1, 2 * P, N)
        quantize_h(0, 0, 4, tag="d_raw0")
        quantize_wd(0, 0, N, d_bf0[:])
        quantize_h(1, 0, 4, tag="h_bf00")
        quantize_wd(1, 0, 2 * P, d_bf1[0][:])
        bias = tile("bias", [P, 32], F32, tag="h_bf10")
        nc.vector.transpose(bias[:], bias_rows[:])
        output("s", 0, 4, 0, 1)
        up(1, 6)
        gate(1, 4)
        gate(1, 5)
        quantize_wd(1, 2 * P, N, d_bf1[1][:])
        quantize_h(0, 4, 6, tag="g_bf0")
        quantize_h(1, 4, 6, tag="ub10")
        gate(0, 7)
        gate(1, 6)
        quantize_h(0, 6, 8)
        gate(1, 7)
        for u in range(1, 4):
            output("s", 0, 4, u, u + 1)
        for u0 in (0, 2):
            output("s", 4, 6, u0, u0 + 2)
        quantize_h(1, 6, 7, tag="h_bf06")
        quantize_h(1, 7, 8)
        last(6, 8, "ssvv", ((0, 2), (2, 4)))
